import numpy as np, ml_dtypes
CORES = [51,54,179,182]
N = 4
BF = ml_dtypes.bfloat16
V, G, W, CAP, QA, QB, RO = 704, 672, 2048, 112, 4, 2, 4
def deal(rng, a):
    return np.stack([rng.permutation(np.resize(np.array(a), 8)) for q in range(N)])
def parts(rng):
    sh = (N, 8, 16, V)
    mid = rng.integers(20, 236, (N, 8, 16, 16)); kin = rng.integers(0, 16, (N, 8, 1, V))
    x = np.take_along_axis(mid, kin, 3) + rng.integers(-20, 21, sh)
    low = deal(rng, [0.003, 0.01, 0.03])[:, :, None, None]; flat = deal(rng, [0, 1])[:, :, None, None] == 1
    r = np.where(flat, 255, rng.integers(130, 256, sh)); r = np.where(rng.random(sh) < low, rng.integers(1, 130, sh), r)
    p = np.where(rng.random(sh) < 0.15, rng.integers(1, 130, sh), 0)
    keep = deal(rng, [0.4, 0.7, 0.9])[:, :, None, None]
    s = np.where(rng.random(sh) < keep, np.arange(V), rng.integers(0, W, sh))
    c = np.where(rng.random(sh) < 0.5, rng.integers(0, V, sh), rng.integers(0, W, sh))
    h = deal(rng, [180, 230, 500, 1000, 1200]) + rng.integers(0, 32, (N, 8))
    return x, r, p, c, s, h
def pack(x, r, p, c, s, h):
    v = {"x": x, "reach": r, "past": p}
    d = {k: np.ascontiguousarray(v[k].reshape(N, 128, V)).astype(np.float32).astype(BF) for k in v}
    d["cand"] = np.ascontiguousarray(c.reshape(N, 128, V)).astype(np.int32); d["succ"] = np.ascontiguousarray(s.reshape(N, 128, V)).astype(np.int32)
    d["th"] = h.reshape(N, 8, 1).astype(np.int32)
    return d
def setup_inputs(rng):
    return pack(*parts(rng))
def setup_inputs_ends(rng):
    sh = (N, 8, 16, V); one = (N, 8, 1, V)
    x = 255 * np.where(rng.random(one) < 0.7, rng.integers(0, 2, one), rng.integers(0, 2, sh))
    x = np.where((rng.random(one) < 0.2) & (rng.random(sh) < 0.3), x + np.where(x == 0, 1, -1), x)
    k = rng.random(one); r = np.where(k < 0.5, 255, np.where(k < 0.6, 1, np.where(rng.random(sh) < 0.5, 1, 255)))
    p = 255 * ((rng.random(one) < 0.25) & (rng.random(sh) < 0.2)).astype(np.int64)
    c = np.where(rng.random(sh) < 0.65, (W - 1) * rng.integers(0, 2, sh), rng.integers(0, W, sh))
    s = np.where((rng.random(one) < 0.5) | (rng.random(sh) < 0.65), (W - 1) * rng.integers(0, 2, sh), rng.integers(0, W, sh))
    h = 4095 * rng.integers(0, 2, (N, 8)); h[:, 0] = 0; h[:, 4] = 4095; h[:, 7] = 4095
    for a in (0, 1, V - QA, V - 1, G - 1): p[..., a] = 0; r[..., a] = 255
    p[..., 2] = 255; r[..., 2] = 1; x[..., 0] = 0; x[..., V - QA] = 0
    for a in (1, V - 1): x[:, 1::2, :, a] = 255; x[:, ::2, :, a] = 0
    c[..., 0] = 2; c[:, :, 15, 0] = V - 1
    c[..., V - QA] = 2; c[:, :, 14, V - QA] = V - 1; c[:, :, 15, V - QA] = 1
    s[..., 0] = 0; s[..., G - 1] = W - 1
    return pack(x, r, p, c, s, h)
def setup_inputs_corners(rng):
    x, r, p, c, s, h = parts(rng); act = np.arange(0, G, QB); here = np.arange(V); ptr = np.array([0, V - 1, V, V + G - 1, V + G, W - 1])
    for q in range(N):
        for g in range(8):
            k = (g + q) % 8
            if k < 6:
                n = (0, 1, CAP - 1, CAP, CAP + 1, len(act))[k]; a = rng.permutation(act)[:n]
                h[q, g] = 0; x[q, g] = x[q, g][:, rng.integers(0, 16, V)]; r[q, g] = 200; r[q, g, :, V - 1] = 5
                p[q, g] = np.where(rng.random((16, V)) < 0.05, 10, 0)
                w = np.tile(here, (16, 1)); w[rng.integers(0, 16, n), a] = V - 1; s[q, g] = w
            elif k == 6:
                h[q, g] = 4095; p[q, g] = 0; c[q, g] = here - here % QA + (here + QA - 1) % QA
            else:
                h[q, g] = 4095; full = rng.random(V) < 0.5; full[0] = True; full[V - 1] = False; m = rng.random(V) < 0.5; n = int(np.count_nonzero(m))
                w = p[q, g].copy(); w[:, full] = 255; p[q, g] = w
                w = np.where(rng.random((16, V)) < 0.5, rng.integers(V, W, (16, V)), (here + QA * rng.integers(0, V // QA, (16, V))) % V)
                w[:, m] = rng.choice(here[full], (16, n)); w[15, m] = rng.integers(0, V, n); c[q, g] = w
                s[q, g] = np.where(rng.random((16, V)) < 0.3, here, ptr[rng.integers(0, 6, (16, V))])
    return pack(x, r, p, c, s, h)
def setup_inputs_ties(rng):
    x, r, p, c, s, h = parts(rng); sh = (N, 8, 16, V)
    x = 8 * rng.integers(0, 2, sh); pool = rng.integers(0, V, (N, 8, 1, 24)); pool[..., 0] = 0; pool[..., 1] = V - 1; pool[..., 2] = V; pool[..., 3] = W - 1
    few = np.take_along_axis(pool, rng.integers(0, 24, sh), 3); c[:, ::2] = few[:, ::2]
    m = np.arange(16)[:, None] == rng.integers(0, 16, (N, 8, 1, 1))
    r = np.where(m, rng.integers(100, 102, sh), rng.integers(101, 256, sh)); p = np.where(m, rng.integers(99, 101, sh), 0)
    h = deal(rng, [24, 32, 40, 48, 64])
    return pack(x, r, p, c, s, h)
def setup_inputs_border(rng):
    x, r, p, c, s, h = parts(rng); x = rng.integers(0, 256, x.shape); h = rng.integers(1, 33, h.shape); s[...] = np.arange(V)
    goal = np.zeros((N, 8, 3), np.int64); e, y, w = G - 1, V - 3, V - 2
    for q in range(N):
        for g in range(8):
            n, turn = ((0, 0), (0, int(rng.integers(1, 3))), (CAP - 1, 0), (CAP, 0), (CAP + 1, 0), (G, 0))[(g + q) % 6]
            o = [4 * rng.permutation(G // 4 - 1) + i for i in range(4)]
            v = o[turn][0]; j = o[0][1]; v1 = o[1][1]; u = o[1][2]; b = o[3][1]; z = o[3][2]
            for a in (v, e, j, y, v1, w, u, b): s[q, g, :, a] = z; c[q, g, :, a] = rng.integers(V, W, 16)
            for a in (v, v1, u): r[q, g, :, a] = rng.integers(140, 200, 16); p[q, g, :, a] = rng.integers(0, 41, 16)
            for a in (e, j): r[q, g, :, a] = rng.integers(200, 255, 16); p[q, g, :, a] = 0
            for a in (y, w): r[q, g, :, a] = 255; p[q, g, :, a] = 0
            r[q, g, :, z] = 255; r[q, g, :, V - 1] = 1
            i, k = rng.integers(0, 16, 2); d = int(rng.integers(1, 41))
            r[q, g, :, b] = r[q, g, :, u]; p[q, g, :, b] = p[q, g, :, u]; r[q, g, i, b] -= d; p[q, g, k, b] += d
            for a, f in ((v, e), (j, y), (v1, y), (w, y), (u, b)): x[q, g, :, a] = x[q, g, :, f]
            for a, f in ((v, e), (j, y), (v1, j), (w, y), (u, b)): c[q, g, int(rng.integers(0, 16)), a] = f
            a = rng.permutation(np.setdiff1d(np.arange(0, G, QB), np.array([v, j])))[:n]
            s[q, g][rng.integers(0, 16, len(a)), a] = V - 1
            goal[q, g] = (e, u, j)
    k = np.arange(G, V - 3)
    for q in range(N):
        for g in range(8):
            see = np.concatenate([V + goal[(q + 1) % N, g], V + G + goal[(q - 1) % N, g]])
            r[q, g, :, G:V - 3] = 255; p[q, g, :, G:V - 3] = 0
            s[q, g][rng.integers(0, 16, len(k)), k] = see[((k - G) // 4) % 6]
    return pack(x, r, p, c, s, h)
def setup_inputs_spread(rng):
    sh = (N, 8, 16, V); one = (N, 8, 1, V)
    def uneven(): return np.floor(np.exp2(8 * rng.random(one)) * rng.random(sh)).astype(np.int64)
    def lean():
        e = deal(rng, [1.0, 2.0, 4.0])[:, :, None, None]; v = np.minimum((W * rng.random(sh) ** e).astype(np.int64), W - 1)
        return np.where(deal(rng, [0, 0, 1])[:, :, None, None] == 1, W - 1 - v, v)
    x = uneven(); r = np.maximum(255 - uneven(), 1); p = np.where(rng.random(one) < 0.3, uneven(), 0)
    c = lean(); s = np.where(rng.random(one) < rng.random(sh), np.arange(V), lean())
    h = np.minimum(np.floor(np.exp2(12 * rng.random((N, 8)))).astype(np.int64), 4095)
    return pack(x, r, p, c, s, h)
def check_inputs(d):
    bad = []
    for k, lo, hi in (("x", 0, 255), ("reach", 1, 255), ("past", 0, 255), ("cand", 0, W - 1), ("succ", 0, W - 1), ("th", 0, 4095)):
        a = np.asarray(d[k]).astype(np.float64)
        if not (np.all(a >= lo) and np.all(a <= hi)): bad.append("range of " + k)
        elif not np.all(a == np.floor(a)): bad.append("whole numbers in " + k)
    return bad
def at(a, ix):
    return np.take_along_axis(a, ix[:, :, None, :], 3)
def reference(x, reach, past, cand, succ, th):
    X = x.astype(np.float32).astype(np.int32).reshape(N, 8, 16, V)
    R = reach.astype(np.float32).astype(np.int32).reshape(N, 8, 16, V); P = past.astype(np.float32).astype(np.int32).reshape(N, 8, 16, V)
    R = np.concatenate([R, np.roll(R[..., :G], -1, axis=0), np.roll(R[..., :G], 1, axis=0)], axis=3)
    P = np.concatenate([P, np.roll(P[..., :G], -1, axis=0), np.roll(P[..., :G], 1, axis=0)], axis=3)
    C = cand.astype(np.int64).reshape(N, 8, 16, V); S = succ.astype(np.int64).reshape(N, 8, 16, V); H = th.astype(np.int64).reshape(N, 8)
    F = np.zeros((N, 8, W), np.int64) + np.arange(W); M = np.zeros(N, np.int64); odd = (np.arange(16) % 2 == 1)[:, None]; NONE = 2 ** 20
    qi, gi = np.arange(N)[:, None, None], np.arange(8)[None, :, None]
    for t in range(RO):
        r_old, p_old, f_old = R[..., :G].copy(), P[..., :G].copy(), F[..., :G].copy()
        a = slice(t % QA, V, QA); v = np.arange(t % QA, V, QA); L = len(v)
        c = np.take_along_axis(F, C[..., a].reshape(N, 8, 16 * L), 2)
        xc, rc, pc = [at(w, i).reshape(N, 8, 16, 16, L) for w, i in ((X, np.minimum(c, V - 1)), (R, c), (P, c))]
        xv, rv, pv = [w[..., a][:, :, :, None, :] for w in (X, R, P)]
        c = c.reshape(N, 8, 16, L); ordered = np.any((rv <= pc) | (rc <= pv), axis=2)
        fit = ~ordered & (c < V) & (c % QA != t % QA)
        D = np.where(fit, np.add.reduce(np.abs(xc - xv), axis=2), NONE)
        k = np.argmin(D, axis=2)[:, :, None, :]
        b = np.take_along_axis(c, k, 2)[:, :, 0]; D = np.take_along_axis(D, k, 2)[:, :, 0].astype(np.int64); has = D < NONE; b = np.where(has, b, 0)
        C[..., a] = np.where(ordered & has[:, :, None, :], at(C, b), C[..., a])
        asks = has & (D < H[:, :, None] + (M & 31)[:, None, None]); key = np.where(asks, D * V + v, 2 ** 40)
        best = np.full((N, 8, V), 2 ** 40, np.int64); np.minimum.at(best, (qi, gi, b), key)
        win = asks & (np.take_along_axis(best, b, 2) == key); m = win[:, :, None, :]
        xb, rb, pb, sb = at(X, b), at(R, b), at(P, b), at(S, b)
        X[..., a] = np.where(m, (X[..., a] + xb) >> 1, X[..., a])
        R[..., a] = np.where(m, np.minimum(R[..., a], rb), R[..., a]); P[..., a] = np.where(m, np.maximum(P[..., a], pb), P[..., a])
        S[..., a] = np.where(m & odd, sb, S[..., a])
        i, j, l = np.nonzero(win); F[i, j, b[i, j, l]] = v[l]
        M = np.add.reduce(win.astype(np.int64).reshape(N, -1), axis=1)
        a = slice(t % QB, V, QB); L = len(range(t % QB, V, QB))
        c = np.take_along_axis(F, S[..., a].reshape(N, 8, 16 * L), 2)
        low = np.min(at(R, c).reshape(N, 8, 16, 16, L), axis=3); R[..., a] = np.minimum(R[..., a], low)
        ch = np.any(R[..., :G] != r_old, axis=2) | np.any(P[..., :G] != p_old, axis=2) | (F[..., :G] != f_old)
        go = ch & (np.add.accumulate(ch.astype(np.int64), axis=2) <= CAP)
        for turn, o in ((-1, V), (1, V + G)):
            w = np.roll(go, turn, axis=0); m = w[:, :, None, :]; f = np.roll(F[..., :G], turn, axis=0)
            R[..., o:o + G] = np.where(m, np.roll(R[..., :G], turn, axis=0), R[..., o:o + G])
            P[..., o:o + G] = np.where(m, np.roll(P[..., :G], turn, axis=0), P[..., o:o + G])
            F[..., o:o + G] = np.where(w & (f < G), f + o, F[..., o:o + G])
    return {"yx": X.reshape(N, 128, V).astype(np.float32).astype(BF), "yr": np.ascontiguousarray(R[..., :V]).reshape(N, 128, V).astype(np.float32).astype(BF), "yc": C.reshape(N, 128, V).astype(np.float32)}

@@ -1,0 +1,660 @@
+from concourse.bass import DstId, RemoteDMATransfer
+from concourse.mybir import AluOpType as A, AxisListType, ActivationFunctionType as AF
+
+V, G, W, CAP, RO = 704, 672, 2048, 112, 4
+L = V // 4
+NE = 16 * L
+DUMP = W
+GB_ = 800
+XC = 3
+V3, VL3 = 56, 64
+NR = 16 * 88
+BIGX = 512.0
+WO = 16384.0
+WB = 1048576.0
+TILES = [(0, 0), (0, 1), (1, 0), (1, 1), (2, 0), (2, 1), (3, 0), (3, 1), (0, 2), (1, 2), (2, 2), (3, 2)]
+
+SCRATCH = {}
+
+
+def _declare():
+    bf = [("X", V), ("R", 784), ("P", 784), ("RF", W + L), ("PF", W), ("XF", W), ("XM", V), ("BF", W + L), ("BT", 800), ("UT", 800),
+          ("GR", 2 * GB_), ("GP", 2 * GB_), ("GB", 2 * GB_), ("RVB0", NE), ("RVB1", NE), ("PVB0", NE), ("PVB1", NE), ("XVB", NE), ("GX", NE),
+          ("AX", NE), ("A1", NE), ("A2", NE), ("BC", NE), ("GA", 2 * NE), ("GS", 2 * NE), ("RST", NR), ("E8", 256), ("IW", 160), ("NI", 128),
+          ("Z1", 144), ("ZO", 144), ("Z0", 144), ("ZN", 144), ("ZB", 144), ("ZS", 144), ("BO", 128), ("BN", 128), ("BW", 128), ("BQ", 128),
+          ("SW", 512), ("AE", 256), ("AT", 256), ("LW", 240), ("LM", 256), ("ON", 128), ("KC", 192), ("LC", 12), ("VL", 32), ("C3", G),
+          ("K6", 16), ("FT", 192), ("FR", 192), ("F2", 192), ("G2", 192), ("FE", L), ("FW", L), ("LE", 2 * L), ("YP", 12 * L), ("MN", L),
+          ("MX", L), ("WN", L), ("DX", L), ("OM", L), ("HM", L), ("CH", G), ("CN", G), ("SL", 784), ("SN0", 3 * CAP), ("SN1", 3 * CAP),
+          ("MB", 8), ("LR00", 3 * CAP), ("LR01", 3 * CAP), ("LR10", 3 * CAP), ("LR11", 3 * CAP)]
+    f4 = [("CF", V), ("IO", 800), ("IB", 128), ("I8", 256), ("KO", 32), ("RM", 16), ("WT", 32), ("CJ", 56), ("RK", 192), ("Y8", G),
+          ("KT", 192), ("KS", 192), ("KM", 16), ("NA", 32), ("THR", 16), ("TT", 16), ("DS", L), ("DC", L), ("SO", G), ("DT", 176), ("MC", 4)]
+    i4 = [("CI", V), ("SI", V), ("T8", 2), ("PI", 8), ("YI", 384), ("DI", 16), ("XS", L), ("MI", 8)]
+    u2 = [("CU", V), ("SU", V), ("RL", V), ("LS", 16), ("BL", 16), ("SC", 16), ("FL", 44), ("FG", 100), ("DL", 44), ("IL0", 16), ("IL1", 16),
+          ("LI00", 16), ("LI01", 16), ("LI10", 16), ("LI11", 16)]
+    for lst, d in ((bf, "bfloat16"), (f4, "float32"), (i4, "int32"), (u2, "uint16")):
+        for nm, w in lst:
+            SCRATCH[nm] = ("sbuf", [128, w], d)
+    for b in range(8):
+        SCRATCH["B%d" % b] = ("psum", [128, 512], "float32")
+
+
+_declare()
+SEMAPHORES = ["s_v", "s_s", "s_p", "s_g"] + ["d%d" % i for i in range(15)] + ["ar%d%d" % (i, b) for i in range(8) for b in range(2)] + ["lo%d" % i for i in range(8)]
+
+
+def tracker(g, T):
+    eng = {"v": g.vector, "s": g.scalar, "p": g.tensor, "g": g, "y": g.sync}
+    known = {e: {} for e in eng}
+    cnt = {e: 0 for e in eng}
+    recs = {}
+    total = {}
+
+    def view(name, lo=0, hi=None, st=1, p0=0, p1=128):
+        hi = SCRATCH[name][1][1] if hi is None else hi
+        t = T[name]
+        return (t[p0:p1, lo:hi] if st == 1 else t[p0:p1, lo:hi:st], [(name, lo, hi)])
+
+    def ind(win, off):
+        return (win[0].indirect(off[0]), win[1] + off[1])
+
+    def need(e, rec):
+        sem, val, clock, _ = rec
+        if known[e].get(sem, 0) < val:
+            eng[e].wait_ge(T.sem[sem], val)
+            for k, x in clock.items():
+                if known[e].get(k, 0) < x:
+                    known[e][k] = x
+
+    def depend(e, outs, ins):
+        deps = []
+        for (lst, wr) in ((ins, False), (outs, True)):
+            for v in lst:
+                for (name, lo, hi) in v[1]:
+                    bank = SCRATCH[name][0] == "psum"
+                    for (a, b, w, rec) in recs.get(name, []):
+                        if bank:
+                            if rec[3] != e:
+                                deps.append(rec)
+                        elif a < hi and lo < b and (wr or w):
+                            deps.append(rec)
+        deps.sort(key=lambda r: -r[1])
+        for r in deps:
+            need(e, r)
+
+    def note(rec, outs, ins):
+        for (lst, wr) in ((ins, False), (outs, True)):
+            for v in lst:
+                for (name, lo, hi) in v[1]:
+                    old = recs.get(name, [])
+                    if SCRATCH[name][0] == "psum":
+                        recs[name] = [(0, 512, True, rec)]
+                        continue
+                    if wr:
+                        old = [r for r in old if not (lo <= r[0] and r[1] <= hi)]
+                    else:
+                        old = [r for r in old if not (not r[2] and lo <= r[0] and r[1] <= hi and r[3][3] == rec[3] and rec[3] is not None)]
+                    recs[name] = old + [(lo, hi, wr, rec)]
+
+    def comp(e, fn, out, ins, *args, **kw):
+        depend(e, [out], ins)
+        cnt[e] += 1
+        sem = "s_" + e
+        rec = (sem, cnt[e], dict(known[e]), e)
+        rec[2][sem] = cnt[e]
+        fn(*args, **kw).then_inc(T.sem[sem], 1)
+        total[sem] = cnt[e]
+        note(rec, [out], ins)
+        return rec
+
+    def dma(e, sem, out, in_):
+        o = [out] if len(out) > 1 else []
+        i = [in_] if len(in_) > 1 else []
+        depend(e, o, i)
+        eng[e].dma_start(out[0], in_[0]).then_inc(T.sem[sem], 16)
+        rec = (sem, 16, dict(known[e]), None)
+        rec[2][sem] = 16
+        total[sem] = 16
+        note(rec, o, i)
+
+    def sent(call, sem, val, srcs):
+        depend("g", [], srcs)
+        call()
+        rec = (sem, val, dict(known["g"]), None)
+        rec[2][sem] = val
+        total[sem] = val
+        note(rec, [], srcs)
+
+    def arrives(sem, val, out):
+        total[sem] = val
+        note((sem, val, {sem: val}, None), [out], [])
+
+    def finish():
+        for k in sorted(total):
+            if known["y"].get(k, 0) < total[k]:
+                g.sync.wait_ge(T.sem[k], total[k])
+    return view, ind, comp, dma, sent, arrives, finish, need
+
+
+def rank_program(g, core, T, topo):
+    rank = T.rank_of(core)
+    if rank is None:
+        return
+    n = len(T.cores)
+
+    def shares(c):
+        q, used = T.rank_of(c), {}
+        for d in sorted([T.cores[(q - 1) % n], T.cores[(q + 1) % n]], key=lambda z: len(topo.engines(c, z))):
+            used[d] = [e for e in topo.engines(c, d) if not any(e in x for x in used.values())]
+        return used
+    nb = [(T.cores[(rank - 1) % n], 0), (T.cores[(rank + 1) % n], 1)]
+    eng = shares(core)
+    arrive_n = [len(shares(T.cores[(rank + 1) % n])[core]), len(shares(T.cores[(rank - 1) % n])[core])]
+    local_n = sum(len(x) for x in eng.values())
+
+    view, ind, comp, dma, sent, arrives, finish, need = tracker(g, T)
+    vec, sca, ten = g.vector, g.scalar, g.tensor
+
+    def cp(o, i): comp("v", vec.tensor_copy, o, [i], o[0], i[0])
+    def tt(o, a, b, op): comp("v", vec.tensor_tensor, o, [a, b], o[0], a[0], b[0], op)
+    def ts(o, a, s1, op0, s2=None, op1=None):
+        ins = [a] + [s for s in (s1, s2) if isinstance(s, tuple)]
+        u1 = s1[0] if isinstance(s1, tuple) else s1
+        u2 = s2[0] if isinstance(s2, tuple) else s2
+        if op1 is None:
+            comp("v", vec.tensor_scalar, o, ins, o[0], a[0], u1, None, op0)
+        else:
+            comp("v", vec.tensor_scalar, o, ins, o[0], a[0], u1, u2, op0, op1)
+    def ms(o, c): comp("v", vec.memset, o, [], o[0], c)
+    def scan(o, a, b, init, op0, op1): comp("v", vec.tensor_tensor_scan, o, [a, b], o[0], a[0], b[0], init, op0, op1)
+    def tr(o, i): comp("v", vec.transpose, o, [i], o[0], i[0])
+    def red(o, i): comp("v", vec.tensor_reduce, o, [i], o[0], i[0], AxisListType.X, A.add)
+    def act(o, i, f, bias=0.0): comp("s", sca.activation, o, [i], o[0], i[0], f, bias=bias)
+    def mm(o, l, r, start, stop): return comp("p", ten.matmul, o, [l, r], o[0], l[0], r[0], start, stop)
+    def iota(o, pat, base, cm): comp("g", g.iota, o, [], o[0], pat, base, cm, allow_small_or_imprecise_dtypes=True)
+    def gfill(name, lo, hi, c): iota(view(name, lo, hi), [[0, hi - lo]], c, 0)
+
+    I = view("IW", 16, 144)
+
+    def zq(z, q): return view(z, 15 - q, 143 - q)
+
+    def listed(o, z, name, lo, hi):
+        for q in range(16):
+            mm(o, zq(z, q), view(name, lo + q, hi, 16), q == 0, q == 15)
+
+    def fused(src, dst, arr, lsem):
+        out = []
+        for d, blk in nb:
+            rid, pid = topo.addr(d, core)
+            out.append(RemoteDMATransfer(dst_ids=[DstId(rid=rid, pnc=pid)], dma_engine_mask=sum(1 << e for e in eng[d]),
+                                         remote_sem=T.sem["%s%d" % (arr, blk)], src=src[0], dst=dst(blk)))
+        sent(lambda: g.remote_dma_fused(out, local_sem=T.sem[lsem]), lsem, local_n, [src])
+
+    dma("y", "d0", view("R", 0, V), (T.reach[:],))
+    comp("g", g.iota, view("PI", 0, 1), [], T.PI[:, 0:1], [[0, 1]], 0, 1)
+    iota(view("IO"), [[1, 800]], 0, 0)
+    dma("s", "d1", view("P", 0, V), (T.past[:],))
+    dma("y", "d2", view("CI"), (T.cand[:],))
+    dma("s", "d3", view("X"), (T.x[:],))
+    dma("y", "d4", view("SI"), (T.succ[:],))
+    dma("s", "d5", view("T8", 0, 1, 1, 0, 8), (T.th[:],))
+    fused(view("R", 0, G), lambda b: T.RF[:, V + G * b: V + G * b + G], "ar0", "lo0")
+    fused(view("P", 0, G), lambda b: T.PF[:, V + G * b: V + G * b + G], "ar1", "lo1")
+    for b in range(2):
+        arrives("ar0%d" % b, arrive_n[b], view("RF", V + G * b, V + G * b + G))
+        arrives("ar1%d" % b, arrive_n[b], view("PF", V + G * b, V + G * b + G))
+    iota(view("IB"), [[16, 8], [0, 16]], 0, 0)
+    for h in range(2):
+        iota(view("I8", 128 * h, 128 * h + 128, 1, 0, 8), [[2, 4], [0, 32]], h, -1)
+
+    def ko(i): return view("KO", i, i + 1)
+    def pi(i): return view("PI", i, i + 1)
+    def rm(i): return view("RM", i, i + 1)
+    ts(pi(1), pi(0), 15, A.bitwise_and)
+    ts(pi(2), pi(0), 112, A.bitwise_and)
+    ts(pi(3), pi(0), 4, A.arith_shift_right, 1, A.bitwise_and)
+    ts(pi(4), pi(0), 31, A.bitwise_and)
+    ts(pi(5), pi(0), 1, A.bitwise_and)
+    cp(ko(1), pi(2)); cp(ko(0), pi(1)); cp(ko(2), pi(3)); cp(ko(9), pi(4)); cp(ko(20), pi(5))
+    ts(ko(4), pi(0), 16.0, A.add)
+    ts(ko(5), ko(1), 15.0, A.add)
+    ts(view("IW"), view("IO", 0, 160), ko(4), A.is_equal)
+    ts(view("Z1"), view("IO", 0, 144), ko(5), A.is_equal)
+    ts(view("KC"), view("IO", 0, 192), 0.0, A.mult, ko(0), A.add)
+    ts(view("NI"), I, -1.0, A.mult)
+    ts(view("ZO"), view("Z1"), WO, A.mult)
+    ts(view("KC"), view("KC"), 1.0 / 16, A.mult)
+    gfill("XF", V, W, int(BIGX))
+    gfill("UT", 0, 800, 0)
+    for nm, w in (("RK", 192), ("FT", 192), ("F2", 192), ("WT", 16)):
+        gfill(nm, 0, w, 0)
+    for i in range(10):
+        gfill("WT", i, i + 1, 2 ** i)
+    gfill("BF", V, W + L, 0)
+    gfill("R", V, 784, 0); gfill("P", V, 784, 0)
+    gfill("LW", 0, 240, 0); gfill("LM", 0, 256, 0)
+    gfill("RF", W, W + L, 0)
+    gfill("RST", 0, NR, 0)
+    gfill("C3", 0, G, 113)
+    for nm in ("GB", "GR", "GP"):
+        for b in range(2):
+            gfill(nm, GB_ * b + G, GB_ * b + GB_, 0)
+
+    def spread(dst, src, t):
+        return [lambda k=k: cp(view(dst, k, NE, 16), view(src, t, V, 4)) for k in range(16)]
+
+    def spread_s(dst, src, t):
+        act(view(dst), ind(view(src, 0, V), view("RL", L * t, L * t + L)), AF.Copy)
+
+    def run(l):
+        for f in l:
+            f()
+
+    def xmask(dst, t):
+        ts(view(dst, t, V, 4), view("X", t, V, 4), 0.0, A.mult, BIGX, A.add)
+    for r in range(2):
+        ts(view("RL", L * r, L * r + L), view("IO", 0, V, 4), float(r), A.add)
+    cp(view("RF", 0, V), view("R", 0, V))
+    run(spread("RVB0", "R", 0))
+    cp(view("PF", 0, V), view("P", 0, V))
+    cp(view("CU", 0, L), view("CI", 0, V, 4))
+    cp(view("XF", 0, V), view("X"))
+    xmask("XF", 0)
+    spread_s("XVB", "X", 0)
+    run(spread("PVB0", "P", 0))
+
+    def key_x_gather(t):
+        act(view("GX"), ind(view("XF"), view("CU", L * t, L * t + L)), AF.Copy)
+
+    def key_start():
+        mm(view("B0", 0, 192), I, view("KC"), True, False)
+
+    CH = [(c, min(c + 512, NE), "B%d" % (2 + c // 512)) for c in range(0, NE, 512)]
+
+    def x_diff(lo, hi):
+        for c, e, b in CH[lo:hi]:
+            mm(view(b, 0, e - c), I, view("GX", c, e), True, False)
+            mm(view(b, 0, e - c), view("NI"), view("XVB", c, e), False, True)
+
+    def x_size(lo, hi):
+        for c, e, b in CH[lo:hi]:
+            act(view("AX", c, e), view(b, 0, e - c), AF.Abs)
+
+    def key_add(z, src, lo, hi, stop=False):
+        for k in range(16):
+            mm(view("B0", lo, hi), zq(z, k), view(src, 16 * lo + k, 16 * hi, 16), False, stop and k == 15)
+
+    def sig_part(which, first, last, bank=2):
+        z = {"P": "BO", "R": "BN", "BF": "BW"}[which]
+        for h in range(2):
+            mm(view("B%d" % (bank + h), 0, 336), view(z), view(which, 336 * h, 336 * h + 336), first, last)
+
+    def key_bits(t):
+        act(view("BC"), ind(view("BF", 0, W), view("CU", L * t, L * t + L)), AF.Copy)
+    ts(view("BO"), view("IB"), ko(1), A.is_equal)
+    ts(view("BN"), view("BO"), -1.0, A.mult)
+    sig_part("P", True, False, 6); sig_part("R", False, True, 6)
+    key_x_gather(0)
+    for h in range(2):
+        act(view("SO", 336 * h, 336 * h + 336), view("B%d" % (6 + h), 0, 336), AF.Copy)
+    key_start()
+    ts(view("E8", 0, 256, 1, 0, 8), view("I8", 0, 256, 1, 0, 8), 0.0, A.is_equal)
+    ts(view("MI", 4, 5, 1, 0, 8), view("T8", 0, 1, 1, 0, 8), 4080, A.bitwise_and)
+    ts(view("MI", 5, 6, 1, 0, 8), view("T8", 0, 1, 1, 0, 8), 15, A.bitwise_and)
+    cp(view("MB", 4, 6, 1, 0, 8), view("MI", 4, 6, 1, 0, 8))
+    for h in range(2):
+        for i in range(2):
+            mm(view("B1", h, h + 1), view("E8", 128 * h, 128 * h + 128, 1, 0, 8), view("MB", 4 + i, 5 + i, 1, 0, 8), i == 0, i == 1)
+
+    def chain_constants():
+        for b in range(6):
+            cp(view("THR", 2 * b, 2 * b + 2), view("B1", 0, 2))
+        cp(view("YI", 0, 50), view("IO", 0, 50))
+        for i in range(5):
+            ts(view("YI", 64 + i, 65 + i), pi(0), i, A.arith_shift_right, 1, A.bitwise_and)
+        for i in range(5):
+            ts(view("YI", 80 + 50 * i, 130 + 50 * i), view("YI", 0, 50), i + 1, A.arith_shift_right, 1, A.bitwise_and)
+        ts(view("KO", 24, 29), view("YI", 64, 69), 2.0, A.mult, -1.0, A.add)
+        for i in range(5):
+            ts(view("UT", 5 + i, 800, 16), view("YI", 80 + 50 * i, 130 + 50 * i), 2.0, A.mult, -1.0, A.add)
+        for i in range(5):
+            ts(view("UT", i, 800, 16), view("IO", 0, 50), 0.0, A.mult, ko(24 + i), A.add)
+        tr(view("BT"), view("UT"))
+        cp(view("BF", 0, V), view("BT", 0, V))
+        key_bits(0)
+        spread_s("PVB1", "P", 1)
+        ts(view("RK", 0, 192, 16), view("IO", 0, 12), 0.0, A.mult, 2.0 ** 28, A.add)
+        for h in range(2):
+            ts(view("FT", 16 * h + 12, 192, 32), view("IO", 0, 192, 32), ko(9), A.add)
+        for i in (13, 14, 15):
+            ts(view("FT", i, 192, 16), view("IO", 0, 12), 0.0, A.mult, 1.0, A.add)
+        for w in range(2):
+            ts(view("LC", 6 * w, 6 * w + 6), view("IO", 16 * w, 192, 32), ko(0), A.add, 16.0, A.mult)
+        ts(ko(3), ko(2), -1.0, A.mult, 1.0, A.add)
+        ts(view("RM"), view("IO", 0, 16), ko(0), A.is_equal)
+        for h in range(2):
+            for w in range(2):
+                z = 16 - 16 * (h - w)
+                ts(view("SW", 128 * (2 * h + w), 128 * (2 * h + w) + 128), view("IW", z, z + 128), ko(2 if w else 3), A.mult, 16.0, A.mult)
+        ts(ko(6), ko(0), 10.0, A.is_lt)
+        ts(ko(16), rm(13), 256.0, A.mult)
+        tt(ko(17), rm(10), rm(11), A.add)
+        ts(ko(15), ko(6), WB, A.mult)
+        ts(ko(17), ko(17), -256.0, A.mult)
+        ts(view("AT", 0, 128), I, ko(15), A.mult)
+        tt(ko(17), ko(17), rm(12), A.subtract)
+        for d, c in ((-3, ko(16)), (-2, ko(16)), (-1, rm(13)), (3, ko(17))):
+            ts(view("AT", 128, 256), view("IW", 16 - d, 144 - d), c, A.mult)
+            tt(view("AT", 0, 128), view("AT", 0, 128), view("AT", 128, 256), A.add)
+        for h in range(2):
+            ts(view("AE", 128 * h, 128 * h + 128), view("AT", 0, 128), ko(2 if h else 3), A.mult)
+        tt(view("WT", 16, 32), view("WT", 0, 16), view("RM"), A.mult)
+        red(ko(10), view("WT", 16, 32))
+        ts(ko(7), ko(10), 0.5, A.mult)
+        ts(view("ZB"), view("Z1"), ko(7), A.mult)
+
+    def rival_constants():
+        ts(view("BQ"), view("BO"), rm(0), A.mult, 512.0, A.mult)
+        ms(view("LW", 112, 128), 512.0)
+        ts(ko(18), ko(4), 75.0, A.is_lt, 512.0, A.mult)
+        ts(ko(19), ko(18), -1.0, A.mult, 512.0, A.add)
+        ts(view("LM", 112, 128), view("LM", 112, 128), ko(18), A.add)
+        ts(view("LM", 128, 144), view("LM", 128, 144), ko(19), A.add)
+        ts(view("TT", 0, 12), view("THR", 0, 12), 4096.0, A.min)
+
+    def merge_constants():
+        ts(ko(13), rm(13), -1536.0, A.mult)
+        ts(ko(14), rm(14), -0.5, A.mult)
+        tt(ko(13), ko(13), rm(12), A.subtract)
+        tt(ko(14), ko(14), ko(7), A.add)
+        ts(view("FL"), view("IO", 0, V, 16), ko(0), A.add)
+        tt(ko(13), ko(13), ko(14), A.add)
+        ts(view("VL", 0, 11), view("IO", 0, L, 16), ko(0), A.add)
+        ts(view("ZS"), view("Z1"), ko(13), A.mult)
+        ms(view("VL", 16, 27), float(DUMP))
+        cp(view("SU", 2 * L, 3 * L), view("SI", 2, V, 4))
+        cp(view("CF"), view("CI"))
+        cp(view("XM"), view("X"))
+        ts(view("RST", 0, NR, 16), view("IO", 0, NR // 16), 0.0, A.mult, 512.0, A.add)
+
+    def exchange_constants():
+        ts(view("BW"), view("BO"), ko(7), A.mult, 8192.0, A.mult)
+        ts(view("Y8"), view("IO", 0, G), 8192.0, A.mult, -511.5 * 8192.0, A.add)
+        tt(view("SO"), view("SO"), view("Y8"), A.add)
+        cp(view("CU", L, 2 * L), view("CI", 1, V, 4))
+        ts(view("Z0"), view("Z1"), rm(0), A.mult)
+        ts(view("ZN"), view("Z0"), -1024.0, A.mult)
+        ts(view("CJ", 0, 42), view("IO", 0, G, 16), ko(0), A.add, 112.0 - 1023.0, A.add)
+        ts(view("CJ", 44, 51), view("IO", 0, CAP, 16), ko(0), A.add, 672.0, A.add)
+        ms(view("ON"), 1.0 / 16)
+        ts(view("RL", 2 * L, 3 * L), view("IO", 0, V, 4), 2.0, A.add)
+
+    def ghost_constants():
+        for b in range(2):
+            w = GB_ * b
+            for i, (nm, src) in enumerate((("GR", view("RF", V + G * b, V + G * b + G)), ("GP", view("PF", V + G * b, V + G * b + G)), ("GB", view("BT", 0, G)))):
+                dma("y", "d%d" % (9 + 3 * b + i), view(nm, w, w + G), src)
+
+    def list_constants(t):
+        out = [lambda: cp(view("CU", L * t + L, L * t + 2 * L), view("CI", t + 1, V, 4))]
+        if t == 1:
+            out.append(lambda: cp(view("SU", 3 * L, 4 * L), view("SI", 3, V, 4)))
+            out.append(lambda: ts(view("RL", 3 * L, 4 * L), view("IO", 0, V, 4), 3.0, A.add))
+        return out
+
+    later = []
+
+    def fill(k):
+        for _ in range(min(k, len(later))):
+            later.pop(0)()
+
+    for t in range(RO):
+        last = t == RO - 1
+        cu = lambda lo, hi: view("CU", L * t + lo, L * t + hi)
+        su = lambda r, lo, hi: view("SU", L * r + lo, L * r + hi)
+        actv = lambda nm: view(nm, t, V, 4)
+        bl = view("BL", 0, 11)
+        pvb, rvb = "PVB%d" % (t % 2), "RVB%d" % (t % 2)
+        for lo, hi in ((0, 112), (112, L)):
+            tt(view("A1", 16 * lo, 16 * hi), ind(view("RF", 0, W), cu(lo, hi)), view(pvb, 16 * lo, 16 * hi), A.is_le)
+        for lo, hi in ((0, 112), (112, L)):
+            tt(view("A2", 16 * lo, 16 * hi), ind(view("PF"), cu(lo, hi)), view(rvb, 16 * lo, 16 * hi), A.is_ge)
+        if 0 < t < RO - 1:
+            spread_s("PVB%d" % ((t + 1) % 2), "P", t + 1)
+            spread_s("RVB%d" % ((t + 1) % 2), "R", t + 1)
+        key_add("ZO", "A1", 0, 112)
+        if t:
+            key_add("Z1", "AX", 32 * XC, L)
+        key_add("ZO", "A1", 112, L)
+        if t == 0:
+            x_diff(0, 6)
+            x_size(0, 6)
+            key_add("Z1", "AX", 0, L)
+        key_add("ZO", "A2", 0, 112)
+        key_add("ZO", "A2", 112, L, True)
+        if t == 0:
+            chain_constants()
+            ghost_constants()
+        if not last:
+            later.extend(list_constants(t) if t else [])
+            later.extend(spread("XVB", "X", t + 1))
+        fill(8)
+        tr(view("KT"), view("B0", 0, 192))
+        scan(view("KS"), view("RK"), view("KT"), 0.0, A.add, A.min)
+        ts(view("KM", 0, 12), view("KS", 15, 192, 16), 16000.0, A.min)
+        ts(view("DI", 0, 12), view("KM", 0, 12), -0.47, A.add)
+        tt(view("K6", 0, 12), view("KM", 0, 12), view("DI", 0, 12), A.subtract)
+        mm(view("B1", 0, 12), I, view("LC"), True, False)
+        for w in range(2):
+            for h in range(2):
+                j = 128 * (2 * h + w)
+                mm(view("B1", 6 * w, 6 * w + 6), view("SW", j, j + 128), view("K6", h, 12, 2), False, w == 1 and h == 1)
+        cp(view("FT", 10, 192, 16), view("DI", 0, 12))
+        tt(view("FT", 11, 192, 16), view("DI", 0, 12), view("FT", 10, 192, 16), A.subtract)
+        ts(view("OM"), view("B0", 0, L), WO, A.is_ge)
+        tr(view("FR"), view("FT"))
+        for w in range(2):
+            cp(view("LS", w, 12, 2), view("B1", 6 * w, 6 * w + 6))
+        tt(view("FE"), ind(view("BC"), view("LS", 0, 11)), view("FR", 0, L), A.add)
+        mm(view("B6", 0, L), view("AE", 0, 128), view("FE"), True, True)
+        mm(view("B7", 0, L), view("AE", 128, 256), view("FE"), True, True)
+        cp(view("LE", 0, L), view("B6", 0, L))
+        act(view("LE", L, 2 * L), view("B7", 0, L), AF.Copy)
+        listed(view("B0", 0, 11), "ZB", "FE", 0, L)
+        if t == 0:
+            rival_constants()
+        tt(view("NA", 0, 12), view("KM", 0, 12), view("TT", 0, 12), A.is_ge)
+        ts(view("NA", 16, 28), view("KM", 0, 12), 4096.0, A.is_ge, 2.0, A.mult)
+        cp(view("DS"), actv("SI"))
+        tt(view("F2", 0, 192, 16), view("NA", 0, 12), view("NA", 16, 28), A.add)
+        tr(view("G2"), view("F2"))
+        fill(4)
+        done = {}
+        for i in (0, 1, 2, 3, 4, 5, 6, 7, 8, 10, 9, 11):
+            a, j = TILES[i]
+            c = (0, 117, 234)[j]
+            if i in (9, 11):
+                need("p", done[i - 1])
+            done[i] = mm(view("B%d" % (2 + i // 2), L * (i % 2), L * (i % 2) + L, 1, 0, 118), view("LE", c, c + 118, 1, 32 * a, 32 * a + 32),
+                         view("FE", 0, L, 1, 32 * a, 32 * a + 32), True, True)
+        ts(bl, view("B0", 0, 11), 511.5, A.add)
+        mm(view("B0", 64, 64 + L), view("BQ"), view("G2", 0, L), True, True)
+        tt(view("MN"), ind(view("R"), bl), view(rvb, 0, NE, 16), A.min)
+        mm(view("B1", 0, L), I, view("MN"), True, False)
+        mm(view("B1", 0, L), view("BQ"), view("G2", 0, L), False, False)
+        for b in range(6):
+            o = view("YP", 352 * b, 352 * b + 352, 1, 0, 118)
+            i = view("B%d" % (2 + b), 0, 352, 1, 0, 118)
+            if b % 2 == 1:
+                ts(o, i, 10 * WB, A.is_gt)
+            else:
+                act(o, i, AF.Relu, -10 * WB)
+            for i in (2 * b, 2 * b + 1):
+                a, j = TILES[i]
+                if j == 1:
+                    l = view("LM", 112 - 32 * a, 240 - 32 * a, 1, 0, 118)
+                else:
+                    k = 112 - 16 * (2 * a + j // 2)
+                    l = view("LW", k, k + 128, 1, 0, 118)
+                mm(view("B1", 0, L), l, view("YP", L * i, L * i + L, 1, 0, 118), False, i == 11)
+        if t == 0:
+            merge_constants()
+        ts(view("HM"), view("B0", 64, 64 + L), 1000.0, A.is_lt)
+        tt(view("DS"), ind(view("SI"), bl), view("DS"), A.subtract)
+        ts(view("DS"), view("DS"), ko(20), A.mult)
+        tt(view("MX"), ind(view("P"), bl), view(pvb, 0, NE, 16), A.max)
+        fill(10)
+
+        def candidates():
+            cp(view("DC"), actv("CF"))
+            tt(view("HM"), view("HM"), view("OM"), A.mult)
+            tt(view("DC"), ind(view("CF"), bl), view("DC"), A.subtract)
+            tt(view("DC"), view("DC"), view("HM"), A.mult)
+            tt(actv("CF"), actv("CF"), view("DC"), A.add)
+
+        def halves():
+            tt(view("XS"), ind(view("XM"), bl), actv("X"), A.add)
+            ts(view("XS"), view("XS"), 1, A.arith_shift_right)
+            tt(view("DX"), view("XS"), actv("X"), A.subtract)
+
+        def features():
+            tt(view("DX"), view("DX"), view("WN"), A.mult)
+            tt(actv("X"), actv("X"), view("DX"), A.add)
+        mm(view("B0", 0, 11), I, view("VL", 0, 11), True, False)
+        mm(view("B0", 0, 11), I, view("VL", 16, 27), False, False)
+        ts(view("WN"), view("B1", 0, L), 512.0, A.is_lt)
+        tt(view("FW"), view("FE"), view("WN"), A.mult)
+        tt(actv("R"), view("B1", 0, L), actv("R"), A.min)
+        act(view("RF", 0, V), ind(view("R", 0, V), view("FL")), AF.Copy)
+        for q in range(16):
+            mm(view("B0", 0, 11), zq("ZS", q), view("FW", q, L, 16), False, q == 15)
+        tt(view("DS"), view("DS"), view("WN"), A.mult)
+        tt(actv("SI"), actv("SI"), view("DS"), A.add)
+        cp(view("SC", 0, 11), view("B0", 0, 11))
+        cp(su(t, 0, L), actv("SI"))
+        cp(ind(view("RF"), view("SC", 0, 11)), actv("R"))
+        o = (t + 2) % 4
+        rf = view("RF", 0, W)
+        v3 = VL3 if last else V3
+        for lo, hi in ((0, 88), (88, L)):
+            act(view("GA", 16 * lo, 16 * hi), ind(rf, su(o, lo, hi)), AF.Copy)
+        for lo, hi in ((v3, 112), (112, L)):
+            act(view("GA", NE + 16 * lo, NE + 16 * hi), ind(rf, su(t, lo, hi)), AF.Copy)
+        cp(view("GA", NE, NE + 16 * v3), ind(rf, su(t, 0, v3)))
+
+        def low(r, lo, hi):
+            a, e = (NE if r == t else 0) + 16 * lo, (NE if r == t else 0) + 16 * hi
+            scan(view("GS", a, e), view("RST", 0, e - a), view("GA", a, e), 0.0, A.add, A.min)
+            z = view("R", r + 4 * lo, r + 4 * hi - 3, 4)
+            tt(z, view("GS", a + 15, e, 16), z, A.min)
+        if not last:
+            cp(ind(view("BF"), view("SC", 0, 11)), view("BT", t, V, 4))
+            listed(view("B0", 0, 44), "ZB", "BF", 0, V)
+            tt(view("MX"), view("MX"), view("WN"), A.mult)
+            tt(actv("P"), actv("P"), view("MX"), A.max)
+            if t == 0:
+                exchange_constants()
+            sig_part("P", True, False)
+            sig_part("BF", False, False)
+        low(t, 0, v3)
+        if last:
+            halves()
+            features()
+            dma("y", "d7", (T.yx[:],), view("X"))
+        low(o, 0, 88)
+        if last:
+            candidates()
+            dma("y", "d8", (T.yc[:],), view("CF"))
+        else:
+            ts(view("FL"), view("B0", 0, 44), 511.5, A.add)
+        low(o, 88, L)
+        if not last:
+            halves()
+        low(t, v3, 112)
+        low(t, 112, L)
+        if last:
+            dma("y", "d6", (T.yr[:],), view("R", 0, V))
+            break
+        sig_part("R", False, True)
+        for h in range(2):
+            tt(view("CH", 336 * h, 336 * h + 336), view("B%d" % (2 + h), 0, 336), view("SO", 336 * h, 336 * h + 336), A.not_equal)
+        for h in range(2):
+            act(view("SO", 336 * h, 336 * h + 336), view("B%d" % (2 + h), 0, 336), AF.Copy)
+        act(view("PF", 0, V), ind(view("P", 0, V), view("FL")), AF.Copy)
+        for q in range(16):
+            mm(view("B1", 0, 42), zq("ZN", q), view("CH", q, G, 16), q == 0, False)
+        scan(view("CN"), view("CH"), view("C3"), 0.0, A.add, A.min)
+        for q in range(16):
+            mm(view("B1", 0, 42), zq("Z0", q), view("CN", q, G, 16), False, q == 15)
+        features()
+        cp(actv("XM"), actv("X"))
+        xmask("XM", t + 1)
+        act(view("XF", 0, V), ind(view("XM"), view("FL")), AF.Copy)
+        key_x_gather(t + 1)
+        key_bits(t + 1)
+        cp(view("SL", 0, CAP), view("BT", G, G + CAP))
+        ts(view("DT", 0, 42), view("B1", 0, 42), -911.0, A.is_ge, 4096.0, A.mult)
+        tt(view("DT", 44, 86), view("B1", 0, 42), view("DT", 0, 42), A.add)
+        tt(view("DT", 88, 130), view("DT", 44, 86), view("CJ", 0, 42), A.min)
+        ts(view("DL", 0, 42), view("DT", 88, 130), 1023.0, A.add)
+        cp(ind(view("SL"), view("DL", 0, 42)), view("BT", 0, G))
+        e = t % 2
+        il, sn = "IL%d" % e, "SN%d" % e
+        jl = view(il, 0, 7)
+        listed(view("B1", 0, 7), "ZB", "SL", 0, CAP)
+        ms(view(il, 7, 8), 0); ms(view(il, 15, 16), 0)
+        fill(2)
+        ts(jl, view("B1", 0, 7), 511.5, A.add)
+        cp(view(sn, 2 * CAP, 3 * CAP), ind(view("BF"), jl))
+        ts(view("DT", 132, 139), view("B1", 0, 7), 511.5, A.add)
+        listed(view("B1", 0, 7), "ZB", sn, 2 * CAP, 3 * CAP)
+        cp(view(sn, 0, CAP), ind(view("R"), jl))
+        cp(view(sn, CAP, 2 * CAP), ind(view("P"), jl))
+        fused(view(sn), lambda b: T["LR%d%d" % (e, b)][:], "ar%d" % (2 + 2 * t), "lo%d" % (2 + 2 * t))
+        tt(view("DT", 140, 147), view("CJ", 44, 51), view("DT", 132, 139), A.subtract)
+        ts(view("DT", 148, 155), view("B1", 0, 7), 160.0, A.is_ge)
+        tt(view("DT", 148, 155), view("DT", 148, 155), view("DT", 140, 147), A.mult)
+        tt(view("DT", 148, 155), view("DT", 148, 155), view("DT", 132, 139), A.add)
+        cp(view(il, 8, 15), view("DT", 148, 155))
+        fused(view(il), lambda b: T["LI%d%d" % (e, b)][:], "ar%d" % (3 + 2 * t), "lo%d" % (3 + 2 * t))
+        for b in range(2):
+            arrives("ar%d%d" % (2 + 2 * t, b), arrive_n[b], view("LR%d%d" % (e, b)))
+            arrives("ar%d%d" % (3 + 2 * t, b), arrive_n[b], view("LI%d%d" % (e, b)))
+        red(view("MC", 0, 1), view("WN"))
+        cp(view("MB", 0, 1), view("MC", 0, 1))
+        mm(view("B1", 0, 1), view("ON"), view("MB", 0, 1), True, True)
+        cp(view("RF", 0, V), ind(view("R", 0, V), view("FL")))
+        fill(99)
+        if t == 0:
+            spread_s("RVB1", "R", 1)
+        key_start()
+        x_diff(0, XC)
+        x_size(0, XC)
+        cp(view("MI", 0, 1), view("B1", 0, 1))
+        candidates()
+        ts(view("MI", 1, 2), view("MI", 0, 1), 31, A.bitwise_and)
+        cp(view("MC", 1, 2), view("MI", 1, 2))
+        ts(view("TT", 0, 12), view("THR", 0, 12), view("MC", 1, 2), A.add, 4096.0, A.min)
+
+        def taken(nm, lo, c):
+            for b in range(2):
+                cp(ind(view(nm, GB_ * b, GB_ * b + GB_), view("LI%d%d" % (e, b), lo, lo + 7)), view("LR%d%d" % (e, b), c, c + CAP))
+
+        def renamed(dst, nm, b):
+            return view(dst, V + G * b, V + G * b + G), ind(view(nm, GB_ * b, GB_ * b + GB_), view("FG", 50 * b, 50 * b + 42))
+        taken("GB", 8, 2 * CAP)
+        for q in range(16):
+            mm(view("B1", 0, 92), zq("ZB", q), view("GB", q, 1472, 16), q == 0, q == 15)
+        x_diff(XC, 6)
+        key_add("Z1", "AX", 0, 32 * XC)
+        taken("GR", 0, 0)
+        taken("GP", 0, CAP)
+        ts(view("FG", 0, 92), view("B1", 0, 92), 511.5, A.add)
+        cp(*renamed("RF", "GR", 0))
+        if t:
+            act(*renamed("RF", "GR", 1), AF.Copy)
+        else:
+            cp(*renamed("RF", "GR", 1))
+        for b in range(2):
+            act(*renamed("PF", "GP", b), AF.Copy)
+        x_size(XC, 6)
+    finish()

@@ -1,36 +1,43 @@
 from concourse.bass import DstId, RemoteDMATransfer
 from concourse.mybir import AluOpType as A, AxisListType, ActivationFunctionType as AF
+import math
 
 V, G, W, CAP, RO = 704, 672, 2048, 112, 4
 L = V // 4
+H = V // 2
 NE = 16 * L
 DUMP = W
-GB_ = 800
-XC = 3
-V3, VL3 = 56, 64
-NR = 16 * 88
+MV = 4
+NS_ = 8 - MV + 1
+XV_ = (3, 3, 3, 3)
+PS_ = (14, 14, 14, 14)
+CUTS = (0, 64, 128, L)
 BIGX = 512.0
 WO = 16384.0
 WB = 1048576.0
+BIGT = 114688.0
+MAGIC = 2.0 ** 31
 TILES = [(0, 0), (0, 1), (1, 0), (1, 1), (2, 0), (2, 1), (3, 0), (3, 1), (0, 2), (1, 2), (2, 2), (3, 2)]
 
+MATS = ["NI", "I256", "IBG", "NBG", "BO", "BN", "BW", "BV", "BQ"]
 SCRATCH = {}
 
 
 def _declare():
-    bf = [("X", V), ("R", 784), ("P", 784), ("RF", W + L), ("PF", W), ("XF", W), ("XM", V), ("BF", W + L), ("BT", 800), ("UT", 800),
-          ("GR", 2 * GB_), ("GP", 2 * GB_), ("GB", 2 * GB_), ("RVB0", NE), ("RVB1", NE), ("PVB0", NE), ("PVB1", NE), ("XVB", NE), ("GX", NE),
-          ("AX", NE), ("A1", NE), ("A2", NE), ("BC", NE), ("GA", 2 * NE), ("GS", 2 * NE), ("RST", NR), ("E8", 256), ("IW", 160), ("NI", 128),
-          ("Z1", 144), ("ZO", 144), ("Z0", 144), ("ZN", 144), ("ZB", 144), ("ZS", 144), ("BO", 128), ("BN", 128), ("BW", 128), ("BQ", 128),
-          ("SW", 512), ("AE", 256), ("AT", 256), ("LW", 240), ("LM", 256), ("ON", 128), ("KC", 192), ("LC", 12), ("VL", 32), ("C3", G),
-          ("K6", 16), ("FT", 192), ("FR", 192), ("F2", 192), ("G2", 192), ("FE", L), ("FW", L), ("LE", 2 * L), ("YP", 12 * L), ("MN", L),
-          ("MX", L), ("WN", L), ("DX", L), ("OM", L), ("HM", L), ("CH", G), ("CN", G), ("SL", 784), ("SN0", 3 * CAP), ("SN1", 3 * CAP),
-          ("MB", 8), ("LR00", 3 * CAP), ("LR01", 3 * CAP), ("LR10", 3 * CAP), ("LR11", 3 * CAP)]
-    f4 = [("CF", V), ("IO", 800), ("IB", 128), ("I8", 256), ("KO", 32), ("RM", 16), ("WT", 32), ("CJ", 56), ("RK", 192), ("Y8", G),
-          ("KT", 192), ("KS", 192), ("KM", 16), ("NA", 32), ("THR", 16), ("TT", 16), ("DS", L), ("DC", L), ("SO", G), ("DT", 176), ("MC", 4)]
-    i4 = [("CI", V), ("SI", V), ("T8", 2), ("PI", 8), ("YI", 384), ("DI", 16), ("XS", L), ("MI", 8)]
-    u2 = [("CU", V), ("SU", V), ("RL", V), ("LS", 16), ("BL", 16), ("SC", 16), ("FL", 44), ("FG", 100), ("DL", 44), ("IL0", 16), ("IL1", 16),
-          ("LI00", 16), ("LI01", 16), ("LI10", 16), ("LI11", 16)]
+    bf = [("XM", V), ("R", V), ("P", V), ("RF", W + L), ("PF", W), ("XF", W), ("BF", W + L), ("BT", V), ("LH", 64),
+          ("RV0", V), ("RV1", V), ("PV0", V), ("PV1", V), ("XV0", V), ("XV1", V), ("GX", NE), ("AX", NE), ("A1", NE), ("A2", NE), ("GP", NE),
+          ("BC", NE), ("GA", NE), ("GS", NE), ("GE", NS_ * H), ("GF", NS_ * H), ("AC", 2 * H), ("RS8", 1024), ("RSE", NS_ * H), ("E8", 256),
+          ("IW", 160), ("MAT", 128 * len(MATS)), ("Z1", 144), ("ZO", 144), ("Z0", 144), ("ZN", 144), ("ZD", 144),
+          ("ZB", 144), ("ZS", 144), ("SW", 512), ("AE", 256), ("AT", 640),
+          ("LW", 240), ("LM", 256), ("ON", 336), ("KC", 192), ("LC", 12), ("VL", 32), ("C3", G), ("K6", 16), ("FT", 192), ("FR", 192),
+          ("F2", 192), ("G2", 192), ("FE", L), ("FW", L), ("LE", 2 * L), ("YP", 12 * L), ("MN", L), ("MX", L), ("DX", L),
+          ("OM", L), ("NS", L), ("QQ", L), ("CH", G), ("CN", G + 16), ("MB", 8), ("M4", 4)]
+    f4 = [("CF", V), ("SF", V), ("IO", 192), ("IB", 128), ("I8", 256), ("KO", 40), ("RM", 16), ("WT", 96), ("RK", 192), ("KT", 192), ("KS", 192),
+          ("NA", 32), ("THR", 16), ("TT", 16), ("DS", L), ("DC", L), ("SV", L), ("CV", L), ("DT", 176), ("MC", 4), ("TP", G), ("T32", 2 * G),
+          ("Y", H), ("YT", H), ("EA", 256), ("FP", 44), ("YB", 256)]
+    i4 = [("CI", V), ("SI", V), ("SE32", H), ("T8", 2), ("PI", 8), ("YI", 96), ("DI", 16), ("XS", L), ("MI", 8)]
+    u2 = [("CK0", L), ("CK1", L), ("SE", H), ("SO", L), ("DL", 88), ("KL", 12), ("PL", 22), ("LS", 16), ("BL", 16), ("SC", 16), ("FL", 44),
+          ("FU", 44), ("SN", G), ("LU0", 2 * G), ("LU1", 2 * G)]
     for lst, d in ((bf, "bfloat16"), (f4, "float32"), (i4, "int32"), (u2, "uint16")):
         for nm, w in lst:
             SCRATCH[nm] = ("sbuf", [128, w], d)
@@ -39,7 +46,7 @@ def _declare():
 
 
 _declare()
-SEMAPHORES = ["s_v", "s_s", "s_p", "s_g"] + ["d%d" % i for i in range(15)] + ["ar%d%d" % (i, b) for i in range(8) for b in range(2)] + ["lo%d" % i for i in range(8)]
+SEMAPHORES = ["s_v", "s_s", "s_p", "s_g"] + ["d%d" % i for i in range(20)] + ["ar%d%d" % (i, b) for i in range(4) for b in range(2)] + ["lo%d" % i for i in range(4)]
 
 
 def tracker(g, T):
@@ -50,12 +57,20 @@ def tracker(g, T):
     total = {}
 
     def view(name, lo=0, hi=None, st=1, p0=0, p1=128):
+        if name in MATS:
+            name, lo, hi = "MAT", 128 * MATS.index(name), 128 * MATS.index(name) + 128
         hi = SCRATCH[name][1][1] if hi is None else hi
         t = T[name]
-        return (t[p0:p1, lo:hi] if st == 1 else t[p0:p1, lo:hi:st], [(name, lo, hi)])
+        return (t[p0:p1, lo:hi] if st == 1 else t[p0:p1, lo:hi:st], [(name, lo, hi, st)])
 
     def ind(win, off):
         return (win[0].indirect(off[0]), win[1] + off[1])
+
+    def meet(a, b):
+        return a[0] < b[1] and b[0] < a[1] and (a[0] - b[0]) % math.gcd(a[2], b[2]) == 0
+
+    def covers(a, b):
+        return a[0] <= b[0] and b[1] <= a[1] and (a[2] == 1 or (a[2] == b[2] and (a[0] - b[0]) % a[2] == 0))
 
     def need(e, rec):
         sem, val, clock, _ = rec
@@ -69,13 +84,12 @@ def tracker(g, T):
         deps = []
         for (lst, wr) in ((ins, False), (outs, True)):
             for v in lst:
-                for (name, lo, hi) in v[1]:
+                for (name, lo, hi, st) in v[1]:
                     bank = SCRATCH[name][0] == "psum"
-                    for (a, b, w, rec) in recs.get(name, []):
-                        if bank:
-                            if rec[3] != e:
-                                deps.append(rec)
-                        elif a < hi and lo < b and (wr or w):
+                    for (fp, w, rec) in recs.get(name, []):
+                        if bank and rec[3] != e:
+                            deps.append(rec)
+                        elif (e != "p" or not bank) and (wr or w) and meet(fp, (lo, hi, st)):
                             deps.append(rec)
         deps.sort(key=lambda r: -r[1])
         for r in deps:
@@ -84,16 +98,16 @@ def tracker(g, T):
     def note(rec, outs, ins):
         for (lst, wr) in ((ins, False), (outs, True)):
             for v in lst:
-                for (name, lo, hi) in v[1]:
+                for (name, lo, hi, st) in v[1]:
                     old = recs.get(name, [])
                     if SCRATCH[name][0] == "psum":
-                        recs[name] = [(0, 512, True, rec)]
-                        continue
+                        old = [r for r in old if r[2][3] == rec[3] != "p"]
+                    fp = (lo, hi, st)
                     if wr:
-                        old = [r for r in old if not (lo <= r[0] and r[1] <= hi)]
+                        old = [r for r in old if not covers(fp, r[0])]
                     else:
-                        old = [r for r in old if not (not r[2] and lo <= r[0] and r[1] <= hi and r[3][3] == rec[3] and rec[3] is not None)]
-                    recs[name] = old + [(lo, hi, wr, rec)]
+                        old = [r for r in old if not (not r[1] and covers(fp, r[0]) and r[2][3] == rec[3] and rec[3] is not None)]
+                    recs[name] = old + [(fp, wr, rec)]
 
     def comp(e, fn, out, ins, *args, **kw):
         depend(e, [out], ins)
@@ -123,6 +137,7 @@ def tracker(g, T):
         rec[2][sem] = val
         total[sem] = val
         note(rec, [], srcs)
+        return rec
 
     def arrives(sem, val, out):
         total[sem] = val
@@ -148,8 +163,10 @@ def rank_program(g, core, T, topo):
         return used
     nb = [(T.cores[(rank - 1) % n], 0), (T.cores[(rank + 1) % n], 1)]
     eng = shares(core)
-    arrive_n = [len(shares(T.cores[(rank + 1) % n])[core]), len(shares(T.cores[(rank - 1) % n])[core])]
+    source = [T.cores[(rank + 1) % n], T.cores[(rank - 1) % n]]
+    arrive_n = [len(shares(c)[core]) for c in source]
     local_n = sum(len(x) for x in eng.values())
+    near, far = sorted((0, 1), key=lambda b: source[b] not in topo.cores_of(core))
 
     view, ind, comp, dma, sent, arrives, finish, need = tracker(g, T)
     vec, sca, ten = g.vector, g.scalar, g.tensor
@@ -169,305 +186,343 @@ def rank_program(g, core, T, topo):
     def tr(o, i): comp("v", vec.transpose, o, [i], o[0], i[0])
     def red(o, i): comp("v", vec.tensor_reduce, o, [i], o[0], i[0], AxisListType.X, A.add)
     def act(o, i, f, bias=0.0): comp("s", sca.activation, o, [i], o[0], i[0], f, bias=bias)
+    def scaled(o, i, c):
+        col = isinstance(c, tuple)
+        comp("s", sca.activation, o, [i, c] if col else [i], o[0], i[0], AF.Copy, scale=c[0] if col else c)
     def mm(o, l, r, start, stop): return comp("p", ten.matmul, o, [l, r], o[0], l[0], r[0], start, stop)
     def iota(o, pat, base, cm): comp("g", g.iota, o, [], o[0], pat, base, cm, allow_small_or_imprecise_dtypes=True)
-    def gfill(name, lo, hi, c): iota(view(name, lo, hi), [[0, hi - lo]], c, 0)
+    def gfill(o, c): iota(o, [[0, len(range(*o[1][0][1:]))]], c, 0)
+    def gcopy(o, i): comp("g", g.affine_select, o, [i], o[0], i[0], [[0, len(range(*o[1][0][1:]))]], A.is_ge, 0.0, 0, 0)
 
     I = view("IW", 16, 144)
 
     def zq(z, q): return view(z, 15 - q, 143 - q)
 
-    def listed(o, z, name, lo, hi):
+    def listed(o, z, name, lo, hi, start=True, stop=True):
         for q in range(16):
-            mm(o, zq(z, q), view(name, lo + q, hi, 16), q == 0, q == 15)
+            mm(o, zq(z, q), view(name, lo + q, hi, 16), start and q == 0, stop and q == 15)
 
-    def fused(src, dst, arr, lsem):
+    def send(e):
         out = []
+        src = view("SN")
         for d, blk in nb:
             rid, pid = topo.addr(d, core)
-            out.append(RemoteDMATransfer(dst_ids=[DstId(rid=rid, pnc=pid)], dma_engine_mask=sum(1 << e for e in eng[d]),
-                                         remote_sem=T.sem["%s%d" % (arr, blk)], src=src[0], dst=dst(blk)))
-        sent(lambda: g.remote_dma_fused(out, local_sem=T.sem[lsem]), lsem, local_n, [src])
-
-    dma("y", "d0", view("R", 0, V), (T.reach[:],))
-    comp("g", g.iota, view("PI", 0, 1), [], T.PI[:, 0:1], [[0, 1]], 0, 1)
-    iota(view("IO"), [[1, 800]], 0, 0)
-    dma("s", "d1", view("P", 0, V), (T.past[:],))
-    dma("y", "d2", view("CI"), (T.cand[:],))
-    dma("s", "d3", view("X"), (T.x[:],))
-    dma("y", "d4", view("SI"), (T.succ[:],))
-    dma("s", "d5", view("T8", 0, 1, 1, 0, 8), (T.th[:],))
-    fused(view("R", 0, G), lambda b: T.RF[:, V + G * b: V + G * b + G], "ar0", "lo0")
-    fused(view("P", 0, G), lambda b: T.PF[:, V + G * b: V + G * b + G], "ar1", "lo1")
-    for b in range(2):
-        arrives("ar0%d" % b, arrive_n[b], view("RF", V + G * b, V + G * b + G))
-        arrives("ar1%d" % b, arrive_n[b], view("PF", V + G * b, V + G * b + G))
-    iota(view("IB"), [[16, 8], [0, 16]], 0, 0)
-    for h in range(2):
-        iota(view("I8", 128 * h, 128 * h + 128, 1, 0, 8), [[2, 4], [0, 32]], h, -1)
+            out.append(RemoteDMATransfer(dst_ids=[DstId(rid=rid, pnc=pid)], dma_engine_mask=sum(1 << x for x in eng[d]),
+                                         remote_sem=T.sem["ar%d%d" % (e, blk)], src=src[0], dst=T["LU%d" % (e % 2)][:, G * blk: G * blk + G]))
+        rec = sent(lambda: g.remote_dma_fused(out, local_sem=T.sem["lo%d" % e]), "lo%d" % e, local_n, [src])
+        for b in range(2):
+            arrives("ar%d%d" % (e, b), arrive_n[b], view("LU%d" % (e % 2), G * b, G * b + G))
+        return rec
 
     def ko(i): return view("KO", i, i + 1)
     def pi(i): return view("PI", i, i + 1)
     def rm(i): return view("RM", i, i + 1)
-    ts(pi(1), pi(0), 15, A.bitwise_and)
-    ts(pi(2), pi(0), 112, A.bitwise_and)
-    ts(pi(3), pi(0), 4, A.arith_shift_right, 1, A.bitwise_and)
-    ts(pi(4), pi(0), 31, A.bitwise_and)
-    ts(pi(5), pi(0), 1, A.bitwise_and)
-    cp(ko(1), pi(2)); cp(ko(0), pi(1)); cp(ko(2), pi(3)); cp(ko(9), pi(4)); cp(ko(20), pi(5))
-    ts(ko(4), pi(0), 16.0, A.add)
-    ts(ko(5), ko(1), 15.0, A.add)
-    ts(view("IW"), view("IO", 0, 160), ko(4), A.is_equal)
-    ts(view("Z1"), view("IO", 0, 144), ko(5), A.is_equal)
-    ts(view("KC"), view("IO", 0, 192), 0.0, A.mult, ko(0), A.add)
-    ts(view("NI"), I, -1.0, A.mult)
-    ts(view("ZO"), view("Z1"), WO, A.mult)
-    ts(view("KC"), view("KC"), 1.0 / 16, A.mult)
-    gfill("XF", V, W, int(BIGX))
-    gfill("UT", 0, 800, 0)
-    for nm, w in (("RK", 192), ("FT", 192), ("F2", 192), ("WT", 16)):
-        gfill(nm, 0, w, 0)
-    for i in range(10):
-        gfill("WT", i, i + 1, 2 ** i)
-    gfill("BF", V, W + L, 0)
-    gfill("R", V, 784, 0); gfill("P", V, 784, 0)
-    gfill("LW", 0, 240, 0); gfill("LM", 0, 256, 0)
-    gfill("RF", W, W + L, 0)
-    gfill("RST", 0, NR, 0)
-    gfill("C3", 0, G, 113)
-    for nm in ("GB", "GR", "GP"):
-        for b in range(2):
-            gfill(nm, GB_ * b + G, GB_ * b + GB_, 0)
+    def half(nm, h, lo=0): return view(nm, lo + 336 * h, lo + 336 * h + 336)
+    def bank(b, w=336, lo=0): return view("B%d" % b, lo, lo + w)
 
-    def spread(dst, src, t):
-        return [lambda k=k: cp(view(dst, k, NE, 16), view(src, t, V, 4)) for k in range(16)]
+    def fourfold(dst, src, t, copy):
+        copy(view(dst, 0, L), view(src, t, V, 4))
+        copy(view(dst, L, 2 * L), view(dst, 0, L))
+        copy(view(dst, 2 * L, 4 * L), view(dst, 0, 2 * L))
 
-    def spread_s(dst, src, t):
-        act(view(dst), ind(view(src, 0, V), view("RL", L * t, L * t + L)), AF.Copy)
-
-    def run(l):
-        for f in l:
-            f()
-
-    def xmask(dst, t):
-        ts(view(dst, t, V, 4), view("X", t, V, 4), 0.0, A.mult, BIGX, A.add)
-    for r in range(2):
-        ts(view("RL", L * r, L * r + L), view("IO", 0, V, 4), float(r), A.add)
-    cp(view("RF", 0, V), view("R", 0, V))
-    run(spread("RVB0", "R", 0))
-    cp(view("PF", 0, V), view("P", 0, V))
-    cp(view("CU", 0, L), view("CI", 0, V, 4))
-    cp(view("XF", 0, V), view("X"))
-    xmask("XF", 0)
-    spread_s("XVB", "X", 0)
-    run(spread("PVB0", "P", 0))
-
-    def key_x_gather(t):
-        act(view("GX"), ind(view("XF"), view("CU", L * t, L * t + L)), AF.Copy)
+    def ck(t, k0, k1): return view("CK%d" % (t % 2), 11 * k0, 11 * k1)
+    def ent(nm, k0, k1): return view(nm, L * k0, L * k1)
 
     def key_start():
-        mm(view("B0", 0, 192), I, view("KC"), True, False)
+        mm(bank(0, 192), I, view("KC"), True, False)
 
-    CH = [(c, min(c + 512, NE), "B%d" % (2 + c // 512)) for c in range(0, NE, 512)]
+    def key_add(z, src, k0, k1, stop=False):
+        for k in range(k0, k1):
+            mm(bank(0, L), zq(z, k), ent(src, k, k + 1), False, stop and k == k1 - 1)
 
-    def x_diff(lo, hi):
-        for c, e, b in CH[lo:hi]:
-            mm(view(b, 0, e - c), I, view("GX", c, e), True, False)
-            mm(view(b, 0, e - c), view("NI"), view("XVB", c, e), False, True)
+    def diff(src, own, k, b):
+        mm(bank(b, H), I, ent(src, k, k + 2), True, False)
+        mm(bank(b, H), view("NI"), view(own, 0, H), False, True)
 
-    def x_size(lo, hi):
-        for c, e, b in CH[lo:hi]:
-            act(view("AX", c, e), view(b, 0, e - c), AF.Abs)
+    def x_vector(t, c):
+        tt(ent("GX", 4 * c, 4 * c + 4), ind(view("XF"), ck(t, 4 * c, 4 * c + 4)), view("XV%d" % (t % 2)), A.subtract)
 
-    def key_add(z, src, lo, hi, stop=False):
-        for k in range(16):
-            mm(view("B0", lo, hi), zq(z, k), view(src, 16 * lo + k, 16 * hi, 16), False, stop and k == 15)
+    def x_size(c):
+        act(ent("AX", 4 * c, 4 * c + 4), ent("GX", 4 * c, 4 * c + 4), AF.Abs)
+        key_add("Z1", "AX", 4 * c, 4 * c + 4)
 
-    def sig_part(which, first, last, bank=2):
-        z = {"P": "BO", "R": "BN", "BF": "BW"}[which]
-        for h in range(2):
-            mm(view("B%d" % (bank + h), 0, 336), view(z), view(which, 336 * h, 336 * h + 336), first, last)
+    def x_scalar(t, c):
+        act(ent("GX", 4 * c, 4 * c + 4), ind(view("XF"), ck(t, 4 * c, 4 * c + 4)), AF.Copy)
+        for i in range(2):
+            diff("GX", "XV%d" % (t % 2), 4 * c + 2 * i, 2 + i)
 
-    def key_bits(t):
-        act(view("BC"), ind(view("BF", 0, W), view("CU", L * t, L * t + L)), AF.Copy)
-    ts(view("BO"), view("IB"), ko(1), A.is_equal)
-    ts(view("BN"), view("BO"), -1.0, A.mult)
-    sig_part("P", True, False, 6); sig_part("R", False, True, 6)
-    key_x_gather(0)
+    def x_scalar_size(c):
+        for i in range(2):
+            act(ent("AX", 4 * c + 2 * i, 4 * c + 2 * i + 2), bank(2 + i, H), AF.Abs)
+        key_add("Z1", "AX", 4 * c, 4 * c + 4)
+
+    def key_bits(t, c):
+        act(ent("BC", 4 * c, 4 * c + 4), ind(view("BF", 0, W), ck(t, 4 * c, 4 * c + 4)), AF.Copy)
+
+    def window(t, bits):
+        nv = XV_[t]
+        bits = list(bits)
+        for c in range(nv):
+            x_vector(t, c)
+        for c in range(nv, 4):
+            x_scalar(t, c)
+            key_bits(t, bits.pop(0))
+            x_scalar_size(c)
+        for c in range(nv):
+            x_size(c)
+            if bits:
+                key_bits(t, bits.pop(0))
+
+    def sig(parts, first, last):
+        for i, (z, nm) in enumerate(parts):
+            for h in range(2):
+                mm(bank(2 + h), view(z), half(nm, h), first and i == 0, last and i == len(parts) - 1)
+
+    dma("y", "d0", view("R"), (T.reach[:],))
+    dma("s", "d1", view("P"), (T.past[:],))
+    comp("g", g.iota, view("PI", 0, 1), [], T.PI[:, 0:1], [[0, 1]], 0, 1)
+    iota(view("IO"), [[1, 192]], 0, 0)
+    dma("y", "d2", view("CI"), (T.cand[:],))
+    dma("s", "d3", view("XM"), (T.x[:],))
+    dma("y", "d5", view("T8", 0, 1, 1, 0, 8), (T.th[:],))
+    dma("y", "d17", view("PF", 0, V), (T.past[:],))
+    dma("y", "d18", view("RF", 0, V), (T.reach[:],))
+    iota(view("IB"), [[16, 8], [0, 16]], 0, 0)
     for h in range(2):
-        act(view("SO", 336 * h, 336 * h + 336), view("B%d" % (6 + h), 0, 336), AF.Copy)
-    key_start()
+        iota(view("I8", 128 * h, 128 * h + 128, 1, 0, 8), [[2, 4], [0, 32]], h, -1)
+    iota(view("RK"), [[0, 12], [-16000, 16]], 16000, 0)
+    gfill(view("FT"), -2)
+    gfill(view("F2"), 0)
+    for i, m in ((1, 15), (2, 112), (3, 16), (4, 31), (5, 1)):
+        ts(pi(i), pi(0), m, A.bitwise_and)
+    ts(ko(4), pi(0), 16.0, A.add)
+    cp(view("KO", 0, 2), view("PI", 1, 3))
+    ts(view("IW"), view("IO", 0, 160), ko(4), A.is_equal)
+    ts(view("RM"), view("IO", 0, 16), ko(0), A.is_equal)
+    ms(view("WT", 16, 32), 0.5)
+    ts(ko(5), pi(2), 15.0, A.add)
+    ts(ko(2), pi(3), 1.0 / 16, A.mult)
+    scaled(view("I256"), I, 256.0)
+    scaled(view("NI"), I, -1.0)
+    scan(view("WT", 0, 16), view("WT", 16, 32), view("WT", 16, 32), 1.0, A.mult, A.min)
+    ts(view("YB", 0, 32), view("IO", 0, 32), 0.5, A.add)
+    ts(view("YB", 32, 54), view("IO", 0, 22), 32.0, A.mult, 0.5, A.add)
+    tt(view("WT", 32, 48), view("WT", 0, 16), view("RM"), A.mult)
+    ts(ko(6), ko(0), 10.0, A.is_lt)
+    tt(ko(17), rm(10), rm(11), A.add)
+    red(ko(10), view("WT", 32, 48))
+    ts(ko(11), ko(6), 2.0, A.mult)
+    tt(ko(12), ko(17), rm(12), A.add)
+    ts(view("YB", 64, 118), view("YB", 0, 54), ko(10), A.mult)
+    ts(view("YI", 0, 54), view("YB", 0, 54), ko(10), A.mult)
+    ts(ko(12), ko(12), -512.0, A.mult, ko(6), A.subtract)
+    ts(view("Z1"), view("IO", 0, 144), ko(5), A.is_equal)
+    tt(view("YB", 0, 54), view("YI", 0, 54), view("YB", 64, 118), A.is_gt)
+    ts(ko(3), ko(2), -1.0, A.mult, 1.0, A.add)
+    ts(view("KO", 22, 24), view("KO", 2, 4), 16.0 * L, A.mult)
+    ts(view("LH", 0, 32), view("YB", 0, 32), ko(11), A.mult)
+    ts(view("LH", 32, 54), view("YB", 32, 54), ko(11), A.mult, ko(12), A.add)
+    for h in range(2):
+        mm(bank(4 + h), view("I256"), half("P", h), True, False)
+        mm(bank(4 + h), view("NI"), half("R", h), False, True)
+    for b in range(22):
+        mm(bank(6 + b // 11, 32, 32 * (b % 11)), I, view("LH", 0, 32), b % 11 == 0, False)
+    for h in range(2):
+        for s in range(32):
+            mm(view("B%d" % (6 + h), s, H, 32), I, view("LH", 32 + 11 * h, 43 + 11 * h), False, s == 31)
+    scaled(view("ZO"), view("Z1"), WO)
+    for h in range(2):
+        for w in range(2):
+            z = 16 - 16 * (h - w)
+            scaled(view("SW", 128 * (2 * h + w), 128 * (2 * h + w) + 128), view("IW", z, z + 128), ko(22 if w else 23))
+    ts(ko(16), rm(13), 256.0, A.mult)
+    ts(ko(15), ko(6), WB, A.mult)
+    ts(ko(17), ko(17), -256.0, A.mult, rm(12), A.subtract)
+    for i, (z, c) in enumerate(((16, ko(15)), (19, ko(16)), (18, ko(16)), (17, rm(13)), (13, ko(17)))):
+        scaled(view("AT", 128 * i, 128 * i + 128), view("IW", z, z + 128), c)
+    ts(view("YB", 128, 139), view("IO", 0, L, 16), ko(0), A.add)
+    ts(ko(24), ko(0), 4.0, A.mult)
+    ts(view("DI", 0, 11), view("YB", 128, 139), -5.0, A.add, 1.0 / 11, A.mult)
+    for w in range(2):
+        ts(view("DL", w, 22, 2), view("IO", 0, L, 16), 4.0, A.mult, ko(24), A.add)
+    ts(view("YB", 144, 155), view("YB", 128, 139), 32.0, A.mult)
+    ts(view("YB", 160, 171), view("DI", 0, 11), -351.0, A.mult)
+    ts(ko(8), ko(2), 16.0, A.mult)
+    tt(view("YB", 160, 171), view("YB", 160, 171), view("YB", 144, 155), A.add)
+    ts(ko(25), ko(0), 1.0 / 16, A.mult)
+    ts(view("KL", 0, 11), view("YB", 160, 171), ko(8), A.add)
+    for h in range(2):
+        ts(half("SN", h), bank(4 + h), 256.0, A.add)
+    first_sent = send(0)
+    ms(view("XF", V, W), BIGX)
+    ts(view("KC"), view("IO"), 0.0, A.mult, ko(25), A.add)
+    for h in range(2):
+        act(half("TP", h), bank(4 + h), AF.Copy)
+    for h in range(2):
+        act(view("BF", H * h, H * h + H), bank(6 + h, H), AF.Copy)
     ts(view("E8", 0, 256, 1, 0, 8), view("I8", 0, 256, 1, 0, 8), 0.0, A.is_equal)
     ts(view("MI", 4, 5, 1, 0, 8), view("T8", 0, 1, 1, 0, 8), 4080, A.bitwise_and)
     ts(view("MI", 5, 6, 1, 0, 8), view("T8", 0, 1, 1, 0, 8), 15, A.bitwise_and)
+    cp(ko(9), pi(4))
     cp(view("MB", 4, 6, 1, 0, 8), view("MI", 4, 6, 1, 0, 8))
     for h in range(2):
         for i in range(2):
-            mm(view("B1", h, h + 1), view("E8", 128 * h, 128 * h + 128, 1, 0, 8), view("MB", 4 + i, 5 + i, 1, 0, 8), i == 0, i == 1)
+            mm(bank(1, 1, h), view("E8", 128 * h, 128 * h + 128, 1, 0, 8), view("MB", 4 + i, 5 + i, 1, 0, 8), h == 0 and i == 0, h == 1 and i == 1)
+    for i in range(5):
+        mm(bank(2, 128), I, view("AT", 128 * i, 128 * i + 128), i == 0, i == 4)
+    for h in range(2):
+        scaled(view("AE", 128 * h, 128 * h + 128), bank(2, 128), ko(2 if h else 3))
+    ms(view("BF", V, W + L), 0.0)
+    cp(view("Y"), ind(view("CI"), view("DL", 0, 22)))
+    fourfold("XV0", "XM", 0, cp)
+    tr(view("YT"), view("Y"))
+    ms(view("XM", 0, V, 4), BIGX)
+    cp(view("CK0"), ind(view("YT"), view("KL", 0, 11)))
+    cp(view("XF", 0, V), view("XM"))
+    key_start()
+    need("y", first_sent)
+    dma("y", "d4", view("SI"), (T.succ[:],))
+    for k in range(8):
+        dma("y", "d%d" % (9 + k), view("SE32", 44 * k, 44 * k + 44), (T.succ[2 * k::16, :],))
+    fourfold("RV0", "R", 0, gcopy)
+    fourfold("PV0", "P", 0, gcopy)
+    gfill(view("RF", W, W + L), 0)
+    gfill(view("NS"), 0)
+    iota(view("M4"), [[-1, 4]], -1, 0)
+    key_bits(0, 0)
+    window(0, (1, 2, 3))
 
-    def chain_constants():
-        for b in range(6):
-            cp(view("THR", 2 * b, 2 * b + 2), view("B1", 0, 2))
-        cp(view("YI", 0, 50), view("IO", 0, 50))
-        for i in range(5):
-            ts(view("YI", 64 + i, 65 + i), pi(0), i, A.arith_shift_right, 1, A.bitwise_and)
-        for i in range(5):
-            ts(view("YI", 80 + 50 * i, 130 + 50 * i), view("YI", 0, 50), i + 1, A.arith_shift_right, 1, A.bitwise_and)
-        ts(view("KO", 24, 29), view("YI", 64, 69), 2.0, A.mult, -1.0, A.add)
-        for i in range(5):
-            ts(view("UT", 5 + i, 800, 16), view("YI", 80 + 50 * i, 130 + 50 * i), 2.0, A.mult, -1.0, A.add)
-        for i in range(5):
-            ts(view("UT", i, 800, 16), view("IO", 0, 50), 0.0, A.mult, ko(24 + i), A.add)
-        tr(view("BT"), view("UT"))
-        cp(view("BF", 0, V), view("BT", 0, V))
-        key_bits(0)
-        spread_s("PVB1", "P", 1)
-        ts(view("RK", 0, 192, 16), view("IO", 0, 12), 0.0, A.mult, 2.0 ** 28, A.add)
+    def thresholds():
+        ms(view("LW"), 0.0); ms(view("LM"), 0.0)
         for h in range(2):
             ts(view("FT", 16 * h + 12, 192, 32), view("IO", 0, 192, 32), ko(9), A.add)
         for i in (13, 14, 15):
-            ts(view("FT", i, 192, 16), view("IO", 0, 12), 0.0, A.mult, 1.0, A.add)
-        for w in range(2):
-            ts(view("LC", 6 * w, 6 * w + 6), view("IO", 16 * w, 192, 32), ko(0), A.add, 16.0, A.mult)
-        ts(ko(3), ko(2), -1.0, A.mult, 1.0, A.add)
-        ts(view("RM"), view("IO", 0, 16), ko(0), A.is_equal)
+            ms(view("FT", i, 192, 16), 1.0)
+        ts(view("LC"), view("IO", 0, 192, 16), ko(0), A.add)
+        ms(view("WT", 48, 64), 2.0)
+        cp(ko(20), pi(5))
+        scan(view("WT", 64, 80), view("WT", 48, 64), view("F2", 0, 16), 0.25, A.mult, A.add)
+        ts(view("BO"), view("IB"), ko(1), A.is_equal)
+        tt(view("WT", 80, 96), view("WT", 64, 80), view("RM"), A.mult)
+        ts(ko(18), ko(4), 75.0, A.is_lt, 512.0, A.mult)
+        red(ko(10), view("WT", 80, 96))
+        ts(ko(19), ko(18), -1.0, A.mult, 512.0, A.add)
+        tt(ko(7), ko(10), ko(6), A.mult)
         for h in range(2):
-            for w in range(2):
-                z = 16 - 16 * (h - w)
-                ts(view("SW", 128 * (2 * h + w), 128 * (2 * h + w) + 128), view("IW", z, z + 128), ko(2 if w else 3), A.mult, 16.0, A.mult)
-        ts(ko(6), ko(0), 10.0, A.is_lt)
-        ts(ko(16), rm(13), 256.0, A.mult)
-        tt(ko(17), rm(10), rm(11), A.add)
-        ts(ko(15), ko(6), WB, A.mult)
-        ts(ko(17), ko(17), -256.0, A.mult)
-        ts(view("AT", 0, 128), I, ko(15), A.mult)
-        tt(ko(17), ko(17), rm(12), A.subtract)
-        for d, c in ((-3, ko(16)), (-2, ko(16)), (-1, rm(13)), (3, ko(17))):
-            ts(view("AT", 128, 256), view("IW", 16 - d, 144 - d), c, A.mult)
-            tt(view("AT", 0, 128), view("AT", 0, 128), view("AT", 128, 256), A.add)
-        for h in range(2):
-            ts(view("AE", 128 * h, 128 * h + 128), view("AT", 0, 128), ko(2 if h else 3), A.mult)
-        tt(view("WT", 16, 32), view("WT", 0, 16), view("RM"), A.mult)
-        red(ko(10), view("WT", 16, 32))
-        ts(ko(7), ko(10), 0.5, A.mult)
+            ts(view("THR", h, 12, 2), view("IO", 0, 6), 0.0, A.mult, bank(1, 1, h), A.add)
         ts(view("ZB"), view("Z1"), ko(7), A.mult)
-
-    def rival_constants():
+        ts(view("TT", 0, 12), view("THR", 0, 12), 4096.0, A.min)
         ts(view("BQ"), view("BO"), rm(0), A.mult, 512.0, A.mult)
         ms(view("LW", 112, 128), 512.0)
-        ts(ko(18), ko(4), 75.0, A.is_lt, 512.0, A.mult)
-        ts(ko(19), ko(18), -1.0, A.mult, 512.0, A.add)
         ts(view("LM", 112, 128), view("LM", 112, 128), ko(18), A.add)
         ts(view("LM", 128, 144), view("LM", 128, 144), ko(19), A.add)
-        ts(view("TT", 0, 12), view("THR", 0, 12), 4096.0, A.min)
 
-    def merge_constants():
-        ts(ko(13), rm(13), -1536.0, A.mult)
-        ts(ko(14), rm(14), -0.5, A.mult)
-        tt(ko(13), ko(13), rm(12), A.subtract)
-        tt(ko(14), ko(14), ko(7), A.add)
-        ts(view("FL"), view("IO", 0, V, 16), ko(0), A.add)
-        tt(ko(13), ko(13), ko(14), A.add)
-        ts(view("VL", 0, 11), view("IO", 0, L, 16), ko(0), A.add)
-        ts(view("ZS"), view("Z1"), ko(13), A.mult)
-        ms(view("VL", 16, 27), float(DUMP))
-        cp(view("SU", 2 * L, 3 * L), view("SI", 2, V, 4))
-        cp(view("CF"), view("CI"))
-        cp(view("XM"), view("X"))
-        ts(view("RST", 0, NR, 16), view("IO", 0, NR // 16), 0.0, A.mult, 512.0, A.add)
+    thresholds()
+    cp(view("CF"), view("CI"))
+    ts(view("DL", 22, 44), view("DL", 0, 22), 1.0, A.add)
 
-    def exchange_constants():
-        ts(view("BW"), view("BO"), ko(7), A.mult, 8192.0, A.mult)
-        ts(view("Y8"), view("IO", 0, G), 8192.0, A.mult, -511.5 * 8192.0, A.add)
-        tt(view("SO"), view("SO"), view("Y8"), A.add)
-        cp(view("CU", L, 2 * L), view("CI", 1, V, 4))
-        ts(view("Z0"), view("Z1"), rm(0), A.mult)
-        ts(view("ZN"), view("Z0"), -1024.0, A.mult)
-        ts(view("CJ", 0, 42), view("IO", 0, G, 16), ko(0), A.add, 112.0 - 1023.0, A.add)
-        ts(view("CJ", 44, 51), view("IO", 0, CAP, 16), ko(0), A.add, 672.0, A.add)
-        ms(view("ON"), 1.0 / 16)
-        ts(view("RL", 2 * L, 3 * L), view("IO", 0, V, 4), 2.0, A.add)
+    def unpack_p(e, b):
+        o = view("PF", V + G * b, V + G * b + G)
+        ts(o, view("LU%d" % (e % 2), G * b, G * b + G), MAGIC - 128.0, A.add, MAGIC, A.subtract)
+        ts(o, o, 0.0, A.max, 1.0 / 256, A.mult)
+        for h in range(2):
+            mm(bank(4 + 2 * (b != near) + h), view("I256"), half("PF", h, V + G * b), True, True)
 
-    def ghost_constants():
-        for b in range(2):
-            w = GB_ * b
-            for i, (nm, src) in enumerate((("GR", view("RF", V + G * b, V + G * b + G)), ("GP", view("PF", V + G * b, V + G * b + G)), ("GB", view("BT", 0, G)))):
-                dma("y", "d%d" % (9 + 3 * b + i), view(nm, w, w + G), src)
+    def unpack_t(e, b):
+        ts(view("T32", G * b, G * b + G), view("LU%d" % (e % 2), G * b, G * b + G), -256.0, A.add)
 
-    def list_constants(t):
-        out = [lambda: cp(view("CU", L * t + L, L * t + 2 * L), view("CI", t + 1, V, 4))]
-        if t == 1:
-            out.append(lambda: cp(view("SU", 3 * L, 4 * L), view("SI", 3, V, 4)))
-            out.append(lambda: ts(view("RL", 3 * L, 4 * L), view("IO", 0, V, 4), 3.0, A.add))
-        return out
-
-    later = []
-
-    def fill(k):
-        for _ in range(min(k, len(later))):
-            later.pop(0)()
+    def unpack_r(b):
+        for h in range(2):
+            tt(half("RF", h, V + G * b), bank(4 + 2 * (b != near) + h), half("T32", h, G * b), A.subtract)
 
     for t in range(RO):
         last = t == RO - 1
-        cu = lambda lo, hi: view("CU", L * t + lo, L * t + hi)
-        su = lambda r, lo, hi: view("SU", L * r + lo, L * r + hi)
+        par = t % 2
+        o = (t + 2) % 4
         actv = lambda nm: view(nm, t, V, 4)
         bl = view("BL", 0, 11)
-        pvb, rvb = "PVB%d" % (t % 2), "RVB%d" % (t % 2)
-        for lo, hi in ((0, 112), (112, L)):
-            tt(view("A1", 16 * lo, 16 * hi), ind(view("RF", 0, W), cu(lo, hi)), view(pvb, 16 * lo, 16 * hi), A.is_le)
-        for lo, hi in ((0, 112), (112, L)):
-            tt(view("A2", 16 * lo, 16 * hi), ind(view("PF"), cu(lo, hi)), view(rvb, 16 * lo, 16 * hi), A.is_ge)
-        if 0 < t < RO - 1:
-            spread_s("PVB%d" % ((t + 1) % 2), "P", t + 1)
-            spread_s("RVB%d" % ((t + 1) % 2), "R", t + 1)
-        key_add("ZO", "A1", 0, 112)
-        if t:
-            key_add("Z1", "AX", 32 * XC, L)
-        key_add("ZO", "A1", 112, L)
+        pv, rv, xv = "PV%d" % par, "RV%d" % par, "XV%d" % par
+        ps = PS_[t]
+        unpack_p(t, near)
+        unpack_t(t, near)
+        unpack_p(t, far)
+        unpack_r(near)
+        unpack_t(t, far)
+        unpack_r(far)
+        runs = [(k, min(k + 4, ps)) for k in range(0, ps, 4)]
+
+        def p_gather(i):
+            k0, k1 = runs[i]
+            act(ent("GP", k0, k1), ind(view("PF"), ck(t, k0, k1)), AF.Copy)
+            for k in range(k0, k1, 2):
+                diff("GP", rv, k, 2 + 4 * (i % 2) + (k - k0) // 2)
+
+        def p_test(i):
+            k0, k1 = runs[i]
+            for k in range(k0, k1, 2):
+                act(ent("A2", k, k + 2), bank(2 + 4 * (i % 2) + (k - k0) // 2, H), AF.Relu, 1.0)
+
+        for c in range(4):
+            tt(ent("A1", 4 * c, 4 * c + 4), ind(view("RF", 0, W), ck(t, 4 * c, 4 * c + 4)), view(pv), A.is_le)
+        for k in range(ps, 16, 2):
+            tt(ent("A2", k, k + 2), ind(view("PF"), ck(t, k, k + 2)), view(rv, 0, H), A.is_ge)
+        p_gather(0)
+        for i in range(len(runs)):
+            if i + 1 < len(runs):
+                p_gather(i + 1)
+            p_test(i)
+            key_add("ZO", "A1", 4 * i, 4 * i + 4)
+            key_add("ZO", "A2", *runs[i])
+        key_add("ZO", "A1", 4 * len(runs), 16)
+        key_add("ZO", "A2", ps, 16, True)
         if t == 0:
-            x_diff(0, 6)
-            x_size(0, 6)
-            key_add("Z1", "AX", 0, L)
-        key_add("ZO", "A2", 0, 112)
-        key_add("ZO", "A2", 112, L, True)
+            ts(view("SF"), view("SI"), ko(20), A.mult)
+        gcopy(view("SV"), actv("SF"))
+        gcopy(view("CV"), actv("CF"))
         if t == 0:
-            chain_constants()
-            ghost_constants()
+            iota(view("RSE"), [[0, H], [-256, NS_]], 256, 0)
+            iota(view("RS8"), [[0, 128], [-256, 8]], 256, 0)
+            gfill(view("ON"), 1)
         if not last:
-            later.extend(list_constants(t) if t else [])
-            later.extend(spread("XVB", "X", t + 1))
-        fill(8)
-        tr(view("KT"), view("B0", 0, 192))
-        scan(view("KS"), view("RK"), view("KT"), 0.0, A.add, A.min)
-        ts(view("KM", 0, 12), view("KS", 15, 192, 16), 16000.0, A.min)
-        ts(view("DI", 0, 12), view("KM", 0, 12), -0.47, A.add)
-        tt(view("K6", 0, 12), view("KM", 0, 12), view("DI", 0, 12), A.subtract)
-        mm(view("B1", 0, 12), I, view("LC"), True, False)
+            fourfold("XV%d" % (1 - par), "XM", t + 1, gcopy)
+            if t == 0:
+                gfill(view("C3"), CAP)
+                gfill(view("CN", 0, 2), 0)
+            fourfold("PV%d" % (1 - par), "P", t + 1, gcopy)
+            fourfold("RV%d" % (1 - par), "R", t + 1, gcopy)
+        ks = view("KS", 15, 192, 16)
+        tr(view("KT"), bank(0, 192))
+        if t:
+            mm(bank(2, L), view("BW"), actv("BF"), True, True)
+            scaled(view("NS"), bank(2, L), 512.0)
+        if not last:
+            act(view("Y"), ind(view("CF"), view("DL", 22 * t + 22, 22 * t + 44)), AF.Copy)
+        scan(view("KS"), view("RK"), view("KT"), 0.0, A.max, A.min)
+        ts(view("OM"), bank(0, L), WO, A.is_ge, 1000.0, A.mult)
+        ts(view("DI", 0, 12), ks, -0.47, A.add)
+        tt(view("NA", 0, 12), ks, view("TT", 0, 12), A.is_ge)
+        tt(view("K6", 0, 12), ks, view("DI", 0, 12), A.subtract)
+        mm(bank(1, 12), I, view("LC"), True, False)
         for w in range(2):
             for h in range(2):
                 j = 128 * (2 * h + w)
-                mm(view("B1", 6 * w, 6 * w + 6), view("SW", j, j + 128), view("K6", h, 12, 2), False, w == 1 and h == 1)
+                mm(view("B1", w, 12, 2), view("SW", j, j + 128), view("K6", h, 12, 2), False, w == 1 and h == 1)
         cp(view("FT", 10, 192, 16), view("DI", 0, 12))
+        ts(view("NA", 16, 28), ks, 4096.0, A.is_ge, 2.0, A.mult)
         tt(view("FT", 11, 192, 16), view("DI", 0, 12), view("FT", 10, 192, 16), A.subtract)
-        ts(view("OM"), view("B0", 0, L), WO, A.is_ge)
-        tr(view("FR"), view("FT"))
-        for w in range(2):
-            cp(view("LS", w, 12, 2), view("B1", 6 * w, 6 * w + 6))
-        tt(view("FE"), ind(view("BC"), view("LS", 0, 11)), view("FR", 0, L), A.add)
-        mm(view("B6", 0, L), view("AE", 0, 128), view("FE"), True, True)
-        mm(view("B7", 0, L), view("AE", 128, 256), view("FE"), True, True)
-        cp(view("LE", 0, L), view("B6", 0, L))
-        act(view("LE", L, 2 * L), view("B7", 0, L), AF.Copy)
-        listed(view("B0", 0, 11), "ZB", "FE", 0, L)
-        if t == 0:
-            rival_constants()
-        tt(view("NA", 0, 12), view("KM", 0, 12), view("TT", 0, 12), A.is_ge)
-        ts(view("NA", 16, 28), view("KM", 0, 12), 4096.0, A.is_ge, 2.0, A.mult)
-        cp(view("DS"), actv("SI"))
         tt(view("F2", 0, 192, 16), view("NA", 0, 12), view("NA", 16, 28), A.add)
+        tr(view("FR"), view("FT"))
+        cp(view("LS", 0, 11), bank(1, 11))
         tr(view("G2"), view("F2"))
-        fill(4)
+        tt(view("FE"), ind(view("BC"), view("LS", 0, 11)), view("FR", 0, L), A.max)
+        mm(bank(0, L), view("BQ"), view("G2", 0, L), True, False)
+        mm(bank(6, L), view("AE", 0, 128), view("FE"), True, True)
+        mm(bank(7, L), view("AE", 128, 256), view("FE"), True, True)
+        if not last:
+            tr(view("YT"), view("Y"))
+        cp(view("LE", 0, L), bank(6, L))
+        act(view("LE", L, 2 * L), bank(7, L), AF.Copy)
+        listed(bank(1, 11), "ZB", "FE", 0, L)
         done = {}
         for i in (0, 1, 2, 3, 4, 5, 6, 7, 8, 10, 9, 11):
             a, j = TILES[i]
@@ -476,18 +531,20 @@ def rank_program(g, core, T, topo):
                 need("p", done[i - 1])
             done[i] = mm(view("B%d" % (2 + i // 2), L * (i % 2), L * (i % 2) + L, 1, 0, 118), view("LE", c, c + 118, 1, 32 * a, 32 * a + 32),
                          view("FE", 0, L, 1, 32 * a, 32 * a + 32), True, True)
-        ts(bl, view("B0", 0, 11), 511.5, A.add)
-        mm(view("B0", 64, 64 + L), view("BQ"), view("G2", 0, L), True, True)
-        tt(view("MN"), ind(view("R"), bl), view(rvb, 0, NE, 16), A.min)
-        mm(view("B1", 0, L), I, view("MN"), True, False)
-        mm(view("B1", 0, L), view("BQ"), view("G2", 0, L), False, False)
+        if not last:
+            cp(view("CK%d" % (1 - par)), ind(view("YT"), view("KL", 0, 11)))
+        ts(bl, bank(1, 11), 511.5, A.add)
+        if t == 0:
+            ts(ko(13), rm(13), -1536.0, A.mult, rm(12), A.subtract)
+            ts(ko(14), rm(14), -0.5, A.mult, ko(7), A.add)
+        tt(view("MN"), ind(view("R"), bl), view(rv, 0, L), A.min)
         for b in range(6):
-            o = view("YP", 352 * b, 352 * b + 352, 1, 0, 118)
-            i = view("B%d" % (2 + b), 0, 352, 1, 0, 118)
+            y = view("YP", H * b, H * b + H, 1, 0, 118)
+            i = view("B%d" % (2 + b), 0, H, 1, 0, 118)
             if b % 2 == 1:
-                ts(o, i, 10 * WB, A.is_gt)
+                ts(y, i, 10 * WB, A.is_gt)
             else:
-                act(o, i, AF.Relu, -10 * WB)
+                act(y, i, AF.Relu, -10 * WB)
             for i in (2 * b, 2 * b + 1):
                 a, j = TILES[i]
                 if j == 1:
@@ -495,166 +552,168 @@ def rank_program(g, core, T, topo):
                 else:
                     k = 112 - 16 * (2 * a + j // 2)
                     l = view("LW", k, k + 128, 1, 0, 118)
-                mm(view("B1", 0, L), l, view("YP", L * i, L * i + L, 1, 0, 118), False, i == 11)
+                mm(bank(0, L), l, view("YP", L * i, L * i + L, 1, 0, 118), False, i == 11)
+            if b == 0:
+                mm(bank(0, L), I, view("MN"), False, False)
+        if not last:
+            act(view("MX"), ind(view("P"), bl), AF.Copy)
         if t == 0:
-            merge_constants()
-        ts(view("HM"), view("B0", 64, 64 + L), 1000.0, A.is_lt)
-        tt(view("DS"), ind(view("SI"), bl), view("DS"), A.subtract)
-        ts(view("DS"), view("DS"), ko(20), A.mult)
-        tt(view("MX"), ind(view("P"), bl), view(pvb, 0, NE, 16), A.max)
-        fill(10)
+            ts(view("VL", 0, 11), view("IO", 0, L, 16), ko(0), A.add)
+            tt(ko(13), ko(13), ko(14), A.add)
+            ms(view("VL", 16, 27), float(DUMP))
+            ts(ko(21), ko(0), -1.0, A.add, 0.5, A.mult)
+            ts(view("ZS"), view("Z1"), ko(13), A.mult)
+            for r in range(2):
+                cp(view("SE", L * r, L * r + L), view("SE32", r, H, 2))
+            ts(ko(21), ko(21), ko(1), A.add)
+            ts(view("KO", 28, 32), view("M4"), rm(13), A.mult)
+            ts(view("EA", 0, 128), view("IO", 0, 128), ko(21), A.is_equal)
+            ts(view("EA", 128, 256), view("IO", 0, 128), -8.0, A.add, ko(21), A.is_equal)
+            scaled(view("BN"), view("BO"), -1.0)
+            scaled(view("BV"), view("BO"), rm(13))
+            scaled(view("BW"), view("BV"), -1.0)
+            for r in range(4):
+                comp("s", sca.activation, view("BT", r, V, 4), [view("BF", r, V, 4), ko(28 + r)], T.BT[:, r:V:4], T.BF[:, r:V:4], AF.Identity,
+                     bias=ko(28 + r)[0])
+        wn, hm = bank(0, L, 256), bank(7, L)
+        tt(view("DS"), ind(view("SF"), bl), view("SV"), A.subtract)
 
         def candidates():
-            cp(view("DC"), actv("CF"))
-            tt(view("HM"), view("HM"), view("OM"), A.mult)
-            tt(view("DC"), ind(view("CF"), bl), view("DC"), A.subtract)
-            tt(view("DC"), view("DC"), view("HM"), A.mult)
-            tt(actv("CF"), actv("CF"), view("DC"), A.add)
-
-        def halves():
-            tt(view("XS"), ind(view("XM"), bl), actv("X"), A.add)
-            ts(view("XS"), view("XS"), 1, A.arith_shift_right)
-            tt(view("DX"), view("XS"), actv("X"), A.subtract)
-
-        def features():
-            tt(view("DX"), view("DX"), view("WN"), A.mult)
-            tt(actv("X"), actv("X"), view("DX"), A.add)
-        mm(view("B0", 0, 11), I, view("VL", 0, 11), True, False)
-        mm(view("B0", 0, 11), I, view("VL", 16, 27), False, False)
-        ts(view("WN"), view("B1", 0, L), 512.0, A.is_lt)
-        tt(view("FW"), view("FE"), view("WN"), A.mult)
-        tt(actv("R"), view("B1", 0, L), actv("R"), A.min)
-        act(view("RF", 0, V), ind(view("R", 0, V), view("FL")), AF.Copy)
-        for q in range(16):
-            mm(view("B0", 0, 11), zq("ZS", q), view("FW", q, L, 16), False, q == 15)
-        tt(view("DS"), view("DS"), view("WN"), A.mult)
-        tt(actv("SI"), actv("SI"), view("DS"), A.add)
-        cp(view("SC", 0, 11), view("B0", 0, 11))
-        cp(su(t, 0, L), actv("SI"))
-        cp(ind(view("RF"), view("SC", 0, 11)), actv("R"))
-        o = (t + 2) % 4
-        rf = view("RF", 0, W)
-        v3 = VL3 if last else V3
-        for lo, hi in ((0, 88), (88, L)):
-            act(view("GA", 16 * lo, 16 * hi), ind(rf, su(o, lo, hi)), AF.Copy)
-        for lo, hi in ((v3, 112), (112, L)):
-            act(view("GA", NE + 16 * lo, NE + 16 * hi), ind(rf, su(t, lo, hi)), AF.Copy)
-        cp(view("GA", NE, NE + 16 * v3), ind(rf, su(t, 0, v3)))
-
-        def low(r, lo, hi):
-            a, e = (NE if r == t else 0) + 16 * lo, (NE if r == t else 0) + 16 * hi
-            scan(view("GS", a, e), view("RST", 0, e - a), view("GA", a, e), 0.0, A.add, A.min)
-            z = view("R", r + 4 * lo, r + 4 * hi - 3, 4)
-            tt(z, view("GS", a + 15, e, 16), z, A.min)
+            mm(hm, view("BQ"), view("G2", 0, L), True, True)
+            tt(view("DC"), ind(view("CF"), bl), view("CV"), A.subtract)
+            tt(hm, view("OM"), hm, A.is_gt)
+            tt(hm, view("DC"), hm, A.mult)
+            tt(actv("CF"), view("CV"), hm, A.add)
+        features = [lambda: tt(view("XS"), ind(view("XM"), bl), view(xv, 0, L), A.add),
+                    lambda: ts(view("XS"), view("XS"), 1, A.arith_shift_right),
+                    lambda: tt(view("DX"), view("XS"), view(xv, 0, L), A.subtract),
+                    lambda: tt(view("DX"), view("DX"), wn, A.mult),
+                    lambda: tt(actv("XM"), view("DX"), view(xv, 0, L), A.add)]
+        mm(bank(1, 11), I, view("VL", 0, 11), True, False)
+        mm(bank(1, 11), I, view("VL", 16, 27), False, False)
+        ts(wn, bank(0, L), 512.0, A.is_lt)
+        tt(view("QQ"), bank(0, L), view("NS"), A.add)
+        tt(view("FW"), view("FE"), wn, A.mult)
+        listed(bank(1, 11), "ZS", "FW", 0, L, False)
+        tt(actv("RF"), actv("RF"), view("QQ"), A.min)
+        tt(view("DS"), view("DS"), wn, A.mult)
+        mm(bank(6, L), view("EA", 128 * (o // 2), 128 * (o // 2) + 128), view("SF", o, V, 4), True, False)
+        mm(bank(6, L), view("EA", 128 * (t // 2), 128 * (t // 2) + 128), view("SV"), False, False)
+        mm(bank(6, L), view("EA", 128 * (t // 2), 128 * (t // 2) + 128), view("DS"), False, True)
+        features.pop(0)()
+        cp(view("SC", 0, 11), bank(1, 11))
+        cp(ind(view("RF"), view("SC", 0, 11)), view("MN"))
         if not last:
-            cp(ind(view("BF"), view("SC", 0, 11)), view("BT", t, V, 4))
-            listed(view("B0", 0, 44), "ZB", "BF", 0, V)
-            tt(view("MX"), view("MX"), view("WN"), A.mult)
-            tt(actv("P"), actv("P"), view("MX"), A.max)
-            if t == 0:
-                exchange_constants()
-            sig_part("P", True, False)
-            sig_part("BF", False, False)
-        low(t, 0, v3)
+            gfill(view("XM", t + 1, V, 4), int(BIGX))
+            sig([("BO", "R"), ("BV", "BF"), ("BN", "P")], True, False)
+        rf = view("RF", 0, W)
+        se = lambda k: view("SE", L * par + 22 * k, L * par + 22 * k + 22)
+        for k in range(MV, 8):
+            act(view("GE", k - MV, NS_ * H, NS_), ind(rf, se(k)), AF.Copy)
+        ac = lambda k: view("AC", H * (k % 2), H * (k % 2) + H)
+        cp(ac(0), ind(rf, se(0)))
+        extra = [lambda: cp(view("SO"), bank(6, L)), lambda: tt(actv("R"), bank(0, L), actv("R"), A.min)]
+        if not last:
+            extra += [lambda: cp(ind(view("BF"), view("SC", 0, 11)), actv("BT")),
+                      lambda: tt(view("MX"), view("MX"), wn, A.mult),
+                      lambda: tt(actv("P"), actv("P"), view("MX"), A.max)]
+        for k in range(1, MV):
+            if extra:
+                extra.pop(0)()
+            tt(ac(k) if k < MV - 1 else view("GE", NS_ - 1, NS_ * H, NS_), ind(rf, se(k)), ac(k - 1), A.min)
+        for c in range(len(CUTS) - 1):
+            act(view("GA", 16 * CUTS[c], 16 * CUTS[c + 1]), ind(rf, view("SO", CUTS[c], CUTS[c + 1])), AF.Copy)
+        if extra:
+            extra.pop(0)()
+        if t == 0:
+            ts(view("YB", 0, 22), view("IO", 0, 22), 16.0, A.mult, ko(0), A.add)
+            ts(view("YI", 0, 22), view("YB", 0, 22), -10.5, A.add, 1.0 / 22, A.mult)
+            ts(view("YB", 32, 54), view("YB", 0, 22), 16.0 * NS_, A.mult, NS_ - 1.0, A.add)
+            ts(view("YB", 64, 86), view("YI", 0, 22), -351.0 * NS_, A.mult)
+            ts(view("Z0"), view("Z1"), rm(0), A.mult)
+            tt(view("YB", 64, 86), view("YB", 64, 86), view("YB", 32, 54), A.add)
+            ts(view("IBG"), I, BIGT, A.mult)
+            cp(view("PL"), view("YB", 64, 86))
+            ts(view("NBG"), I, -BIGT, A.mult)
+        scan(view("GF"), view("RSE"), view("GE"), 0.0, A.max, A.min)
+        while extra:
+            extra.pop(0)()
+        if not last:
+            listed(bank(1, 44), "ZB", "BF", 0, V)
+            sig([("BW", "BF"), ("BO", "P")], False, False)
+            for h in range(2):
+                mm(bank(4 + h), view("I256"), half("P", h), True, False)
+                mm(bank(4 + h), view("NBG"), view("ON"), False, False)
+        rp = view("R", par, V, 2)
+
+        def low(c):
+            a, e = 16 * CUTS[c], 16 * CUTS[c + 1]
+            scan(view("GS", a, e), view("RS8", 0, e - a), view("GA", a, e), 0.0, A.max, A.min)
+            if last and features:
+                features.pop(0)()
+            z = view("R", par + 4 * CUTS[c], 4 * CUTS[c + 1], 2)
+            tt(z, view("GS", a + 7, e, 8), z, A.min)
+        tt(rp, ind(view("GF"), view("PL")), rp, A.min)
+        if not last:
+            ts(view("FL"), bank(1, 44), 511.5, A.add)
+            act(view("DT", 0, 44), bank(1, 44), AF.Identity, 511.5)
+            act(view("PF", 0, V), ind(view("P"), view("FL")), AF.Copy)
+        for c in range(len(CUTS) - 1):
+            low(c)
         if last:
-            halves()
-            features()
-            dma("y", "d7", (T.yx[:],), view("X"))
-        low(o, 0, 88)
-        if last:
+            dma("y", "d6", (T.yr[:],), view("R"))
+            while features:
+                features.pop(0)()
+            dma("y", "d7", (T.yx[:],), view("XM"))
             candidates()
             dma("y", "d8", (T.yc[:],), view("CF"))
-        else:
-            ts(view("FL"), view("B0", 0, 44), 511.5, A.add)
-        low(o, 88, L)
-        if not last:
-            halves()
-        low(t, v3, 112)
-        low(t, 112, L)
-        if last:
-            dma("y", "d6", (T.yr[:],), view("R", 0, V))
             break
-        sig_part("R", False, True)
+        sig([("BN", "R")], False, True)
         for h in range(2):
-            tt(view("CH", 336 * h, 336 * h + 336), view("B%d" % (2 + h), 0, 336), view("SO", 336 * h, 336 * h + 336), A.not_equal)
-        for h in range(2):
-            act(view("SO", 336 * h, 336 * h + 336), view("B%d" % (2 + h), 0, 336), AF.Copy)
-        act(view("PF", 0, V), ind(view("P", 0, V), view("FL")), AF.Copy)
-        for q in range(16):
-            mm(view("B1", 0, 42), zq("ZN", q), view("CH", q, G, 16), q == 0, False)
-        scan(view("CN"), view("CH"), view("C3"), 0.0, A.add, A.min)
-        for q in range(16):
-            mm(view("B1", 0, 42), zq("Z0", q), view("CN", q, G, 16), False, q == 15)
-        features()
-        cp(actv("XM"), actv("X"))
-        xmask("XM", t + 1)
-        act(view("XF", 0, V), ind(view("XM"), view("FL")), AF.Copy)
-        key_x_gather(t + 1)
-        key_bits(t + 1)
-        cp(view("SL", 0, CAP), view("BT", G, G + CAP))
-        ts(view("DT", 0, 42), view("B1", 0, 42), -911.0, A.is_ge, 4096.0, A.mult)
-        tt(view("DT", 44, 86), view("B1", 0, 42), view("DT", 0, 42), A.add)
-        tt(view("DT", 88, 130), view("DT", 44, 86), view("CJ", 0, 42), A.min)
-        ts(view("DL", 0, 42), view("DT", 88, 130), 1023.0, A.add)
-        cp(ind(view("SL"), view("DL", 0, 42)), view("BT", 0, G))
-        e = t % 2
-        il, sn = "IL%d" % e, "SN%d" % e
-        jl = view(il, 0, 7)
-        listed(view("B1", 0, 7), "ZB", "SL", 0, CAP)
-        ms(view(il, 7, 8), 0); ms(view(il, 15, 16), 0)
-        fill(2)
-        ts(jl, view("B1", 0, 7), 511.5, A.add)
-        cp(view(sn, 2 * CAP, 3 * CAP), ind(view("BF"), jl))
-        ts(view("DT", 132, 139), view("B1", 0, 7), 511.5, A.add)
-        listed(view("B1", 0, 7), "ZB", sn, 2 * CAP, 3 * CAP)
-        cp(view(sn, 0, CAP), ind(view("R"), jl))
-        cp(view(sn, CAP, 2 * CAP), ind(view("P"), jl))
-        fused(view(sn), lambda b: T["LR%d%d" % (e, b)][:], "ar%d" % (2 + 2 * t), "lo%d" % (2 + 2 * t))
-        tt(view("DT", 140, 147), view("CJ", 44, 51), view("DT", 132, 139), A.subtract)
-        ts(view("DT", 148, 155), view("B1", 0, 7), 160.0, A.is_ge)
-        tt(view("DT", 148, 155), view("DT", 148, 155), view("DT", 140, 147), A.mult)
-        tt(view("DT", 148, 155), view("DT", 148, 155), view("DT", 132, 139), A.add)
-        cp(view(il, 8, 15), view("DT", 148, 155))
-        fused(view(il), lambda b: T["LI%d%d" % (e, b)][:], "ar%d" % (3 + 2 * t), "lo%d" % (3 + 2 * t))
-        for b in range(2):
-            arrives("ar%d%d" % (2 + 2 * t, b), arrive_n[b], view("LR%d%d" % (e, b)))
-            arrives("ar%d%d" % (3 + 2 * t, b), arrive_n[b], view("LI%d%d" % (e, b)))
-        red(view("MC", 0, 1), view("WN"))
-        cp(view("MB", 0, 1), view("MC", 0, 1))
-        mm(view("B1", 0, 1), view("ON"), view("MB", 0, 1), True, True)
-        cp(view("RF", 0, V), ind(view("R", 0, V), view("FL")))
-        fill(99)
+            mm(bank(4 + h), view("NI"), half("R", h), False, False)
         if t == 0:
-            spread_s("RVB1", "R", 1)
+            ts(view("FP", 0, 42), view("IO", 0, 42), 16.0, A.mult, ko(0), A.add)
+            ts(view("ZN"), view("Z0"), -1.0, A.mult)
+            ms(view("ZD", 0, 1), 0.0)
+            tt(view("ZD", 1, 144), view("Z0", 1, 144), view("Z0", 0, 143), A.subtract)
+        features.pop(0)()
+        ts(half("CH", 0), bank(2), 0.5, A.is_gt)
+        act(half("CH", 1), bank(3), AF.Sign)
+        act(view("RF", 0, V), ind(view("R"), view("FL")), AF.Copy)
+        key_bits(t + 1, 0)
+        tt(view("DT", 44, 86), view("DT", 0, 42), view("FP", 0, 42), A.subtract)
+        ts(view("DT", 88, 130), view("DT", 0, 42), float(G), A.is_lt)
+        scan(view("CN", 2, G + 2), view("CH"), view("C3"), 0.0, A.add, A.min)
+        for h in range(2):
+            mm(bank(4 + h), view("IBG"), half("CN", h, 2), False, False)
+            mm(bank(4 + h), view("NBG"), half("CN", h, 1), False, True)
+        for q in range(16):
+            mm(bank(1, 42), zq("ZD" if q < 15 else "Z0", q), view("CN", 2 + q, G + 2, 16), q == 0, False)
+        mm(bank(1, 41, 1), zq("ZN", 0), view("CN", 17, G - 14 + 2, 16), False, True)
+        tt(view("DT", 44, 86), view("DT", 44, 86), view("DT", 88, 130), A.mult)
+        features.pop(0)()
+        for h in range(2):
+            tt(half("TP", h), bank(4 + h), half("TP", h), A.max)
+        features.pop(0)()
+        tt(view("DT", 132, 174), bank(1, 42), view("DT", 44, 86), A.mult)
+        features.pop(0)()
+        tt(view("FP", 0, 42), view("FP", 0, 42), view("DT", 132, 174), A.add)
+        act(view("XF", 0, V), ind(view("XM"), view("FL")), AF.Copy)
+        red(view("MC", 0, 1), wn)
+        cp(view("FU", 0, 42), view("FP", 0, 42))
+        ts(view("MB", 0, 1), view("MC", 0, 1), 1.0 / 16, A.mult)
+        ts(view("SN"), ind(view("TP"), view("FU", 0, 42)), 256.0, A.add)
+        send(t + 1)
         key_start()
-        x_diff(0, XC)
-        x_size(0, XC)
-        cp(view("MI", 0, 1), view("B1", 0, 1))
+        mm(bank(1, 1), view("ON", 0, 128), view("MB", 0, 1), True, True)
+        if t == 0:
+            ts(view("DL", 44, 66), view("DL", 0, 22), 2.0, A.add)
+            ts(view("DL", 66, 88), view("DL", 0, 22), 3.0, A.add)
+        cp(view("MI", 0, 1), bank(1, 1))
         candidates()
         ts(view("MI", 1, 2), view("MI", 0, 1), 31, A.bitwise_and)
+        tt(actv("SF"), view("SV"), view("DS"), A.add)
         cp(view("MC", 1, 2), view("MI", 1, 2))
+        window(t + 1, (1, 2, 3))
         ts(view("TT", 0, 12), view("THR", 0, 12), view("MC", 1, 2), A.add, 4096.0, A.min)
-
-        def taken(nm, lo, c):
-            for b in range(2):
-                cp(ind(view(nm, GB_ * b, GB_ * b + GB_), view("LI%d%d" % (e, b), lo, lo + 7)), view("LR%d%d" % (e, b), c, c + CAP))
-
-        def renamed(dst, nm, b):
-            return view(dst, V + G * b, V + G * b + G), ind(view(nm, GB_ * b, GB_ * b + GB_), view("FG", 50 * b, 50 * b + 42))
-        taken("GB", 8, 2 * CAP)
-        for q in range(16):
-            mm(view("B1", 0, 92), zq("ZB", q), view("GB", q, 1472, 16), q == 0, q == 15)
-        x_diff(XC, 6)
-        key_add("Z1", "AX", 0, 32 * XC)
-        taken("GR", 0, 0)
-        taken("GP", 0, CAP)
-        ts(view("FG", 0, 92), view("B1", 0, 92), 511.5, A.add)
-        cp(*renamed("RF", "GR", 0))
-        if t:
-            act(*renamed("RF", "GR", 1), AF.Copy)
-        else:
-            cp(*renamed("RF", "GR", 1))
-        for b in range(2):
-            act(*renamed("PF", "GP", b), AF.Copy)
-        x_size(XC, 6)
     finish()

@@ -8,14 +8,17 @@ H = V // 2
 NE = 16 * L
 DUMP = W
 MV = 4
-NS_ = 8 - MV + 1
-XV_ = (3, 3, 3, 3)
-PS_ = (14, 14, 14, 14)
-CUTS = (0, 64, 128, L)
+CHAINS = 2
+NS_ = 8 - MV + CHAINS
+XV_ = 3
+PS_ = 14
+CUTS = (0, 64, 128, 156, L)
+PARTS = (0, 352, G)
 BIGX = 512.0
 WO = 16384.0
 WB = 1048576.0
 BIGT = 114688.0
+WHOLE = 1.5 * 2.0 ** 23
 MAGIC = 2.0 ** 31
 TILES = [(0, 0), (0, 1), (1, 0), (1, 1), (2, 0), (2, 1), (3, 0), (3, 1), (0, 2), (1, 2), (2, 2), (3, 2)]
 
@@ -26,16 +29,16 @@ SCRATCH = {}
 def _declare():
     bf = [("XM", V), ("R", V), ("P", V), ("RF", W + L), ("PF", W), ("XF", W), ("BF", W + L), ("BT", V), ("LH", 64),
           ("RV0", V), ("RV1", V), ("PV0", V), ("PV1", V), ("XV0", V), ("XV1", V), ("GX", NE), ("AX", NE), ("A1", NE), ("A2", NE), ("GP", NE),
-          ("BC", NE), ("GA", NE), ("GS", NE), ("GE", NS_ * H), ("GF", NS_ * H), ("AC", 2 * H), ("RS8", 1024), ("RSE", NS_ * H), ("E8", 256),
+          ("BC", NE), ("GA", NE), ("GS", NE), ("GE", NS_ * H), ("GF", NS_ * H), ("AC", 4 * H), ("RS8", 1024), ("RSE", NS_ * H), ("E8", 256),
           ("IW", 160), ("MAT", 128 * len(MATS)), ("Z1", 144), ("ZO", 144), ("Z0", 144), ("ZN", 144), ("ZD", 144),
           ("ZB", 144), ("ZS", 144), ("SW", 512), ("AE", 256), ("AT", 640),
-          ("LW", 240), ("LM", 256), ("ON", 336), ("KC", 192), ("LC", 12), ("VL", 32), ("C3", G), ("K6", 16), ("FT", 192), ("FR", 192),
-          ("F2", 192), ("G2", 192), ("FE", L), ("FW", L), ("LE", 2 * L), ("YP", 12 * L), ("MN", L), ("MX", L), ("DX", L),
+          ("LW", 240), ("LM", 256), ("ON", 336), ("KC", 192), ("LC", 12), ("VL", 32), ("C3", 336), ("K6", 16), ("FT", 192), ("FR", 192),
+          ("F2", 192), ("G2", 192), ("FE", L), ("FW", L), ("LE", 2 * L), ("YP", 12 * L), ("MN", L), ("MX", L), ("DX", L), ("XB", L),
           ("OM", L), ("NS", L), ("QQ", L), ("CH", G), ("CN", G + 16), ("MB", 8), ("M4", 4)]
     f4 = [("CF", V), ("SF", V), ("IO", 192), ("IB", 128), ("I8", 256), ("KO", 40), ("RM", 16), ("WT", 96), ("RK", 192), ("KT", 192), ("KS", 192),
-          ("NA", 32), ("THR", 16), ("TT", 16), ("DS", L), ("DC", L), ("SV", L), ("CV", L), ("DT", 176), ("MC", 4), ("TP", G), ("T32", 2 * G),
-          ("Y", H), ("YT", H), ("EA", 256), ("FP", 44), ("YB", 256)]
-    i4 = [("CI", V), ("SI", V), ("SE32", H), ("T8", 2), ("PI", 8), ("YI", 96), ("DI", 16), ("XS", L), ("MI", 8)]
+          ("NA", 32), ("THR", 16), ("TT", 16), ("DS", L), ("DC", L), ("XH", L), ("SV", L), ("CV", L), ("DT", 176), ("MC", 4), ("TP", G),
+          ("T32", 2 * G), ("Y", H), ("YT", H), ("EA", 256), ("FP", 44), ("YB", 320)]
+    i4 = [("CI", V), ("SI", V), ("SE32", H), ("T8", 2), ("PI", 8), ("YI", 96), ("DI", 16), ("MI", 8)]
     u2 = [("CK0", L), ("CK1", L), ("SE", H), ("SO", L), ("DL", 88), ("KL", 12), ("PL", 22), ("LS", 16), ("BL", 16), ("SC", 16), ("FL", 44),
           ("FU", 44), ("SN", G), ("LU0", 2 * G), ("LU1", 2 * G)]
     for lst, d in ((bf, "bfloat16"), (f4, "float32"), (i4, "int32"), (u2, "uint16")):
@@ -46,7 +49,16 @@ def _declare():
 
 
 _declare()
-SEMAPHORES = ["s_v", "s_s", "s_p", "s_g"] + ["d%d" % i for i in range(20)] + ["ar%d%d" % (i, b) for i in range(4) for b in range(2)] + ["lo%d" % i for i in range(4)]
+SEMAPHORES = (["s_v", "s_s", "s_p", "s_g"] + ["d%d" % i for i in range(20)] + ["lo%d%d" % (i, c) for i in range(RO) for c in range(len(PARTS) - 1)]
+              + ["ar%d%d%d" % (i, c, b) for i in range(RO) for c in range(len(PARTS) - 1) for b in range(2)])
+
+
+def meet(a, b):
+    return a[0] < b[1] and b[0] < a[1] and (a[0] - b[0]) % math.gcd(a[2], b[2]) == 0
+
+
+def covers(a, b):
+    return a[0] <= b[0] and b[1] <= a[1] and (a[2] == 1 or (a[2] == b[2] and (a[0] - b[0]) % a[2] == 0))
 
 
 def tracker(g, T):
@@ -55,22 +67,6 @@ def tracker(g, T):
     cnt = {e: 0 for e in eng}
     recs = {}
     total = {}
-
-    def view(name, lo=0, hi=None, st=1, p0=0, p1=128):
-        if name in MATS:
-            name, lo, hi = "MAT", 128 * MATS.index(name), 128 * MATS.index(name) + 128
-        hi = SCRATCH[name][1][1] if hi is None else hi
-        t = T[name]
-        return (t[p0:p1, lo:hi] if st == 1 else t[p0:p1, lo:hi:st], [(name, lo, hi, st)])
-
-    def ind(win, off):
-        return (win[0].indirect(off[0]), win[1] + off[1])
-
-    def meet(a, b):
-        return a[0] < b[1] and b[0] < a[1] and (a[0] - b[0]) % math.gcd(a[2], b[2]) == 0
-
-    def covers(a, b):
-        return a[0] <= b[0] and b[1] <= a[1] and (a[2] == 1 or (a[2] == b[2] and (a[0] - b[0]) % a[2] == 0))
 
     def need(e, rec):
         sem, val, clock, _ = rec
@@ -109,45 +105,150 @@ def tracker(g, T):
                         old = [r for r in old if not (not r[1] and covers(fp, r[0]) and r[2][3] == rec[3] and rec[3] is not None)]
                     recs[name] = old + [(fp, wr, rec)]
 
-    def comp(e, fn, out, ins, *args, **kw):
-        depend(e, [out], ins)
-        cnt[e] += 1
-        sem = "s_" + e
-        rec = (sem, cnt[e], dict(known[e]), e)
-        rec[2][sem] = cnt[e]
-        fn(*args, **kw).then_inc(T.sem[sem], 1)
-        total[sem] = cnt[e]
-        note(rec, [out], ins)
+    def issue(e, sem, val, outs, ins, call):
+        if call is None:
+            rec = (sem, val, {sem: val}, None)
+        else:
+            depend(e, outs, ins)
+            if sem is None:
+                cnt[e] += 1
+                call().then_inc(T.sem["s_" + e], 1)
+                rec = ("s_" + e, cnt[e], dict(known[e]), e)
+            else:
+                call()
+                rec = (sem, val, dict(known[e]), None)
+            rec[2][rec[0]] = rec[1]
+        total[rec[0]] = rec[1]
+        note(rec, outs, ins)
         return rec
-
-    def dma(e, sem, out, in_):
-        o = [out] if len(out) > 1 else []
-        i = [in_] if len(in_) > 1 else []
-        depend(e, o, i)
-        eng[e].dma_start(out[0], in_[0]).then_inc(T.sem[sem], 16)
-        rec = (sem, 16, dict(known[e]), None)
-        rec[2][sem] = 16
-        total[sem] = 16
-        note(rec, o, i)
-
-    def sent(call, sem, val, srcs):
-        depend("g", [], srcs)
-        call()
-        rec = (sem, val, dict(known["g"]), None)
-        rec[2][sem] = val
-        total[sem] = val
-        note(rec, [], srcs)
-        return rec
-
-    def arrives(sem, val, out):
-        total[sem] = val
-        note((sem, val, {sem: val}, None), [out], [])
 
     def finish():
         for k in sorted(total):
             if known["y"].get(k, 0) < total[k]:
                 g.sync.wait_ge(T.sem[k], total[k])
-    return view, ind, comp, dma, sent, arrives, finish, need
+    return issue, need, finish
+
+
+CYCLE, PE_CYCLE, HOP, GATHER, SCATTER = 0.0009, 0.00045, 0.18, 1.56, 3.8
+LOAD, LOAD_GAP, CALL, FIRST, NEAR, FAR = 2.2, 0.8, 0.6, 3.5, 3.0, 4.0
+PASSES, SLACK = 3, 0.2
+
+
+def count(v): return 16 * len(range(*v[1][1][1:])) if len(v[1]) > 1 else len(range(*v[1][0][1:]))
+
+
+def price(e, out, ins, both):
+    kinds = [SCRATCH[v[1][0][0]] for v in [out] + ins if count(v) > 1]
+    n = max(count(v) for v in [out] + ins)
+    if e == "p":
+        return PE_CYCLE * max(64, count(ins[1])) * (4 if SCRATCH[ins[1][1][0][0]][2] == "float32" else 1)
+    if e == "g":
+        return 0.17 + 2 * CYCLE * n
+    if len(out[1]) > 1:
+        return 0.05 + SCATTER * CYCLE * n
+    if any(len(v[1]) > 1 for v in ins):
+        return 0.06 + GATHER * CYCLE * n
+    if e == "s":
+        return 0.05 + CYCLE * max(64, n)
+    if both:
+        return CYCLE * max(64, n * (1 if any(k[0] == "psum" for k in kinds) else 2))
+    return CYCLE * max(64, n * (0.5 if all(k[2] in ("bfloat16", "uint16") for k in kinds) else 1))
+
+
+def planner():
+    nodes, recs, runs = [], {}, {}
+
+    def add(e, cost, tail, outs, ins, call, after=None, middle=False):
+        me, before = len(nodes), dict(after or {})
+        for (lst, wr) in ((ins, False), (outs, True)):
+            for v in lst:
+                for (name, lo, hi, st) in v[1]:
+                    fp, old = (lo, hi, st), recs.get(name, [])
+                    if SCRATCH[name][0] == "psum":
+                        run = runs.setdefault(name, [e, []])
+                        if run[0] != e:
+                            run[0], run[1], old = e, [r[2] for r in old], []
+                        before.update({a: HOP for a in run[1]})
+                        if e == "p":
+                            before.update({r[2]: before.get(r[2], 0.0) for r in old if not (middle and r[1])})
+                            recs[name] = (old if middle else []) + [(fp, middle, me)]
+                            continue
+                    before.update({r[2]: HOP for r in old if (wr or r[1]) and r[2] != me and meet(r[0], fp)})
+                    keep = SCRATCH[name][0] == "psum" or not wr
+                    recs[name] = [r for r in old if keep or not covers(fp, r[0])] + [(fp, wr, me)]
+        nodes.append((e, cost, tail, before, call))
+        return me
+
+    def place(rank, before):
+        later = [[] for _ in nodes]
+        for i, b in enumerate(before):
+            for a in b:
+                later[a].append(i)
+        left = [len(b) for b in before]
+        start, can, free, ready = [0.0] * len(nodes), [0.0] * len(nodes), {}, {}
+        for i, x in enumerate(left):
+            free[nodes[i][0]] = 0.0
+            ready.setdefault(nodes[i][0], set())
+            if x == 0:
+                ready[nodes[i][0]].add(i)
+
+        def ahead(now, end, skip):
+            when = {z: max(can[z], free[q], now) for q in ready for z in ready[q] if can[z] < end and z != skip}
+            seen, stack = {}, list(when)
+            while stack:
+                z = stack.pop()
+                for j in later[z]:
+                    k, x = seen.get(j, (0, can[j]))
+                    seen[j] = (k + 1, max(x, when[z] + nodes[z][1] + before[j][z]))
+                    if seen[j][0] == left[j] and seen[j][1] < end:
+                        when[j] = seen[j][1]
+                        stack.append(j)
+            return when
+        todo = len(nodes)
+        while todo:
+            e = min((q for q in ready if ready[q]), key=lambda q: max(free[q], min(can[z] for z in ready[q])))
+            now = max(free[e], min(can[z] for z in ready[e]))
+            i = max((z for z in ready[e] if can[z] <= now), key=lambda z: (rank[z], -z))
+            when = ahead(now, now + nodes[i][1], i)
+            soon = [z for z in when if nodes[z][0] == e and when[z] > now and rank[z] > rank[i]]
+            if soon:
+                j = max(soon, key=lambda z: (rank[z], -z))
+                if max(when[j] + rank[j], when[j] + nodes[j][1] + rank[i]) + SLACK < max(now + rank[i], now + nodes[i][1] + rank[j]):
+                    fill = [z for z in ready[e] if can[z] <= now and nodes[z][1] <= when[j] - now + SLACK]
+                    if not fill:
+                        free[e] = min([when[j]] + [can[z] for z in ready[e] if can[z] > now])
+                        continue
+                    i = max(fill, key=lambda z: (rank[z], -z))
+            todo -= 1
+            ready[e].remove(i)
+            start[i] = max(now, can[i])
+            free[e] = start[i] + nodes[i][1]
+            for j in later[i]:
+                left[j] -= 1
+                can[j] = max(can[j], free[e] + before[j][i])
+                if left[j] == 0:
+                    ready[nodes[j][0]].add(j)
+        return start
+
+    def order():
+        fwd = [{a: w + nodes[a][2] for a, w in nd[3].items()} for nd in nodes]
+        bwd = [{} for _ in nodes]
+        for i, b in enumerate(fwd):
+            for a, w in b.items():
+                bwd[a][i] = w
+        rank = [0.0] * len(nodes)
+        for i in range(len(nodes) - 1, -1, -1):
+            rank[i] = nodes[i][1] + max([w + rank[j] for j, w in bwd[i].items()] + [nodes[i][2]])
+        best = None
+        for _ in range(PASSES):
+            start = place(rank, fwd)
+            end = [s + nd[1] + nd[2] for s, nd in zip(start, nodes)]
+            if best is None or max(end) < best[0]:
+                best = (max(end), start)
+            back = place(end, bwd)
+            rank = [s + nd[1] for s, nd in zip(back, nodes)]
+        return [nodes[i][4] for i in sorted(range(len(nodes)), key=lambda z: (best[1][z], z))]
+    return add, order
 
 
 def rank_program(g, core, T, topo):
@@ -168,11 +269,39 @@ def rank_program(g, core, T, topo):
     local_n = sum(len(x) for x in eng.values())
     near, far = sorted((0, 1), key=lambda b: source[b] not in topo.cores_of(core))
 
-    view, ind, comp, dma, sent, arrives, finish, need = tracker(g, T)
+    issue, need, finish = tracker(g, T)
+    add, order = planner()
+    made = {}
     vec, sca, ten = g.vector, g.scalar, g.tensor
 
+    def view(name, lo=0, hi=None, st=1, p0=0, p1=128):
+        if name in MATS:
+            name, lo, hi = "MAT", 128 * MATS.index(name), 128 * MATS.index(name) + 128
+        hi = SCRATCH[name][1][1] if hi is None else hi
+        t = T[name]
+        return (t[p0:p1, lo:hi] if st == 1 else t[p0:p1, lo:hi:st], [(name, lo, hi, st)])
+
+    def ind(win, off):
+        return (win[0].indirect(off[0]), win[1] + off[1])
+
+    def plan(e, cost, tail, sem, val, outs, ins, fn, waits=(), after=None, middle=False):
+        def call():
+            for a in waits:
+                need(e, made[a])
+            made[me] = issue(e, sem, val, outs, ins, fn)
+        me = add(e, cost, tail, outs, ins, call, (after or {}) | {a: HOP for a in waits}, middle)
+        return me
+
+    def comp(e, fn, out, ins, *args, waits=(), both=False, middle=False, **kw):
+        return plan(e, price(e, out, ins, both), 0.0, None, 1, [out], ins, lambda: fn(*args, **kw), waits, None, middle)
+
+    def dma(e, sem, out, in_, waits=(), after=None):
+        q = g.sync if e == "y" else sca
+        return plan(e, 0.05, LOAD, sem, 16, [v for v in (out,) if len(v) > 1], [v for v in (in_,) if len(v) > 1],
+                    lambda: q.dma_start(out[0], in_[0]).then_inc(T.sem[sem], 16), waits, after)
+
     def cp(o, i): comp("v", vec.tensor_copy, o, [i], o[0], i[0])
-    def tt(o, a, b, op): comp("v", vec.tensor_tensor, o, [a, b], o[0], a[0], b[0], op)
+    def tt(o, a, b, op): comp("v", vec.tensor_tensor, o, [a, b], o[0], a[0], b[0], op, both=True)
     def ts(o, a, s1, op0, s2=None, op1=None):
         ins = [a] + [s for s in (s1, s2) if isinstance(s, tuple)]
         u1 = s1[0] if isinstance(s1, tuple) else s1
@@ -182,362 +311,316 @@ def rank_program(g, core, T, topo):
         else:
             comp("v", vec.tensor_scalar, o, ins, o[0], a[0], u1, u2, op0, op1)
     def ms(o, c): comp("v", vec.memset, o, [], o[0], c)
-    def scan(o, a, b, init, op0, op1): comp("v", vec.tensor_tensor_scan, o, [a, b], o[0], a[0], b[0], init, op0, op1)
+    def scan(o, a, b, init, op0, op1):
+        col = isinstance(init, tuple)
+        comp("v", vec.tensor_tensor_scan, o, [a, b, init] if col else [a, b], o[0], a[0], b[0], init[0] if col else init, op0, op1)
     def tr(o, i): comp("v", vec.transpose, o, [i], o[0], i[0])
     def red(o, i): comp("v", vec.tensor_reduce, o, [i], o[0], i[0], AxisListType.X, A.add)
-    def act(o, i, f, bias=0.0): comp("s", sca.activation, o, [i], o[0], i[0], f, bias=bias)
-    def scaled(o, i, c):
-        col = isinstance(c, tuple)
-        comp("s", sca.activation, o, [i, c] if col else [i], o[0], i[0], AF.Copy, scale=c[0] if col else c)
-    def mm(o, l, r, start, stop): return comp("p", ten.matmul, o, [l, r], o[0], l[0], r[0], start, stop)
+    def act(o, i, f, bias=0.0, scale=1.0):
+        cols = [c for c in (bias, scale) if isinstance(c, tuple)]
+        comp("s", sca.activation, o, [i] + cols, o[0], i[0], f, bias=bias[0] if isinstance(bias, tuple) else bias,
+             scale=scale[0] if isinstance(scale, tuple) else scale)
+    def scaled(o, i, c): act(o, i, AF.Copy, 0.0, c)
+    def mm(o, l, r, start, stop, waits=()):
+        return comp("p", ten.matmul, o, [l, r], o[0], l[0], r[0], start, stop, waits=waits, middle=not (start or stop))
     def iota(o, pat, base, cm): comp("g", g.iota, o, [], o[0], pat, base, cm, allow_small_or_imprecise_dtypes=True)
-    def gfill(o, c): iota(o, [[0, len(range(*o[1][0][1:]))]], c, 0)
-    def gcopy(o, i): comp("g", g.affine_select, o, [i], o[0], i[0], [[0, len(range(*o[1][0][1:]))]], A.is_ge, 0.0, 0, 0)
+    def gfill(o, c): iota(o, [[0, count(o)]], c, 0)
+    def gcopy(o, i): comp("g", g.affine_select, o, [i], o[0], i[0], [[0, count(o)]], A.is_ge, 0.0, 0, 0)
 
     I = view("IW", 16, 144)
 
     def zq(z, q): return view(z, 15 - q, 143 - q)
 
-    def listed(o, z, name, lo, hi, start=True, stop=True):
+    def listed(o, z, name, lo, hi, start=True):
         for q in range(16):
-            mm(o, zq(z, q), view(name, lo + q, hi, 16), start and q == 0, stop and q == 15)
+            mm(o, zq(z, q), view(name, lo + q, hi, 16), start and q == 0, q == 15)
 
-    def send(e):
-        out = []
-        src = view("SN")
+    def send(e, c):
+        lo, hi = PARTS[c], PARTS[c + 1]
+        src, land, out = view("SN", lo, hi), "LU%d" % (e % 2), []
         for d, blk in nb:
             rid, pid = topo.addr(d, core)
             out.append(RemoteDMATransfer(dst_ids=[DstId(rid=rid, pnc=pid)], dma_engine_mask=sum(1 << x for x in eng[d]),
-                                         remote_sem=T.sem["ar%d%d" % (e, blk)], src=src[0], dst=T["LU%d" % (e % 2)][:, G * blk: G * blk + G]))
-        rec = sent(lambda: g.remote_dma_fused(out, local_sem=T.sem["lo%d" % e]), "lo%d" % e, local_n, [src])
+                                         remote_sem=T.sem["ar%d%d%d" % (e, c, blk)], src=src[0], dst=T[land][:, G * blk + lo: G * blk + hi]))
+        sem = "lo%d%d" % (e, c)
+        me = plan("g", CALL + (FIRST if e + c == 0 else 0.0), NEAR, sem, local_n, [], [src], lambda: g.remote_dma_fused(out, local_sem=T.sem[sem]))
         for b in range(2):
-            arrives("ar%d%d" % (e, b), arrive_n[b], view("LU%d" % (e % 2), G * b, G * b + G))
-        return rec
+            plan("n", 0.01, 0.0, "ar%d%d%d" % (e, c, b), arrive_n[b], [view(land, G * b + lo, G * b + hi)], [], None, (),
+                 {me: 0.0 if b == near else FAR - NEAR})
+        return me
 
     def ko(i): return view("KO", i, i + 1)
     def pi(i): return view("PI", i, i + 1)
     def rm(i): return view("RM", i, i + 1)
     def half(nm, h, lo=0): return view(nm, lo + 336 * h, lo + 336 * h + 336)
     def bank(b, w=336, lo=0): return view("B%d" % b, lo, lo + w)
+    def ck(t, k0, k1): return view("CK%d" % (t % 2), 11 * k0, 11 * k1)
+    def ent(nm, k0, k1): return view(nm, L * k0, L * k1)
 
     def fourfold(dst, src, t, copy):
         copy(view(dst, 0, L), view(src, t, V, 4))
         copy(view(dst, L, 2 * L), view(dst, 0, L))
         copy(view(dst, 2 * L, 4 * L), view(dst, 0, 2 * L))
 
-    def ck(t, k0, k1): return view("CK%d" % (t % 2), 11 * k0, 11 * k1)
-    def ent(nm, k0, k1): return view(nm, L * k0, L * k1)
-
-    def key_start():
-        mm(bank(0, 192), I, view("KC"), True, False)
-
-    def key_add(z, src, k0, k1, stop=False):
+    def key_add(z, src, k0, k1):
         for k in range(k0, k1):
-            mm(bank(0, L), zq(z, k), ent(src, k, k + 1), False, stop and k == k1 - 1)
+            mm(bank(0, L), zq(z, k), ent(src, k, k + 1), False, False)
 
     def diff(src, own, k, b):
         mm(bank(b, H), I, ent(src, k, k + 2), True, False)
         mm(bank(b, H), view("NI"), view(own, 0, H), False, True)
 
-    def x_vector(t, c):
-        tt(ent("GX", 4 * c, 4 * c + 4), ind(view("XF"), ck(t, 4 * c, 4 * c + 4)), view("XV%d" % (t % 2)), A.subtract)
+    def turned(t, src):
+        (cp if src == "CI" else lambda o, i: act(o, i, AF.Copy))(view("Y"), ind(view(src), view("DL", 22 * t, 22 * t + 22)))
+        tr(view("YT"), view("Y"))
+        cp(ck(t, 0, 16), ind(view("YT"), view("KL", 0, 11)))
 
-    def x_size(c):
-        act(ent("AX", 4 * c, 4 * c + 4), ent("GX", 4 * c, 4 * c + 4), AF.Abs)
-        key_add("Z1", "AX", 4 * c, 4 * c + 4)
-
-    def x_scalar(t, c):
-        act(ent("GX", 4 * c, 4 * c + 4), ind(view("XF"), ck(t, 4 * c, 4 * c + 4)), AF.Copy)
-        for i in range(2):
-            diff("GX", "XV%d" % (t % 2), 4 * c + 2 * i, 2 + i)
-
-    def x_scalar_size(c):
-        for i in range(2):
-            act(ent("AX", 4 * c + 2 * i, 4 * c + 2 * i + 2), bank(2 + i, H), AF.Abs)
-        key_add("Z1", "AX", 4 * c, 4 * c + 4)
-
-    def key_bits(t, c):
-        act(ent("BC", 4 * c, 4 * c + 4), ind(view("BF", 0, W), ck(t, 4 * c, 4 * c + 4)), AF.Copy)
-
-    def window(t, bits):
-        nv = XV_[t]
-        bits = list(bits)
-        for c in range(nv):
-            x_vector(t, c)
-        for c in range(nv, 4):
-            x_scalar(t, c)
-            key_bits(t, bits.pop(0))
-            x_scalar_size(c)
-        for c in range(nv):
-            x_size(c)
-            if bits:
-                key_bits(t, bits.pop(0))
+    def distances(t):
+        xv = "XV%d" % (t % 2)
+        mm(bank(0, L), I, view("KC", 0, L), True, False)
+        for c in range(0, 16, 4):
+            if c < 4 * XV_:
+                tt(ent("GX", c, c + 4), ind(view("XF"), ck(t, c, c + 4)), view(xv), A.subtract)
+                act(ent("AX", c, c + 4), ent("GX", c, c + 4), AF.Abs)
+            else:
+                act(ent("GX", c, c + 4), ind(view("XF"), ck(t, c, c + 4)), AF.Copy)
+                for i in range(2):
+                    diff("GX", xv, c + 2 * i, 2 + i)
+                    act(ent("AX", c + 2 * i, c + 2 * i + 2), bank(2 + i, H), AF.Abs)
+            key_add("Z1", "AX", c, c + 4)
+            act(ent("BC", c, c + 4), ind(view("BF", 0, W), ck(t, c, c + 4)), AF.Copy)
 
     def sig(parts, first, last):
         for i, (z, nm) in enumerate(parts):
             for h in range(2):
                 mm(bank(2 + h), view(z), half(nm, h), first and i == 0, last and i == len(parts) - 1)
 
-    dma("y", "d0", view("R"), (T.reach[:],))
-    dma("s", "d1", view("P"), (T.past[:],))
-    comp("g", g.iota, view("PI", 0, 1), [], T.PI[:, 0:1], [[0, 1]], 0, 1)
+    gap = lambda a: {a: LOAD_GAP - LOAD}
+    d = dma("y", "d0", view("R"), (T.reach[:],))
+    dma("s", "d3", view("XM"), (T.x[:],), (), gap(dma("s", "d1", view("P"), (T.past[:],))))
+    for sem, dst, src in (("d2", view("CI"), T.cand), ("d5", view("T8", 0, 1, 1, 0, 8), T.th), ("d17", view("PF", 0, V), T.past),
+                          ("d18", view("RF", 0, V), T.reach), ("d4", view("SI"), T.succ)):
+        d = dma("y", sem, dst, (src[:],), (), gap(d))
+    comp("g", g.iota, pi(0), [], T.PI[:, 0:1], [[0, 1]], 0, 1)
     iota(view("IO"), [[1, 192]], 0, 0)
-    dma("y", "d2", view("CI"), (T.cand[:],))
-    dma("s", "d3", view("XM"), (T.x[:],))
-    dma("y", "d5", view("T8", 0, 1, 1, 0, 8), (T.th[:],))
-    dma("y", "d17", view("PF", 0, V), (T.past[:],))
-    dma("y", "d18", view("RF", 0, V), (T.reach[:],))
     iota(view("IB"), [[16, 8], [0, 16]], 0, 0)
     for h in range(2):
         iota(view("I8", 128 * h, 128 * h + 128, 1, 0, 8), [[2, 4], [0, 32]], h, -1)
     iota(view("RK"), [[0, 12], [-16000, 16]], 16000, 0)
-    gfill(view("FT"), -2)
-    gfill(view("F2"), 0)
+    iota(view("RSE"), [[0, H], [-256, NS_]], 256, 0)
+    iota(view("RS8"), [[0, 128], [-256, 8]], 256, 0)
+    iota(view("M4"), [[-1, 4]], -1, 0)
+    for v, c in ((view("FT"), -2), (view("F2"), 0), (view("RF", W, W + L), 0), (view("NS"), 0), (view("ON"), 1), (view("C3"), CAP), (view("CN", 0, 2), 0)):
+        gfill(v, c)
+    for v, c in ((view("XF", V, W), BIGX), (view("BF", V, W + L), 0.0), (view("LW"), 0.0), (view("LM"), 0.0), (view("WT", 16, 32), 0.5),
+                 (view("WT", 48, 64), 2.0), (view("LW", 112, 128), 512.0), (view("VL", 16, 27), float(DUMP)), (view("ZD", 0, 1), 0.0)):
+        ms(v, c)
     for i, m in ((1, 15), (2, 112), (3, 16), (4, 31), (5, 1)):
         ts(pi(i), pi(0), m, A.bitwise_and)
     ts(ko(4), pi(0), 16.0, A.add)
     cp(view("KO", 0, 2), view("PI", 1, 3))
-    ts(view("IW"), view("IO", 0, 160), ko(4), A.is_equal)
-    ts(view("RM"), view("IO", 0, 16), ko(0), A.is_equal)
-    ms(view("WT", 16, 32), 0.5)
     ts(ko(5), pi(2), 15.0, A.add)
     ts(ko(2), pi(3), 1.0 / 16, A.mult)
-    scaled(view("I256"), I, 256.0)
-    scaled(view("NI"), I, -1.0)
+    ts(ko(3), pi(3), -1.0 / 16, A.mult, 1.0, A.add)
+    cp(ko(9), pi(4))
+    cp(ko(20), pi(5))
+    ts(ko(6), pi(1), 10.0, A.is_lt)
+    ts(view("IW"), view("IO", 0, 160), ko(4), A.is_equal)
+    ts(view("RM"), view("IO", 0, 16), ko(0), A.is_equal)
+    ts(view("Z1"), view("IO", 0, 144), ko(5), A.is_equal)
+    ts(view("BO"), view("IB"), ko(1), A.is_equal)
+    for nm, c in (("I256", 256.0), ("NI", -1.0), ("IBG", BIGT), ("NBG", -BIGT)):
+        scaled(view(nm), I, c)
+    for h in range(2):
+        mm(bank(4 + h), view("I256"), half("P", h), True, False)
+        mm(bank(4 + h), view("NI"), half("R", h), False, True)
+        ts(half("SN", h), bank(4 + h), 256.0, A.add)
+        act(half("TP", h), bank(4 + h), AF.Copy)
+    for c in range(len(PARTS) - 1):
+        sent = send(0, c)
+    for k in range(8):
+        dma("y", "d%d" % (9 + k), view("SE32", 44 * k, 44 * k + 44), (T.succ[2 * k::16, :],), [sent])
     scan(view("WT", 0, 16), view("WT", 16, 32), view("WT", 16, 32), 1.0, A.mult, A.min)
     ts(view("YB", 0, 32), view("IO", 0, 32), 0.5, A.add)
     ts(view("YB", 32, 54), view("IO", 0, 22), 32.0, A.mult, 0.5, A.add)
     tt(view("WT", 32, 48), view("WT", 0, 16), view("RM"), A.mult)
-    ts(ko(6), ko(0), 10.0, A.is_lt)
-    tt(ko(17), rm(10), rm(11), A.add)
     red(ko(10), view("WT", 32, 48))
+    tt(ko(26), rm(10), rm(11), A.add)
     ts(ko(11), ko(6), 2.0, A.mult)
-    tt(ko(12), ko(17), rm(12), A.add)
+    ts(ko(12), ko(26), rm(12), A.add, -512.0, A.mult)
+    tt(ko(12), ko(12), ko(6), A.subtract)
     ts(view("YB", 64, 118), view("YB", 0, 54), ko(10), A.mult)
     ts(view("YI", 0, 54), view("YB", 0, 54), ko(10), A.mult)
-    ts(ko(12), ko(12), -512.0, A.mult, ko(6), A.subtract)
-    ts(view("Z1"), view("IO", 0, 144), ko(5), A.is_equal)
     tt(view("YB", 0, 54), view("YI", 0, 54), view("YB", 64, 118), A.is_gt)
-    ts(ko(3), ko(2), -1.0, A.mult, 1.0, A.add)
-    ts(view("KO", 22, 24), view("KO", 2, 4), 16.0 * L, A.mult)
     ts(view("LH", 0, 32), view("YB", 0, 32), ko(11), A.mult)
     ts(view("LH", 32, 54), view("YB", 32, 54), ko(11), A.mult, ko(12), A.add)
     for h in range(2):
-        mm(bank(4 + h), view("I256"), half("P", h), True, False)
-        mm(bank(4 + h), view("NI"), half("R", h), False, True)
-    for b in range(22):
-        mm(bank(6 + b // 11, 32, 32 * (b % 11)), I, view("LH", 0, 32), b % 11 == 0, False)
-    for h in range(2):
+        for b in range(11):
+            mm(bank(6 + h, 32, 32 * b), I, view("LH", 0, 32), b == 0, False)
         for s in range(32):
             mm(view("B%d" % (6 + h), s, H, 32), I, view("LH", 32 + 11 * h, 43 + 11 * h), False, s == 31)
-    scaled(view("ZO"), view("Z1"), WO)
+        act(view("BF", H * h, H * h + H), bank(6 + h, H), AF.Copy)
+    ts(view("KO", 28, 32), view("M4"), rm(13), A.mult)
+    for r in range(4):
+        act(view("BT", r, V, 4), view("BF", r, V, 4), AF.Identity, ko(28 + r))
+    scan(view("WT", 64, 80), view("WT", 48, 64), view("F2", 0, 16), 0.25, A.mult, A.add)
+    tt(view("WT", 80, 96), view("WT", 64, 80), view("RM"), A.mult)
+    red(ko(27), view("WT", 80, 96))
+    tt(ko(7), ko(27), ko(6), A.mult)
+    ts(view("KO", 22, 24), view("KO", 2, 4), 16.0 * L, A.mult)
     for h in range(2):
         for w in range(2):
             z = 16 - 16 * (h - w)
             scaled(view("SW", 128 * (2 * h + w), 128 * (2 * h + w) + 128), view("IW", z, z + 128), ko(22 if w else 23))
+    ts(ko(13), rm(13), -1536.0, A.mult, rm(12), A.subtract)
+    ts(ko(14), rm(14), -0.5, A.mult, ko(7), A.add)
+    tt(ko(13), ko(13), ko(14), A.add)
+    for nm, c in (("ZO", WO), ("ZB", ko(7)), ("ZS", ko(13)), ("Z0", rm(0))):
+        scaled(view(nm), view("Z1"), c)
+    scaled(view("ZN"), view("Z0"), -1.0)
+    tt(view("ZD", 1, 144), view("Z0", 1, 144), view("Z0", 0, 143), A.subtract)
+    ts(view("BQ"), view("BO"), rm(0), A.mult, 512.0, A.mult)
+    scaled(view("BN"), view("BO"), -1.0)
+    scaled(view("BV"), view("BO"), rm(13))
+    scaled(view("BW"), view("BV"), -1.0)
+    ts(ko(21), ko(0), -1.0, A.add, 0.5, A.mult)
+    ts(ko(21), ko(21), ko(1), A.add)
+    ts(view("EA", 0, 128), view("IO", 0, 128), ko(21), A.is_equal)
+    ts(view("EA", 128, 256), view("IO", 0, 128), -8.0, A.add, ko(21), A.is_equal)
+    ts(ko(18), ko(4), 75.0, A.is_lt, 512.0, A.mult)
+    ts(ko(19), ko(18), -1.0, A.mult, 512.0, A.add)
+    ts(view("LM", 112, 128), view("LM", 112, 128), ko(18), A.add)
+    ts(view("LM", 128, 144), view("LM", 128, 144), ko(19), A.add)
     ts(ko(16), rm(13), 256.0, A.mult)
     ts(ko(15), ko(6), WB, A.mult)
-    ts(ko(17), ko(17), -256.0, A.mult, rm(12), A.subtract)
+    ts(ko(17), ko(26), -256.0, A.mult, rm(12), A.subtract)
     for i, (z, c) in enumerate(((16, ko(15)), (19, ko(16)), (18, ko(16)), (17, rm(13)), (13, ko(17)))):
         scaled(view("AT", 128 * i, 128 * i + 128), view("IW", z, z + 128), c)
-    ts(view("YB", 128, 139), view("IO", 0, L, 16), ko(0), A.add)
+        mm(bank(2, 128), I, view("AT", 128 * i, 128 * i + 128), i == 0, i == 4)
+    for h in range(2):
+        scaled(view("AE", 128 * h, 128 * h + 128), bank(2, 128), ko(2 if h else 3))
+    ts(view("YB", 128, 150), view("IO", 0, 22), 16.0, A.mult, ko(0), A.add)
     ts(ko(24), ko(0), 4.0, A.mult)
-    ts(view("DI", 0, 11), view("YB", 128, 139), -5.0, A.add, 1.0 / 11, A.mult)
     for w in range(2):
         ts(view("DL", w, 22, 2), view("IO", 0, L, 16), 4.0, A.mult, ko(24), A.add)
-    ts(view("YB", 144, 155), view("YB", 128, 139), 32.0, A.mult)
-    ts(view("YB", 160, 171), view("DI", 0, 11), -351.0, A.mult)
+    for t in range(1, RO):
+        ts(view("DL", 22 * t, 22 * t + 22), view("DL", 0, 22), float(t), A.add)
+    ts(view("DI", 0, 11), view("YB", 128, 139), -5.0, A.add, 1.0 / 11, A.mult)
+    ts(view("YB", 160, 171), view("YB", 128, 139), 32.0, A.mult)
     ts(ko(8), ko(2), 16.0, A.mult)
-    tt(view("YB", 160, 171), view("YB", 160, 171), view("YB", 144, 155), A.add)
+    ts(view("YB", 176, 187), view("DI", 0, 11), -351.0, A.mult, ko(8), A.add)
+    tt(view("YB", 176, 187), view("YB", 176, 187), view("YB", 160, 171), A.add)
+    cp(view("KL", 0, 11), view("YB", 176, 187))
+    ts(view("YI", 64, 86), view("YB", 128, 150), -10.5, A.add, 1.0 / 22, A.mult)
+    ts(view("YB", 192, 214), view("YB", 128, 150), 16.0 * NS_, A.mult, NS_ - 1.0, A.add)
+    ts(view("YB", 224, 246), view("YI", 64, 86), -351.0 * NS_, A.mult)
+    tt(view("YB", 224, 246), view("YB", 224, 246), view("YB", 192, 214), A.add)
+    cp(view("PL"), view("YB", 224, 246))
     ts(ko(25), ko(0), 1.0 / 16, A.mult)
-    ts(view("KL", 0, 11), view("YB", 160, 171), ko(8), A.add)
-    for h in range(2):
-        ts(half("SN", h), bank(4 + h), 256.0, A.add)
-    first_sent = send(0)
-    ms(view("XF", V, W), BIGX)
     ts(view("KC"), view("IO"), 0.0, A.mult, ko(25), A.add)
+    cp(view("LC"), view("YB", 128, 140))
+    cp(view("VL", 0, 11), view("YB", 128, 139))
+    ts(view("FP", 0, 42), view("IO", 0, 42), 16.0, A.mult, ko(0), A.add)
     for h in range(2):
-        act(half("TP", h), bank(4 + h), AF.Copy)
-    for h in range(2):
-        act(view("BF", H * h, H * h + H), bank(6 + h, H), AF.Copy)
+        ts(view("FT", 16 * h + 12, 192, 32), view("IO", 0, 192, 32), ko(9), A.add)
+    for i in (13, 14, 15):
+        ms(view("FT", i, 192, 16), 1.0)
     ts(view("E8", 0, 256, 1, 0, 8), view("I8", 0, 256, 1, 0, 8), 0.0, A.is_equal)
     ts(view("MI", 4, 5, 1, 0, 8), view("T8", 0, 1, 1, 0, 8), 4080, A.bitwise_and)
     ts(view("MI", 5, 6, 1, 0, 8), view("T8", 0, 1, 1, 0, 8), 15, A.bitwise_and)
-    cp(ko(9), pi(4))
     cp(view("MB", 4, 6, 1, 0, 8), view("MI", 4, 6, 1, 0, 8))
     for h in range(2):
         for i in range(2):
             mm(bank(1, 1, h), view("E8", 128 * h, 128 * h + 128, 1, 0, 8), view("MB", 4 + i, 5 + i, 1, 0, 8), h == 0 and i == 0, h == 1 and i == 1)
-    for i in range(5):
-        mm(bank(2, 128), I, view("AT", 128 * i, 128 * i + 128), i == 0, i == 4)
     for h in range(2):
-        scaled(view("AE", 128 * h, 128 * h + 128), bank(2, 128), ko(2 if h else 3))
-    ms(view("BF", V, W + L), 0.0)
-    cp(view("Y"), ind(view("CI"), view("DL", 0, 22)))
+        ts(view("THR", h, 12, 2), view("IO", 0, 6), 0.0, A.mult, bank(1, 1, h), A.add)
+    ts(view("TT", 0, 12), view("THR", 0, 12), 4096.0, A.min)
+    turned(0, "CI")
     fourfold("XV0", "XM", 0, cp)
-    tr(view("YT"), view("Y"))
-    ms(view("XM", 0, V, 4), BIGX)
-    cp(view("CK0"), ind(view("YT"), view("KL", 0, 11)))
-    cp(view("XF", 0, V), view("XM"))
-    key_start()
-    need("y", first_sent)
-    dma("y", "d4", view("SI"), (T.succ[:],))
-    for k in range(8):
-        dma("y", "d%d" % (9 + k), view("SE32", 44 * k, 44 * k + 44), (T.succ[2 * k::16, :],))
     fourfold("RV0", "R", 0, gcopy)
     fourfold("PV0", "P", 0, gcopy)
-    gfill(view("RF", W, W + L), 0)
-    gfill(view("NS"), 0)
-    iota(view("M4"), [[-1, 4]], -1, 0)
-    key_bits(0, 0)
-    window(0, (1, 2, 3))
-
-    def thresholds():
-        ms(view("LW"), 0.0); ms(view("LM"), 0.0)
-        for h in range(2):
-            ts(view("FT", 16 * h + 12, 192, 32), view("IO", 0, 192, 32), ko(9), A.add)
-        for i in (13, 14, 15):
-            ms(view("FT", i, 192, 16), 1.0)
-        ts(view("LC"), view("IO", 0, 192, 16), ko(0), A.add)
-        ms(view("WT", 48, 64), 2.0)
-        cp(ko(20), pi(5))
-        scan(view("WT", 64, 80), view("WT", 48, 64), view("F2", 0, 16), 0.25, A.mult, A.add)
-        ts(view("BO"), view("IB"), ko(1), A.is_equal)
-        tt(view("WT", 80, 96), view("WT", 64, 80), view("RM"), A.mult)
-        ts(ko(18), ko(4), 75.0, A.is_lt, 512.0, A.mult)
-        red(ko(10), view("WT", 80, 96))
-        ts(ko(19), ko(18), -1.0, A.mult, 512.0, A.add)
-        tt(ko(7), ko(10), ko(6), A.mult)
-        for h in range(2):
-            ts(view("THR", h, 12, 2), view("IO", 0, 6), 0.0, A.mult, bank(1, 1, h), A.add)
-        ts(view("ZB"), view("Z1"), ko(7), A.mult)
-        ts(view("TT", 0, 12), view("THR", 0, 12), 4096.0, A.min)
-        ts(view("BQ"), view("BO"), rm(0), A.mult, 512.0, A.mult)
-        ms(view("LW", 112, 128), 512.0)
-        ts(view("LM", 112, 128), view("LM", 112, 128), ko(18), A.add)
-        ts(view("LM", 128, 144), view("LM", 128, 144), ko(19), A.add)
-
-    thresholds()
+    ms(view("XM", 0, V, 4), BIGX)
+    cp(view("XF", 0, V), view("XM"))
     cp(view("CF"), view("CI"))
-    ts(view("DL", 22, 44), view("DL", 0, 22), 1.0, A.add)
-
-    def unpack_p(e, b):
-        o = view("PF", V + G * b, V + G * b + G)
-        ts(o, view("LU%d" % (e % 2), G * b, G * b + G), MAGIC - 128.0, A.add, MAGIC, A.subtract)
-        ts(o, o, 0.0, A.max, 1.0 / 256, A.mult)
-        for h in range(2):
-            mm(bank(4 + 2 * (b != near) + h), view("I256"), half("PF", h, V + G * b), True, True)
-
-    def unpack_t(e, b):
-        ts(view("T32", G * b, G * b + G), view("LU%d" % (e % 2), G * b, G * b + G), -256.0, A.add)
-
-    def unpack_r(b):
-        for h in range(2):
-            tt(half("RF", h, V + G * b), bank(4 + 2 * (b != near) + h), half("T32", h, G * b), A.subtract)
+    ts(view("SF"), view("SI"), ko(20), A.mult)
+    for r in range(2):
+        cp(view("SE", L * r, L * r + L), view("SE32", r, H, 2))
+    distances(0)
 
     for t in range(RO):
         last = t == RO - 1
-        par = t % 2
-        o = (t + 2) % 4
+        par, o = t % 2, (t + 2) % 4
         actv = lambda nm: view(nm, t, V, 4)
-        bl = view("BL", 0, 11)
+        bl, rf = view("BL", 0, 11), view("RF", 0, W)
         pv, rv, xv = "PV%d" % par, "RV%d" % par, "XV%d" % par
-        ps = PS_[t]
-        unpack_p(t, near)
-        unpack_t(t, near)
-        unpack_p(t, far)
-        unpack_r(near)
-        unpack_t(t, far)
-        unpack_r(far)
-        runs = [(k, min(k + 4, ps)) for k in range(0, ps, 4)]
-
-        def p_gather(i):
-            k0, k1 = runs[i]
-            act(ent("GP", k0, k1), ind(view("PF"), ck(t, k0, k1)), AF.Copy)
-            for k in range(k0, k1, 2):
-                diff("GP", rv, k, 2 + 4 * (i % 2) + (k - k0) // 2)
-
-        def p_test(i):
-            k0, k1 = runs[i]
-            for k in range(k0, k1, 2):
-                act(ent("A2", k, k + 2), bank(2 + 4 * (i % 2) + (k - k0) // 2, H), AF.Relu, 1.0)
-
-        for c in range(4):
-            tt(ent("A1", 4 * c, 4 * c + 4), ind(view("RF", 0, W), ck(t, 4 * c, 4 * c + 4)), view(pv), A.is_le)
-        for k in range(ps, 16, 2):
-            tt(ent("A2", k, k + 2), ind(view("PF"), ck(t, k, k + 2)), view(rv, 0, H), A.is_ge)
-        p_gather(0)
-        for i in range(len(runs)):
-            if i + 1 < len(runs):
-                p_gather(i + 1)
-            p_test(i)
-            key_add("ZO", "A1", 4 * i, 4 * i + 4)
-            key_add("ZO", "A2", *runs[i])
-        key_add("ZO", "A1", 4 * len(runs), 16)
-        key_add("ZO", "A2", ps, 16, True)
-        if t == 0:
-            ts(view("SF"), view("SI"), ko(20), A.mult)
+        for c in range(len(PARTS) - 1):
+            for b in (near, far):
+                lo, hi = G * b + PARTS[c], G * b + PARTS[c + 1]
+                lu, pf, pb = view("LU%d" % par, lo, hi), view("PF", V + lo, V + hi), bank(4 + 2 * (c % 2) + (b != near), hi - lo)
+                ts(pf, lu, MAGIC - 128.0, A.add, MAGIC, A.subtract)
+                ts(pf, pf, 0.0, A.max, 1.0 / 256, A.mult)
+                mm(pb, view("I256"), pf, True, True)
+                ts(view("T32", lo, hi), lu, -256.0, A.add)
+                tt(view("RF", V + lo, V + hi), pb, view("T32", lo, hi), A.subtract)
+        for k in range(0, 16, 4):
+            tt(ent("A1", k, k + 4), ind(rf, ck(t, k, k + 4)), view(pv), A.is_le)
+            key_add("ZO", "A1", k, k + 4)
+        for k in range(0, PS_, 4):
+            act(ent("GP", k, min(k + 4, PS_)), ind(view("PF"), ck(t, k, min(k + 4, PS_))), AF.Copy)
+        for k in range(0, 16, 2):
+            if k < PS_:
+                b = (2, 3, 6, 7)[k // 2 % 4]
+                diff("GP", rv, k, b)
+                act(ent("A2", k, k + 2), bank(b, H), AF.Relu, 1.0)
+            else:
+                tt(ent("A2", k, k + 2), ind(view("PF"), ck(t, k, k + 2)), view(rv, 0, H), A.is_ge)
+            key_add("ZO", "A2", k, k + 2)
+        mm(bank(0, 16, L), I, view("KC", L, 192), False, True)
         gcopy(view("SV"), actv("SF"))
         gcopy(view("CV"), actv("CF"))
-        if t == 0:
-            iota(view("RSE"), [[0, H], [-256, NS_]], 256, 0)
-            iota(view("RS8"), [[0, 128], [-256, 8]], 256, 0)
-            gfill(view("ON"), 1)
-        if not last:
-            fourfold("XV%d" % (1 - par), "XM", t + 1, gcopy)
-            if t == 0:
-                gfill(view("C3"), CAP)
-                gfill(view("CN", 0, 2), 0)
-            fourfold("PV%d" % (1 - par), "P", t + 1, gcopy)
-            fourfold("RV%d" % (1 - par), "R", t + 1, gcopy)
-        ks = view("KS", 15, 192, 16)
-        tr(view("KT"), bank(0, 192))
         if t:
             mm(bank(2, L), view("BW"), actv("BF"), True, True)
             scaled(view("NS"), bank(2, L), 512.0)
         if not last:
-            act(view("Y"), ind(view("CF"), view("DL", 22 * t + 22, 22 * t + 44)), AF.Copy)
-        scan(view("KS"), view("RK"), view("KT"), 0.0, A.max, A.min)
+            for nm, src in (("XV", "XM"), ("PV", "P"), ("RV", "R")):
+                fourfold("%s%d" % (nm, 1 - par), src, t + 1, gcopy)
+            turned(t + 1, "CF")
+        ks = view("KS", 15, 192, 16)
+        tr(view("KT"), bank(0, 192))
         ts(view("OM"), bank(0, L), WO, A.is_ge, 1000.0, A.mult)
+        scan(view("KS"), view("RK"), view("KT"), 0.0, A.max, A.min)
         ts(view("DI", 0, 12), ks, -0.47, A.add)
-        tt(view("NA", 0, 12), ks, view("TT", 0, 12), A.is_ge)
         tt(view("K6", 0, 12), ks, view("DI", 0, 12), A.subtract)
         mm(bank(1, 12), I, view("LC"), True, False)
         for w in range(2):
             for h in range(2):
                 j = 128 * (2 * h + w)
                 mm(view("B1", w, 12, 2), view("SW", j, j + 128), view("K6", h, 12, 2), False, w == 1 and h == 1)
-        cp(view("FT", 10, 192, 16), view("DI", 0, 12))
-        ts(view("NA", 16, 28), ks, 4096.0, A.is_ge, 2.0, A.mult)
-        tt(view("FT", 11, 192, 16), view("DI", 0, 12), view("FT", 10, 192, 16), A.subtract)
-        tt(view("F2", 0, 192, 16), view("NA", 0, 12), view("NA", 16, 28), A.add)
-        tr(view("FR"), view("FT"))
         cp(view("LS", 0, 11), bank(1, 11))
+        cp(view("FT", 10, 192, 16), view("DI", 0, 12))
+        tt(view("FT", 11, 192, 16), view("DI", 0, 12), view("FT", 10, 192, 16), A.subtract)
+        tr(view("FR"), view("FT"))
+        tt(view("NA", 0, 12), ks, view("TT", 0, 12), A.is_ge)
+        ts(view("NA", 16, 28), ks, 4096.0, A.is_ge, 2.0, A.mult)
+        tt(view("F2", 0, 192, 16), view("NA", 0, 12), view("NA", 16, 28), A.add)
         tr(view("G2"), view("F2"))
         tt(view("FE"), ind(view("BC"), view("LS", 0, 11)), view("FR", 0, L), A.max)
-        mm(bank(0, L), view("BQ"), view("G2", 0, L), True, False)
         mm(bank(6, L), view("AE", 0, 128), view("FE"), True, True)
         mm(bank(7, L), view("AE", 128, 256), view("FE"), True, True)
-        if not last:
-            tr(view("YT"), view("Y"))
         cp(view("LE", 0, L), bank(6, L))
         act(view("LE", L, 2 * L), bank(7, L), AF.Copy)
         listed(bank(1, 11), "ZB", "FE", 0, L)
+        ts(bl, bank(1, 11), 511.5, A.add)
+        tt(view("MN"), ind(view("R"), bl), view(rv, 0, L), A.min)
+        tt(view("DS"), ind(view("SF"), bl), view("SV"), A.subtract)
         done = {}
-        for i in (0, 1, 2, 3, 4, 5, 6, 7, 8, 10, 9, 11):
+        for i in range(12):
             a, j = TILES[i]
             c = (0, 117, 234)[j]
-            if i in (9, 11):
-                need("p", done[i - 1])
             done[i] = mm(view("B%d" % (2 + i // 2), L * (i % 2), L * (i % 2) + L, 1, 0, 118), view("LE", c, c + 118, 1, 32 * a, 32 * a + 32),
-                         view("FE", 0, L, 1, 32 * a, 32 * a + 32), True, True)
-        if not last:
-            cp(view("CK%d" % (1 - par)), ind(view("YT"), view("KL", 0, 11)))
-        ts(bl, bank(1, 11), 511.5, A.add)
-        if t == 0:
-            ts(ko(13), rm(13), -1536.0, A.mult, rm(12), A.subtract)
-            ts(ko(14), rm(14), -0.5, A.mult, ko(7), A.add)
-        tt(view("MN"), ind(view("R"), bl), view(rv, 0, L), A.min)
+                         view("FE", 0, L, 1, 32 * a, 32 * a + 32), True, True, [done[i - 1]] if i in (9, 11) else [])
+        mm(bank(0, L), view("BQ"), view("G2", 0, L), True, False)
+        mm(bank(0, L), I, view("MN"), False, False)
         for b in range(6):
             y = view("YP", H * b, H * b + H, 1, 0, 118)
             i = view("B%d" % (2 + b), 0, H, 1, 0, 118)
@@ -553,167 +636,106 @@ def rank_program(g, core, T, topo):
                     k = 112 - 16 * (2 * a + j // 2)
                     l = view("LW", k, k + 128, 1, 0, 118)
                 mm(bank(0, L), l, view("YP", L * i, L * i + L, 1, 0, 118), False, i == 11)
-            if b == 0:
-                mm(bank(0, L), I, view("MN"), False, False)
-        if not last:
-            act(view("MX"), ind(view("P"), bl), AF.Copy)
-        if t == 0:
-            ts(view("VL", 0, 11), view("IO", 0, L, 16), ko(0), A.add)
-            tt(ko(13), ko(13), ko(14), A.add)
-            ms(view("VL", 16, 27), float(DUMP))
-            ts(ko(21), ko(0), -1.0, A.add, 0.5, A.mult)
-            ts(view("ZS"), view("Z1"), ko(13), A.mult)
-            for r in range(2):
-                cp(view("SE", L * r, L * r + L), view("SE32", r, H, 2))
-            ts(ko(21), ko(21), ko(1), A.add)
-            ts(view("KO", 28, 32), view("M4"), rm(13), A.mult)
-            ts(view("EA", 0, 128), view("IO", 0, 128), ko(21), A.is_equal)
-            ts(view("EA", 128, 256), view("IO", 0, 128), -8.0, A.add, ko(21), A.is_equal)
-            scaled(view("BN"), view("BO"), -1.0)
-            scaled(view("BV"), view("BO"), rm(13))
-            scaled(view("BW"), view("BV"), -1.0)
-            for r in range(4):
-                comp("s", sca.activation, view("BT", r, V, 4), [view("BF", r, V, 4), ko(28 + r)], T.BT[:, r:V:4], T.BF[:, r:V:4], AF.Identity,
-                     bias=ko(28 + r)[0])
         wn, hm = bank(0, L, 256), bank(7, L)
-        tt(view("DS"), ind(view("SF"), bl), view("SV"), A.subtract)
-
-        def candidates():
-            mm(hm, view("BQ"), view("G2", 0, L), True, True)
-            tt(view("DC"), ind(view("CF"), bl), view("CV"), A.subtract)
-            tt(hm, view("OM"), hm, A.is_gt)
-            tt(hm, view("DC"), hm, A.mult)
-            tt(actv("CF"), view("CV"), hm, A.add)
-        features = [lambda: tt(view("XS"), ind(view("XM"), bl), view(xv, 0, L), A.add),
-                    lambda: ts(view("XS"), view("XS"), 1, A.arith_shift_right),
-                    lambda: tt(view("DX"), view("XS"), view(xv, 0, L), A.subtract),
-                    lambda: tt(view("DX"), view("DX"), wn, A.mult),
-                    lambda: tt(actv("XM"), view("DX"), view(xv, 0, L), A.add)]
         mm(bank(1, 11), I, view("VL", 0, 11), True, False)
         mm(bank(1, 11), I, view("VL", 16, 27), False, False)
         ts(wn, bank(0, L), 512.0, A.is_lt)
-        tt(view("QQ"), bank(0, L), view("NS"), A.add)
         tt(view("FW"), view("FE"), wn, A.mult)
         listed(bank(1, 11), "ZS", "FW", 0, L, False)
+        cp(view("SC", 0, 11), bank(1, 11))
+        tt(view("QQ"), bank(0, L), view("NS"), A.add)
         tt(actv("RF"), actv("RF"), view("QQ"), A.min)
+        cp(ind(view("RF"), view("SC", 0, 11)), view("MN"))
         tt(view("DS"), view("DS"), wn, A.mult)
         mm(bank(6, L), view("EA", 128 * (o // 2), 128 * (o // 2) + 128), view("SF", o, V, 4), True, False)
         mm(bank(6, L), view("EA", 128 * (t // 2), 128 * (t // 2) + 128), view("SV"), False, False)
         mm(bank(6, L), view("EA", 128 * (t // 2), 128 * (t // 2) + 128), view("DS"), False, True)
-        features.pop(0)()
-        cp(view("SC", 0, 11), bank(1, 11))
-        cp(ind(view("RF"), view("SC", 0, 11)), view("MN"))
+        cp(view("SO"), bank(6, L))
         if not last:
-            gfill(view("XM", t + 1, V, 4), int(BIGX))
             sig([("BO", "R"), ("BV", "BF"), ("BN", "P")], True, False)
-        rf = view("RF", 0, W)
+            tt(actv("SF"), view("SV"), view("DS"), A.add)
+            act(view("MX"), ind(view("P"), bl), AF.Copy)
+            tt(view("MX"), view("MX"), wn, A.mult)
+            tt(actv("P"), actv("P"), view("MX"), A.max)
+            cp(ind(view("BF"), view("SC", 0, 11)), actv("BT"))
+            red(view("MC", 0, 1), wn)
+        tt(actv("R"), bank(0, L), actv("R"), A.min)
+        act(view("XB"), ind(view("XM"), bl), AF.Copy)
+        mm(hm, I, view("XB"), True, False)
+        mm(hm, I, view(xv, 0, L), False, True)
+        act(view("XH"), hm, AF.Identity, WHOLE, 0.4995)
+        act(view("XB"), view("XH"), AF.Identity, -WHOLE)
+        mm(hm, I, view("XB"), True, False)
+        mm(hm, view("NI"), view(xv, 0, L), False, True)
+        act(view("DX"), hm, AF.Copy)
+        tt(view("DX"), view("DX"), wn, A.mult)
+        mm(hm, I, view("DX"), True, False)
+        mm(hm, I, view(xv, 0, L), False, True)
+        act(actv("XM"), hm, AF.Copy)
+        mm(hm, view("BQ"), view("G2", 0, L), True, True)
+        tt(view("DC"), ind(view("CF"), bl), view("CV"), A.subtract)
+        tt(hm, view("OM"), hm, A.is_gt)
+        tt(hm, view("DC"), hm, A.mult)
+        tt(actv("CF"), view("CV"), hm, A.add)
         se = lambda k: view("SE", L * par + 22 * k, L * par + 22 * k + 22)
+        slot = lambda i: view("GE", i, NS_ * H, NS_)
         for k in range(MV, 8):
-            act(view("GE", k - MV, NS_ * H, NS_), ind(rf, se(k)), AF.Copy)
-        ac = lambda k: view("AC", H * (k % 2), H * (k % 2) + H)
-        cp(ac(0), ind(rf, se(0)))
-        extra = [lambda: cp(view("SO"), bank(6, L)), lambda: tt(actv("R"), bank(0, L), actv("R"), A.min)]
-        if not last:
-            extra += [lambda: cp(ind(view("BF"), view("SC", 0, 11)), actv("BT")),
-                      lambda: tt(view("MX"), view("MX"), wn, A.mult),
-                      lambda: tt(actv("P"), actv("P"), view("MX"), A.max)]
-        for k in range(1, MV):
-            if extra:
-                extra.pop(0)()
-            tt(ac(k) if k < MV - 1 else view("GE", NS_ - 1, NS_ * H, NS_), ind(rf, se(k)), ac(k - 1), A.min)
-        for c in range(len(CUTS) - 1):
-            act(view("GA", 16 * CUTS[c], 16 * CUTS[c + 1]), ind(rf, view("SO", CUTS[c], CUTS[c + 1])), AF.Copy)
-        if extra:
-            extra.pop(0)()
-        if t == 0:
-            ts(view("YB", 0, 22), view("IO", 0, 22), 16.0, A.mult, ko(0), A.add)
-            ts(view("YI", 0, 22), view("YB", 0, 22), -10.5, A.add, 1.0 / 22, A.mult)
-            ts(view("YB", 32, 54), view("YB", 0, 22), 16.0 * NS_, A.mult, NS_ - 1.0, A.add)
-            ts(view("YB", 64, 86), view("YI", 0, 22), -351.0 * NS_, A.mult)
-            ts(view("Z0"), view("Z1"), rm(0), A.mult)
-            tt(view("YB", 64, 86), view("YB", 64, 86), view("YB", 32, 54), A.add)
-            ts(view("IBG"), I, BIGT, A.mult)
-            cp(view("PL"), view("YB", 64, 86))
-            ts(view("NBG"), I, -BIGT, A.mult)
+            act(slot(k - MV), ind(rf, se(k)), AF.Copy)
+        ac = lambda k: view("AC", H * (k % 4), H * (k % 4) + H) if k < MV - CHAINS else slot(8 - 2 * MV + CHAINS + k)
+        for k in range(MV):
+            if k < CHAINS:
+                cp(ac(k), ind(rf, se(k)))
+            else:
+                tt(ac(k), ind(rf, se(k)), ac(k - CHAINS), A.min)
         scan(view("GF"), view("RSE"), view("GE"), 0.0, A.max, A.min)
-        while extra:
-            extra.pop(0)()
-        if not last:
-            listed(bank(1, 44), "ZB", "BF", 0, V)
-            sig([("BW", "BF"), ("BO", "P")], False, False)
-            for h in range(2):
-                mm(bank(4 + h), view("I256"), half("P", h), True, False)
-                mm(bank(4 + h), view("NBG"), view("ON"), False, False)
         rp = view("R", par, V, 2)
-
-        def low(c):
-            a, e = 16 * CUTS[c], 16 * CUTS[c + 1]
-            scan(view("GS", a, e), view("RS8", 0, e - a), view("GA", a, e), 0.0, A.max, A.min)
-            if last and features:
-                features.pop(0)()
-            z = view("R", par + 4 * CUTS[c], 4 * CUTS[c + 1], 2)
-            tt(z, view("GS", a + 7, e, 8), z, A.min)
         tt(rp, ind(view("GF"), view("PL")), rp, A.min)
-        if not last:
-            ts(view("FL"), bank(1, 44), 511.5, A.add)
-            act(view("DT", 0, 44), bank(1, 44), AF.Identity, 511.5)
-            act(view("PF", 0, V), ind(view("P"), view("FL")), AF.Copy)
-        for c in range(len(CUTS) - 1):
-            low(c)
+        for lo, hi in zip(CUTS, CUTS[1:]):
+            act(view("GA", 16 * lo, 16 * hi), ind(rf, view("SO", lo, hi)), AF.Copy)
+            scan(view("GS", 16 * lo, 16 * hi), view("RS8", 0, 16 * (hi - lo)), view("GA", 16 * lo, 16 * hi), 0.0, A.max, A.min)
+            z = view("R", par + 4 * lo, 4 * hi, 2)
+            tt(z, view("GS", 16 * lo + 7, 16 * hi, 8), z, A.min)
         if last:
-            dma("y", "d6", (T.yr[:],), view("R"))
-            while features:
-                features.pop(0)()
             dma("y", "d7", (T.yx[:],), view("XM"))
-            candidates()
-            dma("y", "d8", (T.yc[:],), view("CF"))
+            dma("s", "d8", (T.yc[:],), view("CF"))
+            dma("y", "d6", (T.yr[:, 0:4 * CUTS[2]],), view("R", 0, 4 * CUTS[2]))
+            dma("s", "d19", (T.yr[:, 4 * CUTS[2]:V],), view("R", 4 * CUTS[2], V))
             break
-        sig([("BN", "R")], False, True)
-        for h in range(2):
-            mm(bank(4 + h), view("NI"), half("R", h), False, False)
-        if t == 0:
-            ts(view("FP", 0, 42), view("IO", 0, 42), 16.0, A.mult, ko(0), A.add)
-            ts(view("ZN"), view("Z0"), -1.0, A.mult)
-            ms(view("ZD", 0, 1), 0.0)
-            tt(view("ZD", 1, 144), view("Z0", 1, 144), view("Z0", 0, 143), A.subtract)
-        features.pop(0)()
+        listed(bank(1, 44), "ZB", "BF", 0, V)
+        ts(view("FL"), bank(1, 44), 511.5, A.add)
+        act(view("DT", 0, 44), bank(1, 44), AF.Identity, 511.5)
+        sig([("BW", "BF"), ("BO", "P"), ("BN", "R")], False, True)
         ts(half("CH", 0), bank(2), 0.5, A.is_gt)
         act(half("CH", 1), bank(3), AF.Sign)
-        act(view("RF", 0, V), ind(view("R"), view("FL")), AF.Copy)
-        key_bits(t + 1, 0)
-        tt(view("DT", 44, 86), view("DT", 0, 42), view("FP", 0, 42), A.subtract)
-        ts(view("DT", 88, 130), view("DT", 0, 42), float(G), A.is_lt)
-        scan(view("CN", 2, G + 2), view("CH"), view("C3"), 0.0, A.add, A.min)
+        scan(half("CN", 0, 2), half("CH", 0), view("C3"), 0.0, A.add, A.min)
+        scan(half("CN", 1, 2), half("CH", 1), view("C3"), view("CN", 337, 338), A.add, A.min)
         for h in range(2):
-            mm(bank(4 + h), view("IBG"), half("CN", h, 2), False, False)
-            mm(bank(4 + h), view("NBG"), half("CN", h, 1), False, True)
+            for i, (z, r) in enumerate((("I256", half("P", h)), ("NBG", view("ON")), ("NI", half("R", h)), ("IBG", half("CN", h, 2)),
+                                        ("NBG", half("CN", h, 1)))):
+                mm(bank(4 + h), view(z), r, i == 0, i == 4)
+            tt(half("TP", h), bank(4 + h), half("TP", h), A.max)
         for q in range(16):
             mm(bank(1, 42), zq("ZD" if q < 15 else "Z0", q), view("CN", 2 + q, G + 2, 16), q == 0, False)
         mm(bank(1, 41, 1), zq("ZN", 0), view("CN", 17, G - 14 + 2, 16), False, True)
+        tt(view("DT", 44, 86), view("DT", 0, 42), view("FP", 0, 42), A.subtract)
+        ts(view("DT", 88, 130), view("DT", 0, 42), float(G), A.is_lt)
         tt(view("DT", 44, 86), view("DT", 44, 86), view("DT", 88, 130), A.mult)
-        features.pop(0)()
-        for h in range(2):
-            tt(half("TP", h), bank(4 + h), half("TP", h), A.max)
-        features.pop(0)()
         tt(view("DT", 132, 174), bank(1, 42), view("DT", 44, 86), A.mult)
-        features.pop(0)()
         tt(view("FP", 0, 42), view("FP", 0, 42), view("DT", 132, 174), A.add)
-        act(view("XF", 0, V), ind(view("XM"), view("FL")), AF.Copy)
-        red(view("MC", 0, 1), wn)
         cp(view("FU", 0, 42), view("FP", 0, 42))
+        for c, (lo, hi) in enumerate(zip(PARTS, PARTS[1:])):
+            ts(view("SN", lo, hi), ind(view("TP"), view("FU", lo // 16, hi // 16)), 256.0, A.add)
+            send(t + 1, c)
+        gfill(view("XM", t + 1, V, 4), int(BIGX))
+        for dst, src in (("PF", "P"), ("XF", "XM"), ("RF", "R")):
+            act(view(dst, 0, V), ind(view(src), view("FL")), AF.Copy)
         ts(view("MB", 0, 1), view("MC", 0, 1), 1.0 / 16, A.mult)
-        ts(view("SN"), ind(view("TP"), view("FU", 0, 42)), 256.0, A.add)
-        send(t + 1)
-        key_start()
         mm(bank(1, 1), view("ON", 0, 128), view("MB", 0, 1), True, True)
-        if t == 0:
-            ts(view("DL", 44, 66), view("DL", 0, 22), 2.0, A.add)
-            ts(view("DL", 66, 88), view("DL", 0, 22), 3.0, A.add)
         cp(view("MI", 0, 1), bank(1, 1))
-        candidates()
         ts(view("MI", 1, 2), view("MI", 0, 1), 31, A.bitwise_and)
-        tt(actv("SF"), view("SV"), view("DS"), A.add)
         cp(view("MC", 1, 2), view("MI", 1, 2))
-        window(t + 1, (1, 2, 3))
         ts(view("TT", 0, 12), view("THR", 0, 12), view("MC", 1, 2), A.add, 4096.0, A.min)
+        distances(t + 1)
+    for call in order():
+        call()
     finish()

@@ -7,12 +7,11 @@ L = V // 4
 H = V // 2
 NE = 16 * L
 DUMP = W
-MV = 4
-CHAINS = 2
-NS_ = 8 - MV + CHAINS
+SLOTS = 4
 XV_ = 3
-PS_ = 14
-CUTS = (0, 64, 128, 156, L)
+RUNS_R = (0, 4, 8, 12, 14, 16)
+RUNS_P = (0, 4, 8, 12)
+CUTS = (0, 64, 128, 152, 168, L)
 PARTS = (0, 352, G)
 BIGX = 512.0
 WO = 16384.0
@@ -22,6 +21,22 @@ WHOLE = 1.5 * 2.0 ** 23
 MAGIC = 2.0 ** 31
 TILES = [(0, 0), (0, 1), (1, 0), (1, 1), (2, 0), (2, 1), (3, 0), (3, 1), (0, 2), (1, 2), (2, 2), (3, 2)]
 
+_UNPACK = "round0 -m2 past0 round2 -m3 past2 round1 reach0 past1 round3 reach2 past3 -m4 reach1 reach3 "
+_MERGE = ("pv r0 r1 r2 r3 r4 key ordered least d asks dhi k f2 dlo gt fr chosen fe -sf fd le b mn y0 y2 y4 ds ns "
+          "fw qq wn own dsw sc q1 put ")
+_LOW = "gf o0 even o1 low0 o2 low1 o3 low2 "
+_TESTS = "g0 g1 p0 g2 p1 p2 n2 n3 gone le "
+_RIVALS = "off past0 past2 past1 past3 a1 a2 le b pairs y0 y1 y2 y3 y4 y5 xh fw "
+LINES = {"v": _UNPACK + _MERGE + "mx rnew name e0 so dx e1 pnew e2 e3 " + _LOW + "fl low3 ff ch0 df dc cn0 o4 dfm cn1 low4 hm turn tp0 ck go dcm "
+              "fp tp1 fu cf send +x0 mc +x1 m0 +x2 m1",
+         "s": _TESTS + "twice y1 y3 y5 xb mx xh dx e0 e1 e2 e3 o0 o1 o2 o3 o4 xm ch1 XF PF +x3 +n0 +a3 +x0 +n1 +x1 RF +x2",
+         "p": _RIVALS + "oldr old dx oldp so",
+         "g": "send +cv"}
+LAST = {"v": _UNPACK + _MERGE + "rnew dc e0 so e1 hm dcm e2 cf dx e3 " + _LOW + "o4 low3 low4",
+        "s": _TESTS + "y1 y3 y5 xb xh e1 dx e2 e3 o0 xm o1 o2 o3 o4",
+        "p": _RIVALS + "so dx",
+        "g": ""}
+
 MATS = ["NI", "I256", "IBG", "NBG", "BO", "BN", "BW", "BV", "BQ"]
 SCRATCH = {}
 
@@ -29,15 +44,15 @@ SCRATCH = {}
 def _declare():
     bf = [("XM", V), ("R", V), ("P", V), ("RF", W + L), ("PF", W), ("XF", W), ("BF", W + L), ("BT", V), ("LH", 64),
           ("RV0", V), ("RV1", V), ("PV0", V), ("PV1", V), ("XV0", V), ("XV1", V), ("GX", NE), ("AX", NE), ("A1", NE), ("A2", NE), ("GP", NE),
-          ("BC", NE), ("GA", NE), ("GS", NE), ("GE", NS_ * H), ("GF", NS_ * H), ("AC", 4 * H), ("RS8", 1024), ("RSE", NS_ * H), ("E8", 256),
-          ("IW", 160), ("MAT", 128 * len(MATS)), ("Z1", 144), ("ZO", 144), ("Z0", 144), ("ZN", 144), ("ZD", 144),
+          ("BC", NE), ("GA", NE), ("GS", NE), ("GE", SLOTS * H), ("GF", SLOTS * H), ("AC", SLOTS * H), ("RS8", 1024), ("RSE", SLOTS * H),
+          ("E8", 256), ("IW", 160), ("MAT", 128 * len(MATS)), ("Z1", 144), ("ZO", 144), ("Z0", 144), ("ZN", 144), ("ZD", 144),
           ("ZB", 144), ("ZS", 144), ("SW", 512), ("AE", 256), ("AT", 640),
-          ("LW", 240), ("LM", 256), ("ON", 336), ("KC", 192), ("LC", 12), ("VL", 32), ("C3", 336), ("K6", 16), ("FT", 192), ("FR", 192),
-          ("F2", 192), ("G2", 192), ("FE", L), ("FW", L), ("LE", 2 * L), ("YP", 12 * L), ("MN", L), ("MX", L), ("DX", L), ("XB", L),
+          ("LW", 240), ("LM", 256), ("ON", H), ("KC", 192), ("LC", 12), ("C3", 336), ("K6", 16), ("FT", 192), ("FR", 192),
+          ("F2", 192), ("G2", 192), ("FE", L), ("FW", L), ("FD", L), ("LE", 2 * L), ("YP", 12 * L), ("MN", L), ("MX", L), ("DX", L), ("XB", L),
           ("OM", L), ("NS", L), ("QQ", L), ("CH", G), ("CN", G + 16), ("MB", 8), ("M4", 4)]
     f4 = [("CF", V), ("SF", V), ("IO", 192), ("IB", 128), ("I8", 256), ("KO", 40), ("RM", 16), ("WT", 96), ("RK", 192), ("KT", 192), ("KS", 192),
-          ("NA", 32), ("THR", 16), ("TT", 16), ("DS", L), ("DC", L), ("XH", L), ("SV", L), ("CV", L), ("DT", 176), ("MC", 4), ("TP", G),
-          ("T32", 2 * G), ("Y", H), ("YT", H), ("EA", 256), ("FP", 44), ("YB", 320)]
+          ("NA", 48), ("THR", 16), ("TT", 16), ("DS", L), ("DC", L), ("XH", L), ("SV", L), ("CV", L), ("DT", 176), ("MC", 4), ("TP", G),
+          ("Y", H), ("YT", H), ("EA", 384), ("FP", 44), ("YB", 256)]
     i4 = [("CI", V), ("SI", V), ("SE32", H), ("T8", 2), ("PI", 8), ("YI", 96), ("DI", 16), ("MI", 8)]
     u2 = [("CK0", L), ("CK1", L), ("SE", H), ("SO", L), ("DL", 88), ("KL", 12), ("PL", 22), ("LS", 16), ("BL", 16), ("SC", 16), ("FL", 44),
           ("FU", 44), ("SN", G), ("LU0", 2 * G), ("LU1", 2 * G)]
@@ -49,7 +64,7 @@ def _declare():
 
 
 _declare()
-SEMAPHORES = (["s_v", "s_s", "s_p", "s_g"] + ["d%d" % i for i in range(20)] + ["lo%d%d" % (i, c) for i in range(RO) for c in range(len(PARTS) - 1)]
+SEMAPHORES = (["s_v", "s_s", "s_p", "s_g"] + ["d%d" % i for i in range(22)] + ["lo%d%d" % (i, c) for i in range(RO) for c in range(len(PARTS) - 1)]
               + ["ar%d%d%d" % (i, c, b) for i in range(RO) for c in range(len(PARTS) - 1) for b in range(2)])
 
 
@@ -130,8 +145,9 @@ def tracker(g, T):
 
 
 CYCLE, PE_CYCLE, HOP, GATHER, SCATTER = 0.0009, 0.00045, 0.18, 1.56, 3.8
-LOAD, LOAD_GAP, CALL, FIRST, NEAR, FAR = 2.2, 0.8, 0.6, 3.5, 3.0, 4.0
-PASSES, SLACK = 3, 0.2
+LOAD, BYTE, CALL, FIRST, NEAR, FAR = 1.7, 0.00057, 0.6, 3.5, 3.0, 4.0
+SLACK = {"v": 0.1, "s": 0.06, "p": 0.02, "g": 0.0, "y": 0.0, "n": 0.0}
+ORDER = []
 
 
 def count(v): return 16 * len(range(*v[1][1][1:])) if len(v[1]) > 1 else len(range(*v[1][0][1:]))
@@ -158,8 +174,8 @@ def price(e, out, ins, both):
 def planner():
     nodes, recs, runs = [], {}, {}
 
-    def add(e, cost, tail, outs, ins, call, after=None, middle=False):
-        me, before = len(nodes), dict(after or {})
+    def add(e, cost, tail, outs, ins, call, after, middle):
+        me, before = len(nodes), dict(after)
         for (lst, wr) in ((ins, False), (outs, True)):
             for v in lst:
                 for (name, lo, hi, st) in v[1]:
@@ -178,6 +194,10 @@ def planner():
                     recs[name] = [r for r in old if keep or not covers(fp, r[0])] + [(fp, wr, me)]
         nodes.append((e, cost, tail, before, call))
         return me
+
+    def follow(calls):
+        for a, b in zip(calls, calls[1:]):
+            nodes[b][3].setdefault(a, -nodes[a][2])
 
     def place(rank, before):
         later = [[] for _ in nodes]
@@ -213,8 +233,8 @@ def planner():
             soon = [z for z in when if nodes[z][0] == e and when[z] > now and rank[z] > rank[i]]
             if soon:
                 j = max(soon, key=lambda z: (rank[z], -z))
-                if max(when[j] + rank[j], when[j] + nodes[j][1] + rank[i]) + SLACK < max(now + rank[i], now + nodes[i][1] + rank[j]):
-                    fill = [z for z in ready[e] if can[z] <= now and nodes[z][1] <= when[j] - now + SLACK]
+                if max(when[j] + rank[j], when[j] + nodes[j][1] + rank[i]) + SLACK[e] < max(now + rank[i], now + nodes[i][1] + rank[j]):
+                    fill = [z for z in ready[e] if can[z] <= now and nodes[z][1] <= when[j] - now + SLACK[e]]
                     if not fill:
                         free[e] = min([when[j]] + [can[z] for z in ready[e] if can[z] > now])
                         continue
@@ -231,24 +251,29 @@ def planner():
         return start
 
     def order():
-        fwd = [{a: w + nodes[a][2] for a, w in nd[3].items()} for nd in nodes]
-        bwd = [{} for _ in nodes]
-        for i, b in enumerate(fwd):
-            for a, w in b.items():
-                bwd[a][i] = w
-        rank = [0.0] * len(nodes)
-        for i in range(len(nodes) - 1, -1, -1):
-            rank[i] = nodes[i][1] + max([w + rank[j] for j, w in bwd[i].items()] + [nodes[i][2]])
-        best = None
-        for _ in range(PASSES):
+        if not ORDER:
+            fwd = [{a: w + nodes[a][2] for a, w in nd[3].items()} for nd in nodes]
+            bwd = [{} for _ in nodes]
+            for i, b in enumerate(fwd):
+                for a, w in b.items():
+                    bwd[a][i] = w
+            rank, left = [0.0] * len(nodes), [len(b) for b in bwd]
+            todo = [i for i, x in enumerate(left) if x == 0]
+            while todo:
+                i = todo.pop()
+                rank[i] = nodes[i][1] + max([w + rank[j] for j, w in bwd[i].items()] + [nodes[i][2]])
+                for a in fwd[i]:
+                    left[a] -= 1
+                    if left[a] == 0:
+                        todo.append(a)
+            for _ in range(2):
+                start = place(rank, fwd)
+                back = place([s + nd[1] + nd[2] for s, nd in zip(start, nodes)], bwd)
+                rank = [s + nd[1] for s, nd in zip(back, nodes)]
             start = place(rank, fwd)
-            end = [s + nd[1] + nd[2] for s, nd in zip(start, nodes)]
-            if best is None or max(end) < best[0]:
-                best = (max(end), start)
-            back = place(end, bwd)
-            rank = [s + nd[1] for s, nd in zip(back, nodes)]
-        return [nodes[i][4] for i in sorted(range(len(nodes)), key=lambda z: (best[1][z], z))]
-    return add, order
+            ORDER.extend(sorted(range(len(nodes)), key=lambda z: (start[z], z)))
+        return [nodes[i][4] for i in ORDER]
+    return add, follow, order
 
 
 def rank_program(g, core, T, topo):
@@ -270,9 +295,11 @@ def rank_program(g, core, T, topo):
     near, far = sorted((0, 1), key=lambda b: source[b] not in topo.cores_of(core))
 
     issue, need, finish = tracker(g, T)
-    add, order = planner()
-    made = {}
+    add, follow, order = planner()
+    made, named, label = {}, {}, [-1, ""]
     vec, sca, ten = g.vector, g.scalar, g.tensor
+
+    def at(step): label[1] = step
 
     def view(name, lo=0, hi=None, st=1, p0=0, p1=128):
         if name in MATS:
@@ -293,11 +320,13 @@ def rank_program(g, core, T, topo):
         return me
 
     def comp(e, fn, out, ins, *args, waits=(), both=False, middle=False, **kw):
-        return plan(e, price(e, out, ins, both), 0.0, None, 1, [out], ins, lambda: fn(*args, **kw), waits, None, middle)
+        me = plan(e, price(e, out, ins, both), 0.0, None, 1, [out], ins, lambda: fn(*args, **kw), waits, None, middle)
+        named.setdefault((e, label[0], label[1]), []).append(me)
+        return me
 
-    def dma(e, sem, out, in_, waits=(), after=None):
+    def dma(e, sem, out, in_, tail=LOAD + BYTE * 2 * V, waits=(), after=None):
         q = g.sync if e == "y" else sca
-        return plan(e, 0.05, LOAD, sem, 16, [v for v in (out,) if len(v) > 1], [v for v in (in_,) if len(v) > 1],
+        return plan(e, 0.05, tail, sem, 16, [v for v in (out,) if len(v) > 1], [v for v in (in_,) if len(v) > 1],
                     lambda: q.dma_start(out[0], in_[0]).then_inc(T.sem[sem], 16), waits, after)
 
     def cp(o, i): comp("v", vec.tensor_copy, o, [i], o[0], i[0])
@@ -321,6 +350,7 @@ def rank_program(g, core, T, topo):
         comp("s", sca.activation, o, [i] + cols, o[0], i[0], f, bias=bias[0] if isinstance(bias, tuple) else bias,
              scale=scale[0] if isinstance(scale, tuple) else scale)
     def scaled(o, i, c): act(o, i, AF.Copy, 0.0, c)
+    def affine(o, i, c, d): act(o, i, AF.Identity, d, c)
     def mm(o, l, r, start, stop, waits=()):
         return comp("p", ten.matmul, o, [l, r], o[0], l[0], r[0], start, stop, waits=waits, middle=not (start or stop))
     def iota(o, pat, base, cm): comp("g", g.iota, o, [], o[0], pat, base, cm, allow_small_or_imprecise_dtypes=True)
@@ -331,9 +361,9 @@ def rank_program(g, core, T, topo):
 
     def zq(z, q): return view(z, 15 - q, 143 - q)
 
-    def listed(o, z, name, lo, hi, start=True):
+    def listed(o, z, name, lo, hi, start=True, stop=True):
         for q in range(16):
-            mm(o, zq(z, q), view(name, lo + q, hi, 16), start and q == 0, q == 15)
+            mm(o, zq(z, q), view(name, lo + q, hi, 16), start and q == 0, stop and q == 15)
 
     def send(e, c):
         lo, hi = PARTS[c], PARTS[c + 1]
@@ -344,7 +374,8 @@ def rank_program(g, core, T, topo):
                                          remote_sem=T.sem["ar%d%d%d" % (e, c, blk)], src=src[0], dst=T[land][:, G * blk + lo: G * blk + hi]))
         sem = "lo%d%d" % (e, c)
         me = plan("g", CALL + (FIRST if e + c == 0 else 0.0), NEAR, sem, local_n, [], [src], lambda: g.remote_dma_fused(out, local_sem=T.sem[sem]))
-        for b in range(2):
+        named.setdefault(("g", label[0], "send"), []).append(me)
+        for b in (near, far):
             plan("n", 0.01, 0.0, "ar%d%d%d" % (e, c, b), arrive_n[b], [view(land, G * b + lo, G * b + hi)], [], None, (),
                  {me: 0.0 if b == near else FAR - NEAR})
         return me
@@ -371,49 +402,55 @@ def rank_program(g, core, T, topo):
         mm(bank(b, H), view("NI"), view(own, 0, H), False, True)
 
     def turned(t, src):
+        at("twice")
         (cp if src == "CI" else lambda o, i: act(o, i, AF.Copy))(view("Y"), ind(view(src), view("DL", 22 * t, 22 * t + 22)))
-        tr(view("YT"), view("Y"))
-        cp(ck(t, 0, 16), ind(view("YT"), view("KL", 0, 11)))
+        at("turn"); tr(view("YT"), view("Y"))
+        at("ck"); cp(ck(t, 0, 16), ind(view("YT"), view("KL", 0, 11)))
 
     def distances(t):
         xv = "XV%d" % (t % 2)
-        mm(bank(0, L), I, view("KC", 0, L), True, False)
-        for c in range(0, 16, 4):
-            if c < 4 * XV_:
-                tt(ent("GX", c, c + 4), ind(view("XF"), ck(t, c, c + 4)), view(xv), A.subtract)
-                act(ent("AX", c, c + 4), ent("GX", c, c + 4), AF.Abs)
+        label[0] = t
+        at("start"); mm(bank(0, 192), I, view("KC"), True, False)
+        for c in range(4):
+            k = 4 * c
+            at("x%d" % c)
+            if c < XV_:
+                tt(ent("GX", k, k + 4), ind(view("XF"), ck(t, k, k + 4)), view(xv), A.subtract)
+                act(ent("AX", k, k + 4), ent("GX", k, k + 4), AF.Abs)
             else:
-                act(ent("GX", c, c + 4), ind(view("XF"), ck(t, c, c + 4)), AF.Copy)
+                act(ent("GX", k, k + 4), ind(view("XF"), ck(t, k, k + 4)), AF.Copy)
                 for i in range(2):
-                    diff("GX", xv, c + 2 * i, 2 + i)
-                    act(ent("AX", c + 2 * i, c + 2 * i + 2), bank(2 + i, H), AF.Abs)
-            key_add("Z1", "AX", c, c + 4)
-            act(ent("BC", c, c + 4), ind(view("BF", 0, W), ck(t, c, c + 4)), AF.Copy)
+                    at("x%d" % c); diff("GX", xv, k + 2 * i, 2 + i)
+                    at("a%d" % c); act(ent("AX", k + 2 * i, k + 2 * i + 2), bank(2 + i, H), AF.Abs)
+            at("a%d" % c); key_add("Z1", "AX", k, k + 4)
+            at("n%d" % c); act(ent("BC", k, k + 4), ind(view("BF", 0, W), ck(t, k, k + 4)), AF.Copy)
 
-    def sig(parts, first, last):
-        for i, (z, nm) in enumerate(parts):
-            for h in range(2):
-                mm(bank(2 + h), view(z), half(nm, h), first and i == 0, last and i == len(parts) - 1)
+    def sig(z, nm, first=False):
+        for h in range(2):
+            mm(bank(2 + h), view(z), half(nm, h), first, False)
 
-    gap = lambda a: {a: LOAD_GAP - LOAD}
-    d = dma("y", "d0", view("R"), (T.reach[:],))
-    dma("s", "d3", view("XM"), (T.x[:],), (), gap(dma("s", "d1", view("P"), (T.past[:],))))
-    for sem, dst, src in (("d2", view("CI"), T.cand), ("d5", view("T8", 0, 1, 1, 0, 8), T.th), ("d17", view("PF", 0, V), T.past),
-                          ("d18", view("RF", 0, V), T.reach), ("d4", view("SI"), T.succ)):
-        d = dma("y", sem, dst, (src[:],), (), gap(d))
+    d = dma("s", "d1", view("P", 0, H), (T.past[:, 0:H],), LOAD + BYTE * V)
+    dma("s", "d20", view("P", H, V), (T.past[:, H:V],), LOAD + BYTE * 3 * V, (), {d: -LOAD - BYTE * V})
+    d = dma("y", "d0", view("R", 0, H), (T.reach[:, 0:H],), LOAD + BYTE * 2 * V)
+    d, done = dma("y", "d21", view("R", H, V), (T.reach[:, H:V],), LOAD + BYTE * 4 * V, (), {d: -LOAD - BYTE * 2 * V}), 4 * V
+    for sem, dst, src, size in (("d2", view("CI"), T.cand, 4), ("d3", view("XM"), T.x, 2),
+                                ("d5", view("T8", 0, 1, 1, 0, 8), T.th, 0), ("d17", view("PF", 0, V), T.past, 2),
+                                ("d18", view("RF", 0, V), T.reach, 2), ("d4", view("SI"), T.succ, 4)):
+        d = dma("y", sem, dst, (src[:],), LOAD + BYTE * (done + size * V), (), {d: -LOAD - BYTE * done})
+        done += size * V
     comp("g", g.iota, pi(0), [], T.PI[:, 0:1], [[0, 1]], 0, 1)
     iota(view("IO"), [[1, 192]], 0, 0)
     iota(view("IB"), [[16, 8], [0, 16]], 0, 0)
     for h in range(2):
         iota(view("I8", 128 * h, 128 * h + 128, 1, 0, 8), [[2, 4], [0, 32]], h, -1)
     iota(view("RK"), [[0, 12], [-16000, 16]], 16000, 0)
-    iota(view("RSE"), [[0, H], [-256, NS_]], 256, 0)
+    iota(view("RSE"), [[0, H], [-256, SLOTS]], 256, 0)
     iota(view("RS8"), [[0, 128], [-256, 8]], 256, 0)
     iota(view("M4"), [[-1, 4]], -1, 0)
-    for v, c in ((view("FT"), -2), (view("F2"), 0), (view("RF", W, W + L), 0), (view("NS"), 0), (view("ON"), 1), (view("C3"), CAP), (view("CN", 0, 2), 0)):
+    for v, c in ((view("XF", V, W), int(BIGX)), (view("RF", W, W + L), 0), (view("ON"), 1), (view("C3"), CAP), (view("CN", 0, 2), 0)):
         gfill(v, c)
-    for v, c in ((view("XF", V, W), BIGX), (view("BF", V, W + L), 0.0), (view("LW"), 0.0), (view("LM"), 0.0), (view("WT", 16, 32), 0.5),
-                 (view("WT", 48, 64), 2.0), (view("LW", 112, 128), 512.0), (view("VL", 16, 27), float(DUMP)), (view("ZD", 0, 1), 0.0)):
+    for v, c in ((view("BF", V, W + L), 0.0), (view("LW"), 0.0), (view("LM"), 0.0), (view("FT"), -2.0), (view("F2"), 0.0),
+                 (view("WT", 16, 32), 0.5), (view("WT", 48, 64), 2.0), (view("LW", 112, 128), 512.0), (view("ZD", 0, 1), 0.0)):
         ms(v, c)
     for i, m in ((1, 15), (2, 112), (3, 16), (4, 31), (5, 1)):
         ts(pi(i), pi(0), m, A.bitwise_and)
@@ -421,7 +458,7 @@ def rank_program(g, core, T, topo):
     cp(view("KO", 0, 2), view("PI", 1, 3))
     ts(ko(5), pi(2), 15.0, A.add)
     ts(ko(2), pi(3), 1.0 / 16, A.mult)
-    ts(ko(3), pi(3), -1.0 / 16, A.mult, 1.0, A.add)
+    affine(ko(3), ko(2), -1.0, 1.0)
     cp(ko(9), pi(4))
     cp(ko(20), pi(5))
     ts(ko(6), pi(1), 10.0, A.is_lt)
@@ -431,15 +468,14 @@ def rank_program(g, core, T, topo):
     ts(view("BO"), view("IB"), ko(1), A.is_equal)
     for nm, c in (("I256", 256.0), ("NI", -1.0), ("IBG", BIGT), ("NBG", -BIGT)):
         scaled(view(nm), I, c)
-    for h in range(2):
-        mm(bank(4 + h), view("I256"), half("P", h), True, False)
-        mm(bank(4 + h), view("NI"), half("R", h), False, True)
-        ts(half("SN", h), bank(4 + h), 256.0, A.add)
-        act(half("TP", h), bank(4 + h), AF.Copy)
-    for c in range(len(PARTS) - 1):
+    for c, (lo, hi) in enumerate(zip(PARTS, PARTS[1:])):
+        mm(bank(4 + c, hi - lo), view("I256"), view("P", lo, hi), True, False)
+        mm(bank(4 + c, hi - lo), view("NI"), view("R", lo, hi), False, True)
+        ts(view("SN", lo, hi), bank(4 + c, hi - lo), 256.0, A.add)
+        act(view("TP", lo, hi), bank(4 + c, hi - lo), AF.Copy)
         sent = send(0, c)
     for k in range(8):
-        dma("y", "d%d" % (9 + k), view("SE32", 44 * k, 44 * k + 44), (T.succ[2 * k::16, :],), [sent])
+        dma("y", "d%d" % (9 + k), view("SE32", 44 * k, 44 * k + 44), (T.succ[2 * k::16, :],), LOAD + 0.3 * k, [sent])
     scan(view("WT", 0, 16), view("WT", 16, 32), view("WT", 16, 32), 1.0, A.mult, A.min)
     ts(view("YB", 0, 32), view("IO", 0, 32), 0.5, A.add)
     ts(view("YB", 32, 54), view("IO", 0, 22), 32.0, A.mult, 0.5, A.add)
@@ -460,39 +496,40 @@ def rank_program(g, core, T, topo):
         for s in range(32):
             mm(view("B%d" % (6 + h), s, H, 32), I, view("LH", 32 + 11 * h, 43 + 11 * h), False, s == 31)
         act(view("BF", H * h, H * h + H), bank(6 + h, H), AF.Copy)
-    ts(view("KO", 28, 32), view("M4"), rm(13), A.mult)
+    scaled(view("KO", 28, 32), view("M4"), rm(13))
     for r in range(4):
-        act(view("BT", r, V, 4), view("BF", r, V, 4), AF.Identity, ko(28 + r))
+        affine(view("BT", r, V, 4), view("BF", r, V, 4), 1.0, ko(28 + r))
     scan(view("WT", 64, 80), view("WT", 48, 64), view("F2", 0, 16), 0.25, A.mult, A.add)
     tt(view("WT", 80, 96), view("WT", 64, 80), view("RM"), A.mult)
     red(ko(27), view("WT", 80, 96))
     tt(ko(7), ko(27), ko(6), A.mult)
-    ts(view("KO", 22, 24), view("KO", 2, 4), 16.0 * L, A.mult)
+    scaled(view("KO", 22, 24), view("KO", 2, 4), 16.0 * L)
     for h in range(2):
         for w in range(2):
             z = 16 - 16 * (h - w)
             scaled(view("SW", 128 * (2 * h + w), 128 * (2 * h + w) + 128), view("IW", z, z + 128), ko(22 if w else 23))
-    ts(ko(13), rm(13), -1536.0, A.mult, rm(12), A.subtract)
-    ts(ko(14), rm(14), -0.5, A.mult, ko(7), A.add)
-    tt(ko(13), ko(13), ko(14), A.add)
-    for nm, c in (("ZO", WO), ("ZB", ko(7)), ("ZS", ko(13)), ("Z0", rm(0))):
+    ts(ko(13), ko(0), 12.0, A.is_ge, ko(6), A.subtract)
+    ts(ko(14), rm(13), DUMP - 1025.0, A.mult, ko(7), A.add)
+    ts(ko(32), ko(0), 12.0, A.is_ge, rm(15), A.subtract)
+    tt(ko(14), ko(14), ko(32), A.add)
+    for nm, c in (("ZO", WO), ("ZB", ko(7)), ("ZS", ko(14)), ("Z0", rm(0))):
         scaled(view(nm), view("Z1"), c)
     scaled(view("ZN"), view("Z0"), -1.0)
     tt(view("ZD", 1, 144), view("Z0", 1, 144), view("Z0", 0, 143), A.subtract)
-    ts(view("BQ"), view("BO"), rm(0), A.mult, 512.0, A.mult)
-    scaled(view("BN"), view("BO"), -1.0)
-    scaled(view("BV"), view("BO"), rm(13))
-    scaled(view("BW"), view("BV"), -1.0)
-    ts(ko(21), ko(0), -1.0, A.add, 0.5, A.mult)
-    ts(ko(21), ko(21), ko(1), A.add)
+    scaled(ko(33), rm(0), 512.0)
+    for nm, src, c in (("BQ", "BO", ko(33)), ("BN", "BO", -1.0), ("BV", "BO", rm(13)), ("BW", "BV", -1.0)):
+        scaled(view(nm), view(src), c)
+    affine(ko(21), ko(0), 0.5, -0.5)
+    affine(ko(21), ko(21), 1.0, ko(1))
     ts(view("EA", 0, 128), view("IO", 0, 128), ko(21), A.is_equal)
     ts(view("EA", 128, 256), view("IO", 0, 128), -8.0, A.add, ko(21), A.is_equal)
+    act(view("EA", 256, 384), I, AF.Copy)
     ts(ko(18), ko(4), 75.0, A.is_lt, 512.0, A.mult)
-    ts(ko(19), ko(18), -1.0, A.mult, 512.0, A.add)
-    ts(view("LM", 112, 128), view("LM", 112, 128), ko(18), A.add)
-    ts(view("LM", 128, 144), view("LM", 128, 144), ko(19), A.add)
-    ts(ko(16), rm(13), 256.0, A.mult)
-    ts(ko(15), ko(6), WB, A.mult)
+    affine(ko(19), ko(18), -1.0, 512.0)
+    affine(view("LM", 112, 128), view("LM", 112, 128), 1.0, ko(18))
+    affine(view("LM", 128, 144), view("LM", 128, 144), 1.0, ko(19))
+    scaled(ko(16), rm(13), 256.0)
+    scaled(ko(15), ko(6), WB)
     ts(ko(17), ko(26), -256.0, A.mult, rm(12), A.subtract)
     for i, (z, c) in enumerate(((16, ko(15)), (19, ko(16)), (18, ko(16)), (17, rm(13)), (13, ko(17)))):
         scaled(view("AT", 128 * i, 128 * i + 128), view("IW", z, z + 128), c)
@@ -512,19 +549,18 @@ def rank_program(g, core, T, topo):
     tt(view("YB", 176, 187), view("YB", 176, 187), view("YB", 160, 171), A.add)
     cp(view("KL", 0, 11), view("YB", 176, 187))
     ts(view("YI", 64, 86), view("YB", 128, 150), -10.5, A.add, 1.0 / 22, A.mult)
-    ts(view("YB", 192, 214), view("YB", 128, 150), 16.0 * NS_, A.mult, NS_ - 1.0, A.add)
-    ts(view("YB", 224, 246), view("YI", 64, 86), -351.0 * NS_, A.mult)
+    affine(view("YB", 192, 214), view("YB", 128, 150), 16.0 * SLOTS, SLOTS - 1.0)
+    ts(view("YB", 224, 246), view("YI", 64, 86), -351.0 * SLOTS, A.mult)
     tt(view("YB", 224, 246), view("YB", 224, 246), view("YB", 192, 214), A.add)
     cp(view("PL"), view("YB", 224, 246))
-    ts(ko(25), ko(0), 1.0 / 16, A.mult)
-    ts(view("KC"), view("IO"), 0.0, A.mult, ko(25), A.add)
-    cp(view("LC"), view("YB", 128, 140))
-    cp(view("VL", 0, 11), view("YB", 128, 139))
-    ts(view("FP", 0, 42), view("IO", 0, 42), 16.0, A.mult, ko(0), A.add)
+    scaled(ko(25), ko(0), 1.0 / 16)
+    affine(view("KC"), view("IO"), 0.0, ko(25))
+    act(view("LC"), view("YB", 128, 140), AF.Copy)
+    affine(view("FP", 0, 42), view("IO", 0, 42), 16.0, ko(0))
     for h in range(2):
-        ts(view("FT", 16 * h + 12, 192, 32), view("IO", 0, 192, 32), ko(9), A.add)
+        affine(view("FT", 16 * h + 12, 192, 32), view("IO", 0, 192, 32), 1.0, ko(9))
     for i in (13, 14, 15):
-        ms(view("FT", i, 192, 16), 1.0)
+        affine(view("FT", i, 192, 16), view("IO", 0, 12), 0.0, 1.0)
     ts(view("E8", 0, 256, 1, 0, 8), view("I8", 0, 256, 1, 0, 8), 0.0, A.is_equal)
     ts(view("MI", 4, 5, 1, 0, 8), view("T8", 0, 1, 1, 0, 8), 4080, A.bitwise_and)
     ts(view("MI", 5, 6, 1, 0, 8), view("T8", 0, 1, 1, 0, 8), 15, A.bitwise_and)
@@ -536,15 +572,17 @@ def rank_program(g, core, T, topo):
         ts(view("THR", h, 12, 2), view("IO", 0, 6), 0.0, A.mult, bank(1, 1, h), A.add)
     ts(view("TT", 0, 12), view("THR", 0, 12), 4096.0, A.min)
     turned(0, "CI")
+    at("")
     fourfold("XV0", "XM", 0, cp)
     fourfold("RV0", "R", 0, gcopy)
     fourfold("PV0", "P", 0, gcopy)
     ms(view("XM", 0, V, 4), BIGX)
     cp(view("XF", 0, V), view("XM"))
-    cp(view("CF"), view("CI"))
-    ts(view("SF"), view("SI"), ko(20), A.mult)
     for r in range(2):
         cp(view("SE", L * r, L * r + L), view("SE32", r, H, 2))
+    at("lists")
+    cp(view("CF"), view("CI"))
+    ts(view("SF"), view("SI"), ko(20), A.mult)
     distances(0)
 
     for t in range(RO):
@@ -555,76 +593,89 @@ def rank_program(g, core, T, topo):
         pv, rv, xv = "PV%d" % par, "RV%d" % par, "XV%d" % par
         for c in range(len(PARTS) - 1):
             for b in (near, far):
-                lo, hi = G * b + PARTS[c], G * b + PARTS[c + 1]
-                lu, pf, pb = view("LU%d" % par, lo, hi), view("PF", V + lo, V + hi), bank(4 + 2 * (c % 2) + (b != near), hi - lo)
-                ts(pf, lu, MAGIC - 128.0, A.add, MAGIC, A.subtract)
-                ts(pf, pf, 0.0, A.max, 1.0 / 256, A.mult)
-                mm(pb, view("I256"), pf, True, True)
-                ts(view("T32", lo, hi), lu, -256.0, A.add)
-                tt(view("RF", V + lo, V + hi), pb, view("T32", lo, hi), A.subtract)
-        for k in range(0, 16, 4):
-            tt(ent("A1", k, k + 4), ind(rf, ck(t, k, k + 4)), view(pv), A.is_le)
-            key_add("ZO", "A1", k, k + 4)
-        for k in range(0, PS_, 4):
-            act(ent("GP", k, min(k + 4, PS_)), ind(view("PF"), ck(t, k, min(k + 4, PS_))), AF.Copy)
-        for k in range(0, 16, 2):
-            if k < PS_:
+                lo, hi, i = G * b + PARTS[c], G * b + PARTS[c + 1], 2 * c + (b != near)
+                lu, pf, pb = view("LU%d" % par, lo, hi), view("PF", V + lo, V + hi), bank(4 + i, hi - lo)
+                at("round%d" % i); ts(pf, lu, MAGIC - 128.0, A.add, MAGIC, A.subtract)
+                at("past%d" % i); ts(pf, pf, 0.0, A.max, 1.0 / 256, A.mult)
+                at("off"); mm(pb, view("I256"), view("ON", 0, hi - lo), True, False)
+                at("past%d" % i); mm(pb, view("I256"), pf, False, True)
+                at("reach%d" % i); tt(view("RF", V + lo, V + hi), pb, lu, A.subtract)
+        for i, (k0, k1) in enumerate(zip(RUNS_R, RUNS_R[1:])):
+            at("r%d" % i)
+            tt(ent("A1", k0, k1), ind(rf, ck(t, k0, k1)), view(pv, 0, L * (k1 - k0)), A.is_le)
+            key_add("ZO", "A1", k0, min(k1, 15))
+        for i, (k0, k1) in enumerate(zip(RUNS_P, RUNS_P[1:])):
+            at("g%d" % i)
+            act(ent("GP", k0, k1), ind(view("PF"), ck(t, k0, k1)), AF.Copy)
+            for k in range(k0, k1, 2):
                 b = (2, 3, 6, 7)[k // 2 % 4]
-                diff("GP", rv, k, b)
-                act(ent("A2", k, k + 2), bank(b, H), AF.Relu, 1.0)
-            else:
-                tt(ent("A2", k, k + 2), ind(view("PF"), ck(t, k, k + 2)), view(rv, 0, H), A.is_ge)
-            key_add("ZO", "A2", k, k + 2)
-        mm(bank(0, 16, L), I, view("KC", L, 192), False, True)
+                at("g%d" % i); diff("GP", rv, k, b)
+                at("p%d" % i); act(ent("A2", k, k + 2), bank(b, H), AF.Relu, 1.0)
+                key_add("ZO", "A2", k, k + 2)
+        at("pv")
+        k = RUNS_P[-1]
+        tt(ent("A2", k, 16), ind(view("PF"), ck(t, k, 16)), view(rv, 0, L * (16 - k)), A.is_ge)
+        key_add("ZO", "A2", k, 16)
+        at("key"); mm(bank(0, L), zq("ZO", 15), ent("A1", 15, 16), False, True)
+        at("")
         gcopy(view("SV"), actv("SF"))
-        gcopy(view("CV"), actv("CF"))
-        if t:
-            mm(bank(2, L), view("BW"), actv("BF"), True, True)
-            scaled(view("NS"), bank(2, L), 512.0)
+        at("cv"); gcopy(view("CV"), actv("CF"))
+        at("gone")
+        mm(bank(2, L), view("BW"), actv("BF"), True, True)
+        scaled(view("NS"), bank(2, L), 512.0)
         if not last:
+            at("")
             for nm, src in (("XV", "XM"), ("PV", "P"), ("RV", "R")):
                 fourfold("%s%d" % (nm, 1 - par), src, t + 1, gcopy)
             turned(t + 1, "CF")
         ks = view("KS", 15, 192, 16)
-        tr(view("KT"), bank(0, 192))
-        ts(view("OM"), bank(0, L), WO, A.is_ge, 1000.0, A.mult)
-        scan(view("KS"), view("RK"), view("KT"), 0.0, A.max, A.min)
-        ts(view("DI", 0, 12), ks, -0.47, A.add)
-        tt(view("K6", 0, 12), ks, view("DI", 0, 12), A.subtract)
+        at("key"); tr(view("KT"), bank(0, 192))
+        at("ordered"); ts(view("OM"), bank(0, L), WO, A.is_ge, 1000.0, A.mult)
+        at("least"); scan(view("KS"), view("RK"), view("KT"), 0.0, A.max, A.min)
+        at("d"); ts(view("DI", 0, 12), ks, -0.47, A.add)
+        at("k"); tt(view("K6", 0, 12), ks, view("DI", 0, 12), A.subtract)
+        at("chosen")
         mm(bank(1, 12), I, view("LC"), True, False)
         for w in range(2):
             for h in range(2):
                 j = 128 * (2 * h + w)
                 mm(view("B1", w, 12, 2), view("SW", j, j + 128), view("K6", h, 12, 2), False, w == 1 and h == 1)
         cp(view("LS", 0, 11), bank(1, 11))
-        cp(view("FT", 10, 192, 16), view("DI", 0, 12))
-        tt(view("FT", 11, 192, 16), view("DI", 0, 12), view("FT", 10, 192, 16), A.subtract)
-        tr(view("FR"), view("FT"))
+        at("dhi"); cp(view("FT", 10, 192, 16), view("DI", 0, 12))
+        at("dlo"); tt(view("FT", 11, 192, 16), view("DI", 0, 12), view("FT", 10, 192, 16), A.subtract)
+        at("fr"); tr(view("FR"), view("FT"))
+        at("asks")
         tt(view("NA", 0, 12), ks, view("TT", 0, 12), A.is_ge)
         ts(view("NA", 16, 28), ks, 4096.0, A.is_ge, 2.0, A.mult)
-        tt(view("F2", 0, 192, 16), view("NA", 0, 12), view("NA", 16, 28), A.add)
-        tr(view("G2"), view("F2"))
-        tt(view("FE"), ind(view("BC"), view("LS", 0, 11)), view("FR", 0, L), A.max)
+        at("f2"); tt(view("F2", 0, 192, 16), view("NA", 0, 12), view("NA", 16, 28), A.add)
+        at("gt"); tr(view("G2"), view("F2"))
+        at("fe"); tt(view("FE"), ind(view("BC"), view("LS", 0, 11)), view("FR", 0, L), A.max)
+        at("le")
         mm(bank(6, L), view("AE", 0, 128), view("FE"), True, True)
         mm(bank(7, L), view("AE", 128, 256), view("FE"), True, True)
-        cp(view("LE", 0, L), bank(6, L))
-        act(view("LE", L, 2 * L), bank(7, L), AF.Copy)
+        act(view("LE", 0, L), bank(6, L), AF.Copy)
+        cp(view("LE", L, 2 * L), bank(7, L))
+        at("b")
         listed(bank(1, 11), "ZB", "FE", 0, L)
         ts(bl, bank(1, 11), 511.5, A.add)
-        tt(view("MN"), ind(view("R"), bl), view(rv, 0, L), A.min)
-        tt(view("DS"), ind(view("SF"), bl), view("SV"), A.subtract)
+        ts(view("NA", 32, 43), bank(1, 11), 511.5, A.add)
+        at("mn"); tt(view("MN"), ind(view("R"), bl), view(rv, 0, L), A.min)
+        at("ds"); tt(view("DS"), ind(view("SF"), bl), view("SV"), A.subtract)
+        at("fd"); ts(view("FD"), view("FE"), ko(13), A.mult, ko(6), A.add)
+        at("ns"); tt(view("NS"), view("NS"), view("MN"), A.add)
+        at("pairs")
         done = {}
-        for i in range(12):
+        for i in (8, 10, 0, 1, 2, 3, 4, 5, 6, 7, 9, 11):
             a, j = TILES[i]
             c = (0, 117, 234)[j]
             done[i] = mm(view("B%d" % (2 + i // 2), L * (i % 2), L * (i % 2) + L, 1, 0, 118), view("LE", c, c + 118, 1, 32 * a, 32 * a + 32),
                          view("FE", 0, L, 1, 32 * a, 32 * a + 32), True, True, [done[i - 1]] if i in (9, 11) else [])
-        mm(bank(0, L), view("BQ"), view("G2", 0, L), True, False)
-        mm(bank(0, L), I, view("MN"), False, False)
+        at("gt"); mm(bank(0, L), view("BQ"), view("G2", 0, L), True, False)
         for b in range(6):
+            at("y%d" % b)
             y = view("YP", H * b, H * b + H, 1, 0, 118)
             i = view("B%d" % (2 + b), 0, H, 1, 0, 118)
-            if b % 2 == 1:
+            if b % 2 == 0:
                 ts(y, i, 10 * WB, A.is_gt)
             else:
                 act(y, i, AF.Relu, -10 * WB)
@@ -637,105 +688,130 @@ def rank_program(g, core, T, topo):
                     l = view("LW", k, k + 128, 1, 0, 118)
                 mm(bank(0, L), l, view("YP", L * i, L * i + L, 1, 0, 118), False, i == 11)
         wn, hm = bank(0, L, 256), bank(7, L)
-        mm(bank(1, 11), I, view("VL", 0, 11), True, False)
-        mm(bank(1, 11), I, view("VL", 16, 27), False, False)
-        ts(wn, bank(0, L), 512.0, A.is_lt)
-        tt(view("FW"), view("FE"), wn, A.mult)
+        at("fw")
+        mm(bank(1, 11), view("EA", 256, 384), view("NA", 32, 43), True, False)
+        tt(view("FW"), bank(0, L), view("FD"), A.min)
         listed(bank(1, 11), "ZS", "FW", 0, L, False)
-        cp(view("SC", 0, 11), bank(1, 11))
-        tt(view("QQ"), bank(0, L), view("NS"), A.add)
-        tt(actv("RF"), actv("RF"), view("QQ"), A.min)
-        cp(ind(view("RF"), view("SC", 0, 11)), view("MN"))
-        tt(view("DS"), view("DS"), wn, A.mult)
+        at("sc"); cp(view("SC", 0, 11), bank(1, 11))
+        at("qq"); tt(view("QQ"), bank(0, L), view("NS"), A.add)
+        at("wn"); ts(wn, bank(0, L), 0.5, A.is_lt)
+        at("own"); tt(actv("RF"), actv("RF"), view("QQ"), A.min)
+        at("put"); cp(ind(view("RF"), view("SC", 0, 11)), view("MN"))
+        at("dsw"); tt(view("DS"), view("DS"), wn, A.mult)
+        at("so")
         mm(bank(6, L), view("EA", 128 * (o // 2), 128 * (o // 2) + 128), view("SF", o, V, 4), True, False)
         mm(bank(6, L), view("EA", 128 * (t // 2), 128 * (t // 2) + 128), view("SV"), False, False)
         mm(bank(6, L), view("EA", 128 * (t // 2), 128 * (t // 2) + 128), view("DS"), False, True)
         cp(view("SO"), bank(6, L))
         if not last:
-            sig([("BO", "R"), ("BV", "BF"), ("BN", "P")], True, False)
-            tt(actv("SF"), view("SV"), view("DS"), A.add)
+            at("oldr"); sig("BO", "R", True)
+            at("old"); sig("BV", "BF")
+            at("oldp"); sig("BN", "P")
+            at("sf"); tt(actv("SF"), actv("SF"), view("DS"), A.add)
+            at("mx")
             act(view("MX"), ind(view("P"), bl), AF.Copy)
             tt(view("MX"), view("MX"), wn, A.mult)
-            tt(actv("P"), actv("P"), view("MX"), A.max)
-            cp(ind(view("BF"), view("SC", 0, 11)), actv("BT"))
-            red(view("MC", 0, 1), wn)
-        tt(actv("R"), bank(0, L), actv("R"), A.min)
-        act(view("XB"), ind(view("XM"), bl), AF.Copy)
+            at("pnew"); tt(actv("P"), actv("P"), view("MX"), A.max)
+            at("name"); cp(ind(view("BF"), view("SC", 0, 11)), actv("BT"))
+            at("mc"); red(view("MC", 0, 1), wn)
+        at("q1"); tt(view("FD"), bank(0, L), view("MN"), A.add)
+        at("rnew"); tt(actv("R"), view("FD"), actv("R"), A.min)
+        at("xb"); act(view("XB"), ind(view("XM"), bl), AF.Copy)
+        at("xh")
         mm(hm, I, view("XB"), True, False)
         mm(hm, I, view(xv, 0, L), False, True)
-        act(view("XH"), hm, AF.Identity, WHOLE, 0.4995)
-        act(view("XB"), view("XH"), AF.Identity, -WHOLE)
+        affine(view("XH"), hm, 0.4995, WHOLE)
+        affine(view("XB"), view("XH"), 1.0, -WHOLE)
+        at("dx")
         mm(hm, I, view("XB"), True, False)
         mm(hm, view("NI"), view(xv, 0, L), False, True)
         act(view("DX"), hm, AF.Copy)
         tt(view("DX"), view("DX"), wn, A.mult)
+        at("xm")
         mm(hm, I, view("DX"), True, False)
         mm(hm, I, view(xv, 0, L), False, True)
         act(actv("XM"), hm, AF.Copy)
-        mm(hm, view("BQ"), view("G2", 0, L), True, True)
-        tt(view("DC"), ind(view("CF"), bl), view("CV"), A.subtract)
-        tt(hm, view("OM"), hm, A.is_gt)
-        tt(hm, view("DC"), hm, A.mult)
-        tt(actv("CF"), view("CV"), hm, A.add)
+        hm = bank(6, L)
+        at("hm"); mm(hm, view("BQ"), view("G2", 0, L), True, True)
+        at("dc"); tt(view("DC"), ind(view("CF"), bl), view("CV"), A.subtract)
+        at("hm"); tt(hm, view("OM"), hm, A.is_gt)
+        at("dcm"); tt(hm, view("DC"), hm, A.mult)
+        at("cf"); tt(actv("CF"), view("CV"), hm, A.add)
         se = lambda k: view("SE", L * par + 22 * k, L * par + 22 * k + 22)
-        slot = lambda i: view("GE", i, NS_ * H, NS_)
-        for k in range(MV, 8):
-            act(slot(k - MV), ind(rf, se(k)), AF.Copy)
-        ac = lambda k: view("AC", H * (k % 4), H * (k % 4) + H) if k < MV - CHAINS else slot(8 - 2 * MV + CHAINS + k)
-        for k in range(MV):
-            if k < CHAINS:
-                cp(ac(k), ind(rf, se(k)))
+        for k in range(SLOTS):
+            at("e%d" % k)
+            ac = view("AC", H * k, H * k + H)
+            if last and k == 0:
+                cp(ac, ind(rf, se(SLOTS + k)))
             else:
-                tt(ac(k), ind(rf, se(k)), ac(k - CHAINS), A.min)
-        scan(view("GF"), view("RSE"), view("GE"), 0.0, A.max, A.min)
+                act(ac, ind(rf, se(SLOTS + k)), AF.Copy)
+            tt(view("GE", k, SLOTS * H, SLOTS), ind(rf, se(k)), ac, A.min)
+        at("gf"); scan(view("GF"), view("RSE"), view("GE"), 0.0, A.max, A.min)
         rp = view("R", par, V, 2)
-        tt(rp, ind(view("GF"), view("PL")), rp, A.min)
-        for lo, hi in zip(CUTS, CUTS[1:]):
+        at("even"); tt(rp, ind(view("GF"), view("PL")), rp, A.min)
+        for i, (lo, hi) in enumerate(zip(CUTS, CUTS[1:])):
+            at("o%d" % i)
             act(view("GA", 16 * lo, 16 * hi), ind(rf, view("SO", lo, hi)), AF.Copy)
             scan(view("GS", 16 * lo, 16 * hi), view("RS8", 0, 16 * (hi - lo)), view("GA", 16 * lo, 16 * hi), 0.0, A.max, A.min)
             z = view("R", par + 4 * lo, 4 * hi, 2)
-            tt(z, view("GS", 16 * lo + 7, 16 * hi, 8), z, A.min)
+            at("low%d" % i); tt(z, view("GS", 16 * lo + 7, 16 * hi, 8), z, A.min)
         if last:
             dma("y", "d7", (T.yx[:],), view("XM"))
-            dma("s", "d8", (T.yc[:],), view("CF"))
+            dma("y", "d8", (T.yc[:],), view("CF"))
             dma("y", "d6", (T.yr[:, 0:4 * CUTS[2]],), view("R", 0, 4 * CUTS[2]))
-            dma("s", "d19", (T.yr[:, 4 * CUTS[2]:V],), view("R", 4 * CUTS[2], V))
+            dma("y", "d19", (T.yr[:, 4 * CUTS[2]:V],), view("R", 4 * CUTS[2], V))
             break
+        at("fl")
         listed(bank(1, 44), "ZB", "BF", 0, V)
         ts(view("FL"), bank(1, 44), 511.5, A.add)
-        act(view("DT", 0, 44), bank(1, 44), AF.Identity, 511.5)
-        sig([("BW", "BF"), ("BO", "P"), ("BN", "R")], False, True)
-        ts(half("CH", 0), bank(2), 0.5, A.is_gt)
-        act(half("CH", 1), bank(3), AF.Sign)
-        scan(half("CN", 0, 2), half("CH", 0), view("C3"), 0.0, A.add, A.min)
-        scan(half("CN", 1, 2), half("CH", 1), view("C3"), view("CN", 337, 338), A.add, A.min)
+        at("ff"); ts(view("DT", 0, 44), bank(1, 44), 511.5, A.add)
+        at("new"); sig("BW", "BF"); sig("BO", "P")
         for h in range(2):
-            for i, (z, r) in enumerate((("I256", half("P", h)), ("NBG", view("ON")), ("NI", half("R", h)), ("IBG", half("CN", h, 2)),
+            at("ch%d" % h)
+            mm(bank(2 + h), view("BN"), half("R", h), False, True)
+            if h:
+                act(half("CH", h), bank(2 + h), AF.Sign)
+            else:
+                ts(half("CH", h), bank(2 + h), 0.5, A.is_gt)
+        at("cn0"); scan(half("CN", 0, 2), half("CH", 0), view("C3"), 0.0, A.add, A.min)
+        at("cn1"); scan(half("CN", 1, 2), half("CH", 1), view("C3"), view("CN", 337, 338), A.add, A.min)
+        for h in range(2):
+            at("tp%d" % h)
+            for i, (z, r) in enumerate((("I256", half("P", h)), ("NBG", view("ON", 0, 336)), ("NI", half("R", h)), ("IBG", half("CN", h, 2)),
                                         ("NBG", half("CN", h, 1)))):
                 mm(bank(4 + h), view(z), r, i == 0, i == 4)
             tt(half("TP", h), bank(4 + h), half("TP", h), A.max)
+        at("go")
         for q in range(16):
             mm(bank(1, 42), zq("ZD" if q < 15 else "Z0", q), view("CN", 2 + q, G + 2, 16), q == 0, False)
         mm(bank(1, 41, 1), zq("ZN", 0), view("CN", 17, G - 14 + 2, 16), False, True)
+        at("df")
         tt(view("DT", 44, 86), view("DT", 0, 42), view("FP", 0, 42), A.subtract)
         ts(view("DT", 88, 130), view("DT", 0, 42), float(G), A.is_lt)
-        tt(view("DT", 44, 86), view("DT", 44, 86), view("DT", 88, 130), A.mult)
-        tt(view("DT", 132, 174), bank(1, 42), view("DT", 44, 86), A.mult)
-        tt(view("FP", 0, 42), view("FP", 0, 42), view("DT", 132, 174), A.add)
-        cp(view("FU", 0, 42), view("FP", 0, 42))
+        at("dfm"); tt(view("DT", 44, 86), view("DT", 44, 86), view("DT", 88, 130), A.mult)
+        at("go"); tt(view("DT", 132, 174), bank(1, 42), view("DT", 44, 86), A.mult)
+        at("fp"); tt(view("FP", 0, 42), view("FP", 0, 42), view("DT", 132, 174), A.add)
+        at("fu"); cp(view("FU", 0, 42), view("FP", 0, 42))
+        at("send")
         for c, (lo, hi) in enumerate(zip(PARTS, PARTS[1:])):
             ts(view("SN", lo, hi), ind(view("TP"), view("FU", lo // 16, hi // 16)), 256.0, A.add)
             send(t + 1, c)
-        gfill(view("XM", t + 1, V, 4), int(BIGX))
+        at(""); gfill(view("XM", t + 1, V, 4), int(BIGX))
         for dst, src in (("PF", "P"), ("XF", "XM"), ("RF", "R")):
-            act(view(dst, 0, V), ind(view(src), view("FL")), AF.Copy)
+            at(dst); act(view(dst, 0, V), ind(view(src), view("FL")), AF.Copy)
+        at("m0")
         ts(view("MB", 0, 1), view("MC", 0, 1), 1.0 / 16, A.mult)
         mm(bank(1, 1), view("ON", 0, 128), view("MB", 0, 1), True, True)
-        cp(view("MI", 0, 1), bank(1, 1))
-        ts(view("MI", 1, 2), view("MI", 0, 1), 31, A.bitwise_and)
-        cp(view("MC", 1, 2), view("MI", 1, 2))
-        ts(view("TT", 0, 12), view("THR", 0, 12), view("MC", 1, 2), A.add, 4096.0, A.min)
+        at("m1"); cp(view("MI", 0, 1), bank(1, 1))
+        at("m2"); ts(view("MI", 1, 2), view("MI", 0, 1), 31, A.bitwise_and)
+        at("m3"); cp(view("MC", 1, 2), view("MI", 1, 2))
+        at("m4"); ts(view("TT", 0, 12), view("THR", 0, 12), view("MC", 1, 2), A.add, 4096.0, A.min)
         distances(t + 1)
+    for i in named["v", -1, "lists"]:
+        follow([i, named["v", 0, "round0"][0]])
+    for e in LINES:
+        follow([i for t in range(-1, RO) for w in (LAST if t == RO - 1 else LINES)[e].split()
+                for i in named.get((e, t + (w[0] == "+") - (w[0] == "-"), w.lstrip("+-")), [])])
     for call in order():
         call()
     finish()

from concourse.bass import DstId, RemoteDMATransfer
from concourse.mybir import AluOpType as A, AxisListType, ActivationFunctionType as AF
import math

V, G, W, CAP, RO = 704, 672, 2048, 112, 4
L = V // 4
H = V // 2
NE = 16 * L
DUMP = W
SLOTS = 4
XV_ = 3
RUNS_R = (0, 4, 8, 12, 14, 16)
RUNS_P = (0, 4, 8, 12)
CUTS = (0, 64, 128, 152, 168, L)
PARTS = (0, 352, G)
BIGX = 512.0
WO = 16384.0
WB = 1048576.0
BIGT = 114688.0
WHOLE = 1.5 * 2.0 ** 23
MAGIC = 2.0 ** 31
TILES = [(0, 0), (0, 1), (1, 0), (1, 1), (2, 0), (2, 1), (3, 0), (3, 1), (0, 2), (1, 2), (2, 2), (3, 2)]

_UNPACK = "round0 -m2 past0 round2 -m3 past2 round1 reach0 past1 round3 reach2 past3 -m4 reach1 reach3 "
_MERGE = ("pv r0 r1 r2 r3 r4 key ordered least d asks dhi k f2 dlo gt fr chosen fe -sf fd le b mn y0 y2 y4 ds ns "
          "fw qq wn own dsw sc q1 put ")
_LOW = "gf o0 even o1 low0 o2 low1 o3 low2 "
_TESTS = "g0 g1 p0 g2 p1 p2 n2 n3 gone le "
_RIVALS = "off past0 past2 past1 past3 a1 a2 le b pairs y0 y1 y2 y3 y4 y5 xh fw "
LINES = {"v": _UNPACK + _MERGE + "mx rnew name e0 so dx e1 pnew e2 e3 " + _LOW + "fl low3 ff ch0 df dc cn0 o4 dfm cn1 low4 hm turn tp0 ck go dcm "
              "fp tp1 fu cf send +x0 mc +x1 m0 +x2 m1",
         "s": _TESTS + "twice y1 y3 y5 xb mx xh dx e0 e1 e2 e3 o0 o1 o2 o3 o4 xm ch1 XF PF +x3 +n0 +a3 +x0 +n1 +x1 RF +x2",
         "p": _RIVALS + "oldr old dx oldp so",
         "g": "send +cv"}
LAST = {"v": _UNPACK + _MERGE + "rnew dc e0 so e1 hm dcm e2 cf dx e3 " + _LOW + "o4 low3 low4",
        "s": _TESTS + "y1 y3 y5 xb xh e1 dx e2 e3 o0 xm o1 o2 o3 o4",
        "p": _RIVALS + "so dx",
        "g": ""}

MATS = ["NI", "I256", "IBG", "NBG", "BO", "BN", "BW", "BV", "BQ"]
SCRATCH = {}


def _declare():
    bf = [("XM", V), ("R", V), ("P", V), ("RF", W + L), ("PF", W), ("XF", W), ("BF", W + L), ("BT", V), ("LH", 64),
          ("RV0", V), ("RV1", V), ("PV0", V), ("PV1", V), ("XV0", V), ("XV1", V), ("GX", NE), ("AX", NE), ("A1", NE), ("A2", NE), ("GP", NE),
          ("BC", NE), ("GA", NE), ("GS", NE), ("GE", SLOTS * H), ("GF", SLOTS * H), ("AC", SLOTS * H), ("RS8", 1024), ("RSE", SLOTS * H),
          ("E8", 256), ("IW", 160), ("MAT", 128 * len(MATS)), ("Z1", 144), ("ZO", 144), ("Z0", 144), ("ZN", 144), ("ZD", 144),
          ("ZB", 144), ("ZS", 144), ("SW", 512), ("AE", 256), ("AT", 640),
          ("LW", 240), ("LM", 256), ("ON", H), ("KC", 192), ("LC", 12), ("C3", 336), ("K6", 16), ("FT", 192), ("FR", 192),
          ("F2", 192), ("G2", 192), ("FE", L), ("FW", L), ("FD", L), ("LE", 2 * L), ("YP", 12 * L), ("MN", L), ("MX", L), ("DX", L), ("XB", L),
          ("OM", L), ("NS", L), ("QQ", L), ("CH", G), ("CN", G + 16), ("MB", 8), ("M4", 4)]
    f4 = [("CF", V), ("SF", V), ("IO", 192), ("IB", 128), ("I8", 256), ("KO", 40), ("RM", 16), ("WT", 96), ("RK", 192), ("KT", 192), ("KS", 192),
          ("NA", 48), ("THR", 16), ("TT", 16), ("DS", L), ("DC", L), ("XH", L), ("SV", L), ("CV", L), ("DT", 176), ("MC", 4), ("TP", G),
          ("Y", H), ("YT", H), ("EA", 384), ("FP", 44), ("YB", 256)]
    i4 = [("CI", V), ("SI", V), ("SE32", H), ("T8", 2), ("PI", 8), ("YI", 96), ("DI", 16), ("MI", 8)]
    u2 = [("CK0", L), ("CK1", L), ("SE", H), ("SO", L), ("DL", 88), ("KL", 12), ("PL", 22), ("LS", 16), ("BL", 16), ("SC", 16), ("FL", 44),
          ("FU", 44), ("SN", G), ("LU0", 2 * G), ("LU1", 2 * G)]
    for lst, d in ((bf, "bfloat16"), (f4, "float32"), (i4, "int32"), (u2, "uint16")):
        for nm, w in lst:
            SCRATCH[nm] = ("sbuf", [128, w], d)
    for b in range(8):
        SCRATCH["B%d" % b] = ("psum", [128, 512], "float32")


_declare()
SEMAPHORES = (["s_v", "s_s", "s_p", "s_g"] + ["d%d" % i for i in range(22)] + ["lo%d%d" % (i, c) for i in range(RO) for c in range(len(PARTS) - 1)]
              + ["ar%d%d%d" % (i, c, b) for i in range(RO) for c in range(len(PARTS) - 1) for b in range(2)])


def meet(a, b):
    return a[0] < b[1] and b[0] < a[1] and (a[0] - b[0]) % math.gcd(a[2], b[2]) == 0


def covers(a, b):
    return a[0] <= b[0] and b[1] <= a[1] and (a[2] == 1 or (a[2] == b[2] and (a[0] - b[0]) % a[2] == 0))


def tracker(g, T):
    eng = {"v": g.vector, "s": g.scalar, "p": g.tensor, "g": g, "y": g.sync}
    known = {e: {} for e in eng}
    cnt = {e: 0 for e in eng}
    recs = {}
    total = {}

    def need(e, rec):
        sem, val, clock, _ = rec
        if known[e].get(sem, 0) < val:
            eng[e].wait_ge(T.sem[sem], val)
            for k, x in clock.items():
                if known[e].get(k, 0) < x:
                    known[e][k] = x

    def depend(e, outs, ins):
        deps = []
        for (lst, wr) in ((ins, False), (outs, True)):
            for v in lst:
                for (name, lo, hi, st) in v[1]:
                    bank = SCRATCH[name][0] == "psum"
                    for (fp, w, rec) in recs.get(name, []):
                        if bank and rec[3] != e:
                            deps.append(rec)
                        elif (e != "p" or not bank) and (wr or w) and meet(fp, (lo, hi, st)):
                            deps.append(rec)
        deps.sort(key=lambda r: -r[1])
        for r in deps:
            need(e, r)

    def note(rec, outs, ins):
        for (lst, wr) in ((ins, False), (outs, True)):
            for v in lst:
                for (name, lo, hi, st) in v[1]:
                    old = recs.get(name, [])
                    if SCRATCH[name][0] == "psum":
                        old = [r for r in old if r[2][3] == rec[3] != "p"]
                    fp = (lo, hi, st)
                    if wr:
                        old = [r for r in old if not covers(fp, r[0])]
                    else:
                        old = [r for r in old if not (not r[1] and covers(fp, r[0]) and r[2][3] == rec[3] and rec[3] is not None)]
                    recs[name] = old + [(fp, wr, rec)]

    def issue(e, sem, val, outs, ins, call):
        if call is None:
            rec = (sem, val, {sem: val}, None)
        else:
            depend(e, outs, ins)
            if sem is None:
                cnt[e] += 1
                call().then_inc(T.sem["s_" + e], 1)
                rec = ("s_" + e, cnt[e], dict(known[e]), e)
            else:
                call()
                rec = (sem, val, dict(known[e]), None)
            rec[2][rec[0]] = rec[1]
        total[rec[0]] = rec[1]
        note(rec, outs, ins)
        return rec

    def finish():
        for k in sorted(total):
            if known["y"].get(k, 0) < total[k]:
                g.sync.wait_ge(T.sem[k], total[k])
    return issue, need, finish


CYCLE, PE_CYCLE, HOP, GATHER, SCATTER = 0.0009, 0.00045, 0.18, 1.56, 3.8
LOAD, BYTE, CALL, FIRST, NEAR, FAR = 1.7, 0.00057, 0.6, 3.5, 3.0, 4.0
SLACK = {"v": 0.1, "s": 0.06, "p": 0.02, "g": 0.0, "y": 0.0, "n": 0.0}
ORDER = []


def count(v): return 16 * len(range(*v[1][1][1:])) if len(v[1]) > 1 else len(range(*v[1][0][1:]))


def price(e, out, ins, both):
    kinds = [SCRATCH[v[1][0][0]] for v in [out] + ins if count(v) > 1]
    n = max(count(v) for v in [out] + ins)
    if e == "p":
        return PE_CYCLE * max(64, count(ins[1])) * (4 if SCRATCH[ins[1][1][0][0]][2] == "float32" else 1)
    if e == "g":
        return 0.17 + 2 * CYCLE * n
    if len(out[1]) > 1:
        return 0.05 + SCATTER * CYCLE * n
    if any(len(v[1]) > 1 for v in ins):
        return 0.06 + GATHER * CYCLE * n
    if e == "s":
        return 0.05 + CYCLE * max(64, n)
    if both:
        return CYCLE * max(64, n * (1 if any(k[0] == "psum" for k in kinds) else 2))
    return CYCLE * max(64, n * (0.5 if all(k[2] in ("bfloat16", "uint16") for k in kinds) else 1))


def planner():
    nodes, recs, runs = [], {}, {}

    def add(e, cost, tail, outs, ins, call, after, middle):
        me, before = len(nodes), dict(after)
        for (lst, wr) in ((ins, False), (outs, True)):
            for v in lst:
                for (name, lo, hi, st) in v[1]:
                    fp, old = (lo, hi, st), recs.get(name, [])
                    if SCRATCH[name][0] == "psum":
                        run = runs.setdefault(name, [e, []])
                        if run[0] != e:
                            run[0], run[1], old = e, [r[2] for r in old], []
                        before.update({a: HOP for a in run[1]})
                        if e == "p":
                            before.update({r[2]: before.get(r[2], 0.0) for r in old if not (middle and r[1])})
                            recs[name] = (old if middle else []) + [(fp, middle, me)]
                            continue
                    before.update({r[2]: HOP for r in old if (wr or r[1]) and r[2] != me and meet(r[0], fp)})
                    keep = SCRATCH[name][0] == "psum" or not wr
                    recs[name] = [r for r in old if keep or not covers(fp, r[0])] + [(fp, wr, me)]
        nodes.append((e, cost, tail, before, call))
        return me

    def follow(calls):
        for a, b in zip(calls, calls[1:]):
            nodes[b][3].setdefault(a, -nodes[a][2])

    def place(rank, before):
        later = [[] for _ in nodes]
        for i, b in enumerate(before):
            for a in b:
                later[a].append(i)
        left = [len(b) for b in before]
        start, can, free, ready = [0.0] * len(nodes), [0.0] * len(nodes), {}, {}
        for i, x in enumerate(left):
            free[nodes[i][0]] = 0.0
            ready.setdefault(nodes[i][0], set())
            if x == 0:
                ready[nodes[i][0]].add(i)

        def ahead(now, end, skip):
            when = {z: max(can[z], free[q], now) for q in ready for z in ready[q] if can[z] < end and z != skip}
            seen, stack = {}, list(when)
            while stack:
                z = stack.pop()
                for j in later[z]:
                    k, x = seen.get(j, (0, can[j]))
                    seen[j] = (k + 1, max(x, when[z] + nodes[z][1] + before[j][z]))
                    if seen[j][0] == left[j] and seen[j][1] < end:
                        when[j] = seen[j][1]
                        stack.append(j)
            return when
        todo = len(nodes)
        while todo:
            e = min((q for q in ready if ready[q]), key=lambda q: max(free[q], min(can[z] for z in ready[q])))
            now = max(free[e], min(can[z] for z in ready[e]))
            i = max((z for z in ready[e] if can[z] <= now), key=lambda z: (rank[z], -z))
            when = ahead(now, now + nodes[i][1], i)
            soon = [z for z in when if nodes[z][0] == e and when[z] > now and rank[z] > rank[i]]
            if soon:
                j = max(soon, key=lambda z: (rank[z], -z))
                if max(when[j] + rank[j], when[j] + nodes[j][1] + rank[i]) + SLACK[e] < max(now + rank[i], now + nodes[i][1] + rank[j]):
                    fill = [z for z in ready[e] if can[z] <= now and nodes[z][1] <= when[j] - now + SLACK[e]]
                    if not fill:
                        free[e] = min([when[j]] + [can[z] for z in ready[e] if can[z] > now])
                        continue
                    i = max(fill, key=lambda z: (rank[z], -z))
            todo -= 1
            ready[e].remove(i)
            start[i] = max(now, can[i])
            free[e] = start[i] + nodes[i][1]
            for j in later[i]:
                left[j] -= 1
                can[j] = max(can[j], free[e] + before[j][i])
                if left[j] == 0:
                    ready[nodes[j][0]].add(j)
        return start

    def order():
        if not ORDER:
            fwd = [{a: w + nodes[a][2] for a, w in nd[3].items()} for nd in nodes]
            bwd = [{} for _ in nodes]
            for i, b in enumerate(fwd):
                for a, w in b.items():
                    bwd[a][i] = w
            rank, left = [0.0] * len(nodes), [len(b) for b in bwd]
            todo = [i for i, x in enumerate(left) if x == 0]
            while todo:
                i = todo.pop()
                rank[i] = nodes[i][1] + max([w + rank[j] for j, w in bwd[i].items()] + [nodes[i][2]])
                for a in fwd[i]:
                    left[a] -= 1
                    if left[a] == 0:
                        todo.append(a)
            for _ in range(2):
                start = place(rank, fwd)
                back = place([s + nd[1] + nd[2] for s, nd in zip(start, nodes)], bwd)
                rank = [s + nd[1] for s, nd in zip(back, nodes)]
            start = place(rank, fwd)
            ORDER.extend(sorted(range(len(nodes)), key=lambda z: (start[z], z)))
        return [nodes[i][4] for i in ORDER]
    return add, follow, order


def rank_program(g, core, T, topo):
    rank = T.rank_of(core)
    if rank is None:
        return
    n = len(T.cores)

    def shares(c):
        q, used = T.rank_of(c), {}
        for d in sorted([T.cores[(q - 1) % n], T.cores[(q + 1) % n]], key=lambda z: len(topo.engines(c, z))):
            used[d] = [e for e in topo.engines(c, d) if not any(e in x for x in used.values())]
        return used
    nb = [(T.cores[(rank - 1) % n], 0), (T.cores[(rank + 1) % n], 1)]
    eng = shares(core)
    source = [T.cores[(rank + 1) % n], T.cores[(rank - 1) % n]]
    arrive_n = [len(shares(c)[core]) for c in source]
    local_n = sum(len(x) for x in eng.values())
    near, far = sorted((0, 1), key=lambda b: source[b] not in topo.cores_of(core))

    issue, need, finish = tracker(g, T)
    add, follow, order = planner()
    made, named, label = {}, {}, [-1, ""]
    vec, sca, ten = g.vector, g.scalar, g.tensor

    def at(step): label[1] = step

    def view(name, lo=0, hi=None, st=1, p0=0, p1=128):
        if name in MATS:
            name, lo, hi = "MAT", 128 * MATS.index(name), 128 * MATS.index(name) + 128
        hi = SCRATCH[name][1][1] if hi is None else hi
        t = T[name]
        return (t[p0:p1, lo:hi] if st == 1 else t[p0:p1, lo:hi:st], [(name, lo, hi, st)])

    def ind(win, off):
        return (win[0].indirect(off[0]), win[1] + off[1])

    def plan(e, cost, tail, sem, val, outs, ins, fn, waits=(), after=None, middle=False):
        def call():
            for a in waits:
                need(e, made[a])
            made[me] = issue(e, sem, val, outs, ins, fn)
        me = add(e, cost, tail, outs, ins, call, (after or {}) | {a: HOP for a in waits}, middle)
        return me

    def comp(e, fn, out, ins, *args, waits=(), both=False, middle=False, **kw):
        me = plan(e, price(e, out, ins, both), 0.0, None, 1, [out], ins, lambda: fn(*args, **kw), waits, None, middle)
        named.setdefault((e, label[0], label[1]), []).append(me)
        return me

    def dma(e, sem, out, in_, tail=LOAD + BYTE * 2 * V, waits=(), after=None):
        q = g.sync if e == "y" else sca
        return plan(e, 0.05, tail, sem, 16, [v for v in (out,) if len(v) > 1], [v for v in (in_,) if len(v) > 1],
                    lambda: q.dma_start(out[0], in_[0]).then_inc(T.sem[sem], 16), waits, after)

    def cp(o, i): comp("v", vec.tensor_copy, o, [i], o[0], i[0])
    def tt(o, a, b, op): comp("v", vec.tensor_tensor, o, [a, b], o[0], a[0], b[0], op, both=True)
    def ts(o, a, s1, op0, s2=None, op1=None):
        ins = [a] + [s for s in (s1, s2) if isinstance(s, tuple)]
        u1 = s1[0] if isinstance(s1, tuple) else s1
        u2 = s2[0] if isinstance(s2, tuple) else s2
        if op1 is None:
            comp("v", vec.tensor_scalar, o, ins, o[0], a[0], u1, None, op0)
        else:
            comp("v", vec.tensor_scalar, o, ins, o[0], a[0], u1, u2, op0, op1)
    def ms(o, c): comp("v", vec.memset, o, [], o[0], c)
    def scan(o, a, b, init, op0, op1):
        col = isinstance(init, tuple)
        comp("v", vec.tensor_tensor_scan, o, [a, b, init] if col else [a, b], o[0], a[0], b[0], init[0] if col else init, op0, op1)
    def tr(o, i): comp("v", vec.transpose, o, [i], o[0], i[0])
    def red(o, i): comp("v", vec.tensor_reduce, o, [i], o[0], i[0], AxisListType.X, A.add)
    def act(o, i, f, bias=0.0, scale=1.0):
        cols = [c for c in (bias, scale) if isinstance(c, tuple)]
        comp("s", sca.activation, o, [i] + cols, o[0], i[0], f, bias=bias[0] if isinstance(bias, tuple) else bias,
             scale=scale[0] if isinstance(scale, tuple) else scale)
    def scaled(o, i, c): act(o, i, AF.Copy, 0.0, c)
    def affine(o, i, c, d): act(o, i, AF.Identity, d, c)
    def mm(o, l, r, start, stop, waits=()):
        return comp("p", ten.matmul, o, [l, r], o[0], l[0], r[0], start, stop, waits=waits, middle=not (start or stop))
    def iota(o, pat, base, cm): comp("g", g.iota, o, [], o[0], pat, base, cm, allow_small_or_imprecise_dtypes=True)
    def gfill(o, c): iota(o, [[0, count(o)]], c, 0)
    def gcopy(o, i): comp("g", g.affine_select, o, [i], o[0], i[0], [[0, count(o)]], A.is_ge, 0.0, 0, 0)

    I = view("IW", 16, 144)

    def zq(z, q): return view(z, 15 - q, 143 - q)

    def listed(o, z, name, lo, hi, start=True, stop=True):
        for q in range(16):
            mm(o, zq(z, q), view(name, lo + q, hi, 16), start and q == 0, stop and q == 15)

    def send(e, c):
        lo, hi = PARTS[c], PARTS[c + 1]
        src, land, out = view("SN", lo, hi), "LU%d" % (e % 2), []
        for d, blk in nb:
            rid, pid = topo.addr(d, core)
            out.append(RemoteDMATransfer(dst_ids=[DstId(rid=rid, pnc=pid)], dma_engine_mask=sum(1 << x for x in eng[d]),
                                         remote_sem=T.sem["ar%d%d%d" % (e, c, blk)], src=src[0], dst=T[land][:, G * blk + lo: G * blk + hi]))
        sem = "lo%d%d" % (e, c)
        me = plan("g", CALL + (FIRST if e + c == 0 else 0.0), NEAR, sem, local_n, [], [src], lambda: g.remote_dma_fused(out, local_sem=T.sem[sem]))
        named.setdefault(("g", label[0], "send"), []).append(me)
        for b in (near, far):
            plan("n", 0.01, 0.0, "ar%d%d%d" % (e, c, b), arrive_n[b], [view(land, G * b + lo, G * b + hi)], [], None, (),
                 {me: 0.0 if b == near else FAR - NEAR})
        return me

    def ko(i): return view("KO", i, i + 1)
    def pi(i): return view("PI", i, i + 1)
    def rm(i): return view("RM", i, i + 1)
    def half(nm, h, lo=0): return view(nm, lo + 336 * h, lo + 336 * h + 336)
    def bank(b, w=336, lo=0): return view("B%d" % b, lo, lo + w)
    def ck(t, k0, k1): return view("CK%d" % (t % 2), 11 * k0, 11 * k1)
    def ent(nm, k0, k1): return view(nm, L * k0, L * k1)

    def fourfold(dst, src, t, copy):
        copy(view(dst, 0, L), view(src, t, V, 4))
        copy(view(dst, L, 2 * L), view(dst, 0, L))
        copy(view(dst, 2 * L, 4 * L), view(dst, 0, 2 * L))

    def key_add(z, src, k0, k1):
        for k in range(k0, k1):
            mm(bank(0, L), zq(z, k), ent(src, k, k + 1), False, False)

    def diff(src, own, k, b):
        mm(bank(b, H), I, ent(src, k, k + 2), True, False)
        mm(bank(b, H), view("NI"), view(own, 0, H), False, True)

    def turned(t, src):
        at("twice")
        (cp if src == "CI" else lambda o, i: act(o, i, AF.Copy))(view("Y"), ind(view(src), view("DL", 22 * t, 22 * t + 22)))
        at("turn"); tr(view("YT"), view("Y"))
        at("ck"); cp(ck(t, 0, 16), ind(view("YT"), view("KL", 0, 11)))

    def distances(t):
        xv = "XV%d" % (t % 2)
        label[0] = t
        at("start"); mm(bank(0, 192), I, view("KC"), True, False)
        for c in range(4):
            k = 4 * c
            at("x%d" % c)
            if c < XV_:
                tt(ent("GX", k, k + 4), ind(view("XF"), ck(t, k, k + 4)), view(xv), A.subtract)
                act(ent("AX", k, k + 4), ent("GX", k, k + 4), AF.Abs)
            else:
                act(ent("GX", k, k + 4), ind(view("XF"), ck(t, k, k + 4)), AF.Copy)
                for i in range(2):
                    at("x%d" % c); diff("GX", xv, k + 2 * i, 2 + i)
                    at("a%d" % c); act(ent("AX", k + 2 * i, k + 2 * i + 2), bank(2 + i, H), AF.Abs)
            at("a%d" % c); key_add("Z1", "AX", k, k + 4)
            at("n%d" % c); act(ent("BC", k, k + 4), ind(view("BF", 0, W), ck(t, k, k + 4)), AF.Copy)

    def sig(z, nm, first=False):
        for h in range(2):
            mm(bank(2 + h), view(z), half(nm, h), first, False)

    d = dma("s", "d1", view("P", 0, H), (T.past[:, 0:H],), LOAD + BYTE * V)
    dma("s", "d20", view("P", H, V), (T.past[:, H:V],), LOAD + BYTE * 3 * V, (), {d: -LOAD - BYTE * V})
    d = dma("y", "d0", view("R", 0, H), (T.reach[:, 0:H],), LOAD + BYTE * 2 * V)
    d, done = dma("y", "d21", view("R", H, V), (T.reach[:, H:V],), LOAD + BYTE * 4 * V, (), {d: -LOAD - BYTE * 2 * V}), 4 * V
    for sem, dst, src, size in (("d2", view("CI"), T.cand, 4), ("d3", view("XM"), T.x, 2),
                                ("d5", view("T8", 0, 1, 1, 0, 8), T.th, 0), ("d17", view("PF", 0, V), T.past, 2),
                                ("d18", view("RF", 0, V), T.reach, 2), ("d4", view("SI"), T.succ, 4)):
        d = dma("y", sem, dst, (src[:],), LOAD + BYTE * (done + size * V), (), {d: -LOAD - BYTE * done})
        done += size * V
    comp("g", g.iota, pi(0), [], T.PI[:, 0:1], [[0, 1]], 0, 1)
    iota(view("IO"), [[1, 192]], 0, 0)
    iota(view("IB"), [[16, 8], [0, 16]], 0, 0)
    for h in range(2):
        iota(view("I8", 128 * h, 128 * h + 128, 1, 0, 8), [[2, 4], [0, 32]], h, -1)
    iota(view("RK"), [[0, 12], [-16000, 16]], 16000, 0)
    iota(view("RSE"), [[0, H], [-256, SLOTS]], 256, 0)
    iota(view("RS8"), [[0, 128], [-256, 8]], 256, 0)
    iota(view("M4"), [[-1, 4]], -1, 0)
    for v, c in ((view("XF", V, W), int(BIGX)), (view("RF", W, W + L), 0), (view("ON"), 1), (view("C3"), CAP), (view("CN", 0, 2), 0)):
        gfill(v, c)
    for v, c in ((view("BF", V, W + L), 0.0), (view("LW"), 0.0), (view("LM"), 0.0), (view("FT"), -2.0), (view("F2"), 0.0),
                 (view("WT", 16, 32), 0.5), (view("WT", 48, 64), 2.0), (view("LW", 112, 128), 512.0), (view("ZD", 0, 1), 0.0)):
        ms(v, c)
    for i, m in ((1, 15), (2, 112), (3, 16), (4, 31), (5, 1)):
        ts(pi(i), pi(0), m, A.bitwise_and)
    ts(ko(4), pi(0), 16.0, A.add)
    cp(view("KO", 0, 2), view("PI", 1, 3))
    ts(ko(5), pi(2), 15.0, A.add)
    ts(ko(2), pi(3), 1.0 / 16, A.mult)
    affine(ko(3), ko(2), -1.0, 1.0)
    cp(ko(9), pi(4))
    cp(ko(20), pi(5))
    ts(ko(6), pi(1), 10.0, A.is_lt)
    ts(view("IW"), view("IO", 0, 160), ko(4), A.is_equal)
    ts(view("RM"), view("IO", 0, 16), ko(0), A.is_equal)
    ts(view("Z1"), view("IO", 0, 144), ko(5), A.is_equal)
    ts(view("BO"), view("IB"), ko(1), A.is_equal)
    for nm, c in (("I256", 256.0), ("NI", -1.0), ("IBG", BIGT), ("NBG", -BIGT)):
        scaled(view(nm), I, c)
    for c, (lo, hi) in enumerate(zip(PARTS, PARTS[1:])):
        mm(bank(4 + c, hi - lo), view("I256"), view("P", lo, hi), True, False)
        mm(bank(4 + c, hi - lo), view("NI"), view("R", lo, hi), False, True)
        ts(view("SN", lo, hi), bank(4 + c, hi - lo), 256.0, A.add)
        act(view("TP", lo, hi), bank(4 + c, hi - lo), AF.Copy)
        sent = send(0, c)
    for k in range(8):
        dma("y", "d%d" % (9 + k), view("SE32", 44 * k, 44 * k + 44), (T.succ[2 * k::16, :],), LOAD + 0.3 * k, [sent])
    scan(view("WT", 0, 16), view("WT", 16, 32), view("WT", 16, 32), 1.0, A.mult, A.min)
    ts(view("YB", 0, 32), view("IO", 0, 32), 0.5, A.add)
    ts(view("YB", 32, 54), view("IO", 0, 22), 32.0, A.mult, 0.5, A.add)
    tt(view("WT", 32, 48), view("WT", 0, 16), view("RM"), A.mult)
    red(ko(10), view("WT", 32, 48))
    tt(ko(26), rm(10), rm(11), A.add)
    ts(ko(11), ko(6), 2.0, A.mult)
    ts(ko(12), ko(26), rm(12), A.add, -512.0, A.mult)
    tt(ko(12), ko(12), ko(6), A.subtract)
    ts(view("YB", 64, 118), view("YB", 0, 54), ko(10), A.mult)
    ts(view("YI", 0, 54), view("YB", 0, 54), ko(10), A.mult)
    tt(view("YB", 0, 54), view("YI", 0, 54), view("YB", 64, 118), A.is_gt)
    ts(view("LH", 0, 32), view("YB", 0, 32), ko(11), A.mult)
    ts(view("LH", 32, 54), view("YB", 32, 54), ko(11), A.mult, ko(12), A.add)
    for h in range(2):
        for b in range(11):
            mm(bank(6 + h, 32, 32 * b), I, view("LH", 0, 32), b == 0, False)
        for s in range(32):
            mm(view("B%d" % (6 + h), s, H, 32), I, view("LH", 32 + 11 * h, 43 + 11 * h), False, s == 31)
        act(view("BF", H * h, H * h + H), bank(6 + h, H), AF.Copy)
    scaled(view("KO", 28, 32), view("M4"), rm(13))
    for r in range(4):
        affine(view("BT", r, V, 4), view("BF", r, V, 4), 1.0, ko(28 + r))
    scan(view("WT", 64, 80), view("WT", 48, 64), view("F2", 0, 16), 0.25, A.mult, A.add)
    tt(view("WT", 80, 96), view("WT", 64, 80), view("RM"), A.mult)
    red(ko(27), view("WT", 80, 96))
    tt(ko(7), ko(27), ko(6), A.mult)
    scaled(view("KO", 22, 24), view("KO", 2, 4), 16.0 * L)
    for h in range(2):
        for w in range(2):
            z = 16 - 16 * (h - w)
            scaled(view("SW", 128 * (2 * h + w), 128 * (2 * h + w) + 128), view("IW", z, z + 128), ko(22 if w else 23))
    ts(ko(13), ko(0), 12.0, A.is_ge, ko(6), A.subtract)
    ts(ko(14), rm(13), DUMP - 1025.0, A.mult, ko(7), A.add)
    ts(ko(32), ko(0), 12.0, A.is_ge, rm(15), A.subtract)
    tt(ko(14), ko(14), ko(32), A.add)
    for nm, c in (("ZO", WO), ("ZB", ko(7)), ("ZS", ko(14)), ("Z0", rm(0))):
        scaled(view(nm), view("Z1"), c)
    scaled(view("ZN"), view("Z0"), -1.0)
    tt(view("ZD", 1, 144), view("Z0", 1, 144), view("Z0", 0, 143), A.subtract)
    scaled(ko(33), rm(0), 512.0)
    for nm, src, c in (("BQ", "BO", ko(33)), ("BN", "BO", -1.0), ("BV", "BO", rm(13)), ("BW", "BV", -1.0)):
        scaled(view(nm), view(src), c)
    affine(ko(21), ko(0), 0.5, -0.5)
    affine(ko(21), ko(21), 1.0, ko(1))
    ts(view("EA", 0, 128), view("IO", 0, 128), ko(21), A.is_equal)
    ts(view("EA", 128, 256), view("IO", 0, 128), -8.0, A.add, ko(21), A.is_equal)
    act(view("EA", 256, 384), I, AF.Copy)
    ts(ko(18), ko(4), 75.0, A.is_lt, 512.0, A.mult)
    affine(ko(19), ko(18), -1.0, 512.0)
    affine(view("LM", 112, 128), view("LM", 112, 128), 1.0, ko(18))
    affine(view("LM", 128, 144), view("LM", 128, 144), 1.0, ko(19))
    scaled(ko(16), rm(13), 256.0)
    scaled(ko(15), ko(6), WB)
    ts(ko(17), ko(26), -256.0, A.mult, rm(12), A.subtract)
    for i, (z, c) in enumerate(((16, ko(15)), (19, ko(16)), (18, ko(16)), (17, rm(13)), (13, ko(17)))):
        scaled(view("AT", 128 * i, 128 * i + 128), view("IW", z, z + 128), c)
        mm(bank(2, 128), I, view("AT", 128 * i, 128 * i + 128), i == 0, i == 4)
    for h in range(2):
        scaled(view("AE", 128 * h, 128 * h + 128), bank(2, 128), ko(2 if h else 3))
    ts(view("YB", 128, 150), view("IO", 0, 22), 16.0, A.mult, ko(0), A.add)
    ts(ko(24), ko(0), 4.0, A.mult)
    for w in range(2):
        ts(view("DL", w, 22, 2), view("IO", 0, L, 16), 4.0, A.mult, ko(24), A.add)
    for t in range(1, RO):
        ts(view("DL", 22 * t, 22 * t + 22), view("DL", 0, 22), float(t), A.add)
    ts(view("DI", 0, 11), view("YB", 128, 139), -5.0, A.add, 1.0 / 11, A.mult)
    ts(view("YB", 160, 171), view("YB", 128, 139), 32.0, A.mult)
    ts(ko(8), ko(2), 16.0, A.mult)
    ts(view("YB", 176, 187), view("DI", 0, 11), -351.0, A.mult, ko(8), A.add)
    tt(view("YB", 176, 187), view("YB", 176, 187), view("YB", 160, 171), A.add)
    cp(view("KL", 0, 11), view("YB", 176, 187))
    ts(view("YI", 64, 86), view("YB", 128, 150), -10.5, A.add, 1.0 / 22, A.mult)
    affine(view("YB", 192, 214), view("YB", 128, 150), 16.0 * SLOTS, SLOTS - 1.0)
    ts(view("YB", 224, 246), view("YI", 64, 86), -351.0 * SLOTS, A.mult)
    tt(view("YB", 224, 246), view("YB", 224, 246), view("YB", 192, 214), A.add)
    cp(view("PL"), view("YB", 224, 246))
    scaled(ko(25), ko(0), 1.0 / 16)
    affine(view("KC"), view("IO"), 0.0, ko(25))
    act(view("LC"), view("YB", 128, 140), AF.Copy)
    affine(view("FP", 0, 42), view("IO", 0, 42), 16.0, ko(0))
    for h in range(2):
        affine(view("FT", 16 * h + 12, 192, 32), view("IO", 0, 192, 32), 1.0, ko(9))
    for i in (13, 14, 15):
        affine(view("FT", i, 192, 16), view("IO", 0, 12), 0.0, 1.0)
    ts(view("E8", 0, 256, 1, 0, 8), view("I8", 0, 256, 1, 0, 8), 0.0, A.is_equal)
    ts(view("MI", 4, 5, 1, 0, 8), view("T8", 0, 1, 1, 0, 8), 4080, A.bitwise_and)
    ts(view("MI", 5, 6, 1, 0, 8), view("T8", 0, 1, 1, 0, 8), 15, A.bitwise_and)
    cp(view("MB", 4, 6, 1, 0, 8), view("MI", 4, 6, 1, 0, 8))
    for h in range(2):
        for i in range(2):
            mm(bank(1, 1, h), view("E8", 128 * h, 128 * h + 128, 1, 0, 8), view("MB", 4 + i, 5 + i, 1, 0, 8), h == 0 and i == 0, h == 1 and i == 1)
    for h in range(2):
        ts(view("THR", h, 12, 2), view("IO", 0, 6), 0.0, A.mult, bank(1, 1, h), A.add)
    ts(view("TT", 0, 12), view("THR", 0, 12), 4096.0, A.min)
    turned(0, "CI")
    at("")
    fourfold("XV0", "XM", 0, cp)
    fourfold("RV0", "R", 0, gcopy)
    fourfold("PV0", "P", 0, gcopy)
    ms(view("XM", 0, V, 4), BIGX)
    cp(view("XF", 0, V), view("XM"))
    for r in range(2):
        cp(view("SE", L * r, L * r + L), view("SE32", r, H, 2))
    at("lists")
    cp(view("CF"), view("CI"))
    ts(view("SF"), view("SI"), ko(20), A.mult)
    distances(0)

    for t in range(RO):
        last = t == RO - 1
        par, o = t % 2, (t + 2) % 4
        actv = lambda nm: view(nm, t, V, 4)
        bl, rf = view("BL", 0, 11), view("RF", 0, W)
        pv, rv, xv = "PV%d" % par, "RV%d" % par, "XV%d" % par
        for c in range(len(PARTS) - 1):
            for b in (near, far):
                lo, hi, i = G * b + PARTS[c], G * b + PARTS[c + 1], 2 * c + (b != near)
                lu, pf, pb = view("LU%d" % par, lo, hi), view("PF", V + lo, V + hi), bank(4 + i, hi - lo)
                at("round%d" % i); ts(pf, lu, MAGIC - 128.0, A.add, MAGIC, A.subtract)
                at("past%d" % i); ts(pf, pf, 0.0, A.max, 1.0 / 256, A.mult)
                at("off"); mm(pb, view("I256"), view("ON", 0, hi - lo), True, False)
                at("past%d" % i); mm(pb, view("I256"), pf, False, True)
                at("reach%d" % i); tt(view("RF", V + lo, V + hi), pb, lu, A.subtract)
        for i, (k0, k1) in enumerate(zip(RUNS_R, RUNS_R[1:])):
            at("r%d" % i)
            tt(ent("A1", k0, k1), ind(rf, ck(t, k0, k1)), view(pv, 0, L * (k1 - k0)), A.is_le)
            key_add("ZO", "A1", k0, min(k1, 15))
        for i, (k0, k1) in enumerate(zip(RUNS_P, RUNS_P[1:])):
            at("g%d" % i)
            act(ent("GP", k0, k1), ind(view("PF"), ck(t, k0, k1)), AF.Copy)
            for k in range(k0, k1, 2):
                b = (2, 3, 6, 7)[k // 2 % 4]
                at("g%d" % i); diff("GP", rv, k, b)
                at("p%d" % i); act(ent("A2", k, k + 2), bank(b, H), AF.Relu, 1.0)
                key_add("ZO", "A2", k, k + 2)
        at("pv")
        k = RUNS_P[-1]
        tt(ent("A2", k, 16), ind(view("PF"), ck(t, k, 16)), view(rv, 0, L * (16 - k)), A.is_ge)
        key_add("ZO", "A2", k, 16)
        at("key"); mm(bank(0, L), zq("ZO", 15), ent("A1", 15, 16), False, True)
        at("")
        gcopy(view("SV"), actv("SF"))
        at("cv"); gcopy(view("CV"), actv("CF"))
        at("gone")
        mm(bank(2, L), view("BW"), actv("BF"), True, True)
        scaled(view("NS"), bank(2, L), 512.0)
        if not last:
            at("")
            for nm, src in (("XV", "XM"), ("PV", "P"), ("RV", "R")):
                fourfold("%s%d" % (nm, 1 - par), src, t + 1, gcopy)
            turned(t + 1, "CF")
        ks = view("KS", 15, 192, 16)
        at("key"); tr(view("KT"), bank(0, 192))
        at("ordered"); ts(view("OM"), bank(0, L), WO, A.is_ge, 1000.0, A.mult)
        at("least"); scan(view("KS"), view("RK"), view("KT"), 0.0, A.max, A.min)
        at("d"); ts(view("DI", 0, 12), ks, -0.47, A.add)
        at("k"); tt(view("K6", 0, 12), ks, view("DI", 0, 12), A.subtract)
        at("chosen")
        mm(bank(1, 12), I, view("LC"), True, False)
        for w in range(2):
            for h in range(2):
                j = 128 * (2 * h + w)
                mm(view("B1", w, 12, 2), view("SW", j, j + 128), view("K6", h, 12, 2), False, w == 1 and h == 1)
        cp(view("LS", 0, 11), bank(1, 11))
        at("dhi"); cp(view("FT", 10, 192, 16), view("DI", 0, 12))
        at("dlo"); tt(view("FT", 11, 192, 16), view("DI", 0, 12), view("FT", 10, 192, 16), A.subtract)
        at("fr"); tr(view("FR"), view("FT"))
        at("asks")
        tt(view("NA", 0, 12), ks, view("TT", 0, 12), A.is_ge)
        ts(view("NA", 16, 28), ks, 4096.0, A.is_ge, 2.0, A.mult)
        at("f2"); tt(view("F2", 0, 192, 16), view("NA", 0, 12), view("NA", 16, 28), A.add)
        at("gt"); tr(view("G2"), view("F2"))
        at("fe"); tt(view("FE"), ind(view("BC"), view("LS", 0, 11)), view("FR", 0, L), A.max)
        at("le")
        mm(bank(6, L), view("AE", 0, 128), view("FE"), True, True)
        mm(bank(7, L), view("AE", 128, 256), view("FE"), True, True)
        act(view("LE", 0, L), bank(6, L), AF.Copy)
        cp(view("LE", L, 2 * L), bank(7, L))
        at("b")
        listed(bank(1, 11), "ZB", "FE", 0, L)
        ts(bl, bank(1, 11), 511.5, A.add)
        ts(view("NA", 32, 43), bank(1, 11), 511.5, A.add)
        at("mn"); tt(view("MN"), ind(view("R"), bl), view(rv, 0, L), A.min)
        at("ds"); tt(view("DS"), ind(view("SF"), bl), view("SV"), A.subtract)
        at("fd"); ts(view("FD"), view("FE"), ko(13), A.mult, ko(6), A.add)
        at("ns"); tt(view("NS"), view("NS"), view("MN"), A.add)
        at("pairs")
        done = {}
        for i in (8, 10, 0, 1, 2, 3, 4, 5, 6, 7, 9, 11):
            a, j = TILES[i]
            c = (0, 117, 234)[j]
            done[i] = mm(view("B%d" % (2 + i // 2), L * (i % 2), L * (i % 2) + L, 1, 0, 118), view("LE", c, c + 118, 1, 32 * a, 32 * a + 32),
                         view("FE", 0, L, 1, 32 * a, 32 * a + 32), True, True, [done[i - 1]] if i in (9, 11) else [])
        at("gt"); mm(bank(0, L), view("BQ"), view("G2", 0, L), True, False)
        for b in range(6):
            at("y%d" % b)
            y = view("YP", H * b, H * b + H, 1, 0, 118)
            i = view("B%d" % (2 + b), 0, H, 1, 0, 118)
            if b % 2 == 0:
                ts(y, i, 10 * WB, A.is_gt)
            else:
                act(y, i, AF.Relu, -10 * WB)
            for i in (2 * b, 2 * b + 1):
                a, j = TILES[i]
                if j == 1:
                    l = view("LM", 112 - 32 * a, 240 - 32 * a, 1, 0, 118)
                else:
                    k = 112 - 16 * (2 * a + j // 2)
                    l = view("LW", k, k + 128, 1, 0, 118)
                mm(bank(0, L), l, view("YP", L * i, L * i + L, 1, 0, 118), False, i == 11)
        wn, hm = bank(0, L, 256), bank(7, L)
        at("fw")
        mm(bank(1, 11), view("EA", 256, 384), view("NA", 32, 43), True, False)
        tt(view("FW"), bank(0, L), view("FD"), A.min)
        listed(bank(1, 11), "ZS", "FW", 0, L, False)
        at("sc"); cp(view("SC", 0, 11), bank(1, 11))
        at("qq"); tt(view("QQ"), bank(0, L), view("NS"), A.add)
        at("wn"); ts(wn, bank(0, L), 0.5, A.is_lt)
        at("own"); tt(actv("RF"), actv("RF"), view("QQ"), A.min)
        at("put"); cp(ind(view("RF"), view("SC", 0, 11)), view("MN"))
        at("dsw"); tt(view("DS"), view("DS"), wn, A.mult)
        at("so")
        mm(bank(6, L), view("EA", 128 * (o // 2), 128 * (o // 2) + 128), view("SF", o, V, 4), True, False)
        mm(bank(6, L), view("EA", 128 * (t // 2), 128 * (t // 2) + 128), view("SV"), False, False)
        mm(bank(6, L), view("EA", 128 * (t // 2), 128 * (t // 2) + 128), view("DS"), False, True)
        cp(view("SO"), bank(6, L))
        if not last:
            at("oldr"); sig("BO", "R", True)
            at("old"); sig("BV", "BF")
            at("oldp"); sig("BN", "P")
            at("sf"); tt(actv("SF"), actv("SF"), view("DS"), A.add)
            at("mx")
            act(view("MX"), ind(view("P"), bl), AF.Copy)
            tt(view("MX"), view("MX"), wn, A.mult)
            at("pnew"); tt(actv("P"), actv("P"), view("MX"), A.max)
            at("name"); cp(ind(view("BF"), view("SC", 0, 11)), actv("BT"))
            at("mc"); red(view("MC", 0, 1), wn)
        at("q1"); tt(view("FD"), bank(0, L), view("MN"), A.add)
        at("rnew"); tt(actv("R"), view("FD"), actv("R"), A.min)
        at("xb"); act(view("XB"), ind(view("XM"), bl), AF.Copy)
        at("xh")
        mm(hm, I, view("XB"), True, False)
        mm(hm, I, view(xv, 0, L), False, True)
        affine(view("XH"), hm, 0.4995, WHOLE)
        affine(view("XB"), view("XH"), 1.0, -WHOLE)
        at("dx")
        mm(hm, I, view("XB"), True, False)
        mm(hm, view("NI"), view(xv, 0, L), False, True)
        act(view("DX"), hm, AF.Copy)
        tt(view("DX"), view("DX"), wn, A.mult)
        at("xm")
        mm(hm, I, view("DX"), True, False)
        mm(hm, I, view(xv, 0, L), False, True)
        act(actv("XM"), hm, AF.Copy)
        hm = bank(6, L)
        at("hm"); mm(hm, view("BQ"), view("G2", 0, L), True, True)
        at("dc"); tt(view("DC"), ind(view("CF"), bl), view("CV"), A.subtract)
        at("hm"); tt(hm, view("OM"), hm, A.is_gt)
        at("dcm"); tt(hm, view("DC"), hm, A.mult)
        at("cf"); tt(actv("CF"), view("CV"), hm, A.add)
        se = lambda k: view("SE", L * par + 22 * k, L * par + 22 * k + 22)
        for k in range(SLOTS):
            at("e%d" % k)
            ac = view("AC", H * k, H * k + H)
            if last and k == 0:
                cp(ac, ind(rf, se(SLOTS + k)))
            else:
                act(ac, ind(rf, se(SLOTS + k)), AF.Copy)
            tt(view("GE", k, SLOTS * H, SLOTS), ind(rf, se(k)), ac, A.min)
        at("gf"); scan(view("GF"), view("RSE"), view("GE"), 0.0, A.max, A.min)
        rp = view("R", par, V, 2)
        at("even"); tt(rp, ind(view("GF"), view("PL")), rp, A.min)
        for i, (lo, hi) in enumerate(zip(CUTS, CUTS[1:])):
            at("o%d" % i)
            act(view("GA", 16 * lo, 16 * hi), ind(rf, view("SO", lo, hi)), AF.Copy)
            scan(view("GS", 16 * lo, 16 * hi), view("RS8", 0, 16 * (hi - lo)), view("GA", 16 * lo, 16 * hi), 0.0, A.max, A.min)
            z = view("R", par + 4 * lo, 4 * hi, 2)
            at("low%d" % i); tt(z, view("GS", 16 * lo + 7, 16 * hi, 8), z, A.min)
        if last:
            dma("y", "d7", (T.yx[:],), view("XM"))
            dma("y", "d8", (T.yc[:],), view("CF"))
            dma("y", "d6", (T.yr[:, 0:4 * CUTS[2]],), view("R", 0, 4 * CUTS[2]))
            dma("y", "d19", (T.yr[:, 4 * CUTS[2]:V],), view("R", 4 * CUTS[2], V))
            break
        at("fl")
        listed(bank(1, 44), "ZB", "BF", 0, V)
        ts(view("FL"), bank(1, 44), 511.5, A.add)
        at("ff"); ts(view("DT", 0, 44), bank(1, 44), 511.5, A.add)
        at("new"); sig("BW", "BF"); sig("BO", "P")
        for h in range(2):
            at("ch%d" % h)
            mm(bank(2 + h), view("BN"), half("R", h), False, True)
            if h:
                act(half("CH", h), bank(2 + h), AF.Sign)
            else:
                ts(half("CH", h), bank(2 + h), 0.5, A.is_gt)
        at("cn0"); scan(half("CN", 0, 2), half("CH", 0), view("C3"), 0.0, A.add, A.min)
        at("cn1"); scan(half("CN", 1, 2), half("CH", 1), view("C3"), view("CN", 337, 338), A.add, A.min)
        for h in range(2):
            at("tp%d" % h)
            for i, (z, r) in enumerate((("I256", half("P", h)), ("NBG", view("ON", 0, 336)), ("NI", half("R", h)), ("IBG", half("CN", h, 2)),
                                        ("NBG", half("CN", h, 1)))):
                mm(bank(4 + h), view(z), r, i == 0, i == 4)
            tt(half("TP", h), bank(4 + h), half("TP", h), A.max)
        at("go")
        for q in range(16):
            mm(bank(1, 42), zq("ZD" if q < 15 else "Z0", q), view("CN", 2 + q, G + 2, 16), q == 0, False)
        mm(bank(1, 41, 1), zq("ZN", 0), view("CN", 17, G - 14 + 2, 16), False, True)
        at("df")
        tt(view("DT", 44, 86), view("DT", 0, 42), view("FP", 0, 42), A.subtract)
        ts(view("DT", 88, 130), view("DT", 0, 42), float(G), A.is_lt)
        at("dfm"); tt(view("DT", 44, 86), view("DT", 44, 86), view("DT", 88, 130), A.mult)
        at("go"); tt(view("DT", 132, 174), bank(1, 42), view("DT", 44, 86), A.mult)
        at("fp"); tt(view("FP", 0, 42), view("FP", 0, 42), view("DT", 132, 174), A.add)
        at("fu"); cp(view("FU", 0, 42), view("FP", 0, 42))
        at("send")
        for c, (lo, hi) in enumerate(zip(PARTS, PARTS[1:])):
            ts(view("SN", lo, hi), ind(view("TP"), view("FU", lo // 16, hi // 16)), 256.0, A.add)
            send(t + 1, c)
        at(""); gfill(view("XM", t + 1, V, 4), int(BIGX))
        for dst, src in (("PF", "P"), ("XF", "XM"), ("RF", "R")):
            at(dst); act(view(dst, 0, V), ind(view(src), view("FL")), AF.Copy)
        at("m0")
        ts(view("MB", 0, 1), view("MC", 0, 1), 1.0 / 16, A.mult)
        mm(bank(1, 1), view("ON", 0, 128), view("MB", 0, 1), True, True)
        at("m1"); cp(view("MI", 0, 1), bank(1, 1))
        at("m2"); ts(view("MI", 1, 2), view("MI", 0, 1), 31, A.bitwise_and)
        at("m3"); cp(view("MC", 1, 2), view("MI", 1, 2))
        at("m4"); ts(view("TT", 0, 12), view("THR", 0, 12), view("MC", 1, 2), A.add, 4096.0, A.min)
        distances(t + 1)
    for i in named["v", -1, "lists"]:
        follow([i, named["v", 0, "round0"][0]])
    for e in LINES:
        follow([i for t in range(-1, RO) for w in (LAST if t == RO - 1 else LINES)[e].split()
                for i in named.get((e, t + (w[0] == "+") - (w[0] == "-"), w.lstrip("+-")), [])])
    for call in order():
        call()
    finish()
